import numpy as np
import ml_dtypes


def mxq(x, axis, fmt="e4m3"):
    dtype, down = {"e4m3": (ml_dtypes.float8_e4m3fn, 7), "e5m2": (ml_dtypes.float8_e5m2, 14)}[fmt]
    v = np.moveaxis(np.asarray(x, np.float32).astype(ml_dtypes.bfloat16).astype(np.float64), axis, -1)
    blocks = v.reshape(v.shape[:-1] + (-1, 32))
    amax = np.abs(blocks).max(-1, keepdims=True)
    byte = np.maximum(np.where(amax > 0, np.frexp(amax)[1] - 1 + 127, 0) - down, 1)
    scale = np.exp2(byte - 127.0)
    codes = (blocks / scale).astype(np.float32).astype(dtype).astype(np.float64)
    return np.moveaxis((codes * scale).reshape(v.shape), -1, axis)


WIDE = False


def mx_kscale(k):
    if not WIDE:
        return np.ones(k)
    levels = np.array([24, -24, 12, -12, 0])
    if k % 512:
        return np.exp2(np.random.permutation(np.resize(levels, k // 32))).repeat(32)
    a = np.empty((k // 512, 16))
    for p in range(k // 512):
        a[p, :8] = np.random.permutation(np.resize(levels, 8))
        for g in range(8):
            far = levels[np.abs(levels - a[p, g]) >= 10]
            a[p, g + 8] = far[np.random.randint(len(far))]
    return np.exp2(a.ravel()).repeat(32)


def f64(x):
    return np.asarray(x).astype(np.float64)


def striped(idx):
    return np.tile(idx.reshape(-1, 16).T, (8, 1)).astype(np.uint16)


def unstriped(offs):
    return offs[:16].T.reshape(-1).astype(np.int64)


E2M1 = np.array([0.0, 0.5, 1.0, 1.5, 2.0, 3.0, 4.0, 6.0, -0.0, -0.5, -1.0, -1.5, -2.0, -3.0, -4.0, -6.0])


def pack_weight(w, fmt):
    k, n = w.shape
    w = f64(np.asarray(w, np.float32).astype(ml_dtypes.bfloat16)).reshape(k // 32, 32, n)
    amax = np.abs(w).max(1)
    if fmt == "e4m3":
        byte = np.frexp(amax)[1] - 1 + 127 - 7
    else:
        mant, ex = np.frexp(amax / 6.0)
        byte = np.where(mant > 0.5, ex, ex - 1) + 127
    byte = np.clip(np.where(amax > 0, byte, 1), 1, 254)
    scaled = (w * np.exp2(127.0 - byte)[:, None, :]).reshape(k, n).astype(np.float32)
    by_word = np.ascontiguousarray(scaled.reshape(k // 512, 128, 4, n).transpose(0, 1, 3, 2))
    if fmt == "e4m3":
        words = by_word.astype(ml_dtypes.float8_e4m3fn).view(np.uint8)
    else:
        c = by_word.astype(ml_dtypes.float4_e2m1fn).view(np.uint8) & 0xF
        words = (c[..., 0::2] | (c[..., 1::2] << 4)).reshape(k // 512, 128, 2 * n)
    return np.ascontiguousarray(words), np.ascontiguousarray(byte.astype(np.uint8).reshape(k // 512, 16, n))


def unpack_weight(words, scales, fmt):
    g, _, n = scales.shape
    words = np.ascontiguousarray(words).reshape(g, 128, n, -1)
    if fmt == "e4m3":
        vals = words.view(ml_dtypes.float8_e4m3fn).astype(np.float64)
    else:
        nib = np.empty((g, 128, n, 4), np.uint8)
        nib[..., 0::2] = words & 0xF
        nib[..., 1::2] = words >> 4
        vals = E2M1[nib]
    vals = vals * np.repeat(np.exp2(scales.astype(np.float64) - 127.0), 8, axis=1)[..., None]
    return vals.transpose(0, 1, 3, 2).reshape(g * 512, n)


def pack_table4(v):
    words, scales = pack_weight(v, "e2m1")
    g, t = words.shape[0] // 2, v.shape[1]
    return np.ascontiguousarray(words.reshape(g, 2, 128, t, 2).transpose(0, 2, 3, 1, 4).reshape(g, 128, t, 4)), scales


def unpack_table4(words, scales):
    g, _, t, _ = words.shape
    return unpack_weight(words.reshape(g, 128, t, 2, 2).transpose(0, 3, 1, 2, 4).reshape(2 * g, 128, 2 * t), scales, "e2m1")


K, M, N, T, J = 1024, 1024, 1024, 2048, 1024


def setup_inputs():
    n = np.random.standard_normal
    s = mx_kscale(K)[:, None]
    s2 = mx_kscale(M)[:, None]
    h = np.tanh(n((N, T)))
    p_tab = pack_table4(h * s2)
    p_wn = pack_weight(n((K, N)) / np.sqrt(K) / s, "e4m3")
    p_un = pack_weight(n((M, N)) / np.sqrt(M) / s2, "e4m3")
    return {
        "x": (n((K, J)) * s).astype(np.float32),
        "tab_words": p_tab[0],
        "tab_scales": p_tab[1],
        "wn_words": p_wn[0],
        "wn_scales": p_wn[1],
        "un_words": p_un[0],
        "un_scales": p_un[1],
        "bn": (0.3 * n(N)).astype(np.float32),
        "hT": (h).astype(np.float32),
        "wgo": np.tile(np.random.uniform(0.5, 2.0, J), (128, 1)).astype(np.float32),
        "offs": striped(np.random.permutation(T)[:J]),
    }


def reference(x, tab_words, tab_scales, wn_words, wn_scales, un_words, un_scales, bn, hT, wgo, offs):
    idx = unstriped(offs)
    x_ = mxq(f64(x), 0, "e4m3")
    tab_ = unpack_table4(tab_words, tab_scales)[:, idx]
    wn_ = unpack_weight(wn_words, wn_scales, "e4m3")
    un_ = unpack_weight(un_words, un_scales, "e4m3")
    sn = wn_.T @ x_ + un_.T @ tab_
    out = np.zeros((N, T))
    out[:, idx] = f64(wgo)[0] * (np.tanh(sn + f64(bn)[:, None]) + f64(hT)[:, idx])
    return out

@@ -1,0 +1,211 @@
+from contextlib import ExitStack
+
+import concourse.mybir as mybir
+from concourse.masks import make_identity
+
+K, M, N, T, J = 1024, 1024, 1024, 2048, 1024
+FLOPS = 2 * (K + M) * N * J
+
+F32 = mybir.dt.float32
+BF16 = mybir.dt.bfloat16
+I32 = mybir.dt.int32
+U32 = mybir.dt.uint32
+U16 = mybir.dt.uint16
+U8 = mybir.dt.uint8
+FP8X4 = mybir.dt.float8_e4m3fn_x4
+FP4X4 = mybir.dt.float4_e2m1fn_x4
+ADD = mybir.AluOpType.add
+MULT = mybir.AluOpType.mult
+TANH = mybir.ActivationFunctionType.Tanh
+
+P = 128
+PASSES = 2
+HALF = 512
+PIECE = 256
+TILES = N // P
+EARLY = 2
+WINDOWS = 2
+
+
+def tile_list_tgn_rnn_kernel(
+    tc, x, tab_words, tab_scales, wn_words, wn_scales, un_words, un_scales, bn, hT, wgo, offs, out
+):
+    nc = tc.nc
+    with ExitStack() as ctx:
+        keep = ctx.enter_context(tc.tile_pool(name="keep", bufs=1))
+        ring = ctx.enter_context(tc.tile_pool(name="ring", bufs=3))
+        psum = ctx.enter_context(tc.psum_pool(name="psum", bufs=4))
+        psb = ctx.enter_context(tc.psum_pool(name="psb", bufs=1))
+
+        offsets = keep.tile([P, J // 16], U16, name="offsets")
+        tab = keep.tile([P, T], I32, name="tab", align_bytes=64)
+        tab_planes = keep.tile([P, PASSES, T], U8, name="tab_planes", align_bytes=64)
+        w_planes = keep.tile([P, PASSES, N], U8, name="w_planes", align_bytes=64)
+        windows = [keep.tile([P, T], F32, name=f"window{i}") for i in range(WINDOWS)]
+        bias_rows = keep.tile([P, P], F32, name="bias_rows")
+        ident = keep.tile([P, P], F32, name="ident")
+        bias = keep.tile([P, TILES], F32, name="bias")
+        warm = keep.tile([P, 1], F32, name="warm")
+        weights = keep.tile([P, J], F32, name="weights")
+        h = [keep.tile([P, T], F32, name=f"h{r}") for r in range(TILES)]
+        raw = {
+            (a, c): keep.tile([P, 4, PIECE], F32, name=f"raw{a}_{c}")
+            for a in range(PASSES)
+            for c in range(J // PIECE)
+        }
+        head_cols = EARLY * P
+        wn_head = keep.tile([P, PASSES, head_cols], I32, name="wn_head", align_bytes=64)
+        un_head = keep.tile([P, PASSES, head_cols], I32, name="un_head", align_bytes=64)
+        wn_rest = keep.tile([P, PASSES, N - head_cols], I32, name="wn_rest", align_bytes=64)
+        un_rest = keep.tile([P, PASSES, N - head_cols], I32, name="un_rest", align_bytes=64)
+
+        nc.vector.memset(tab_planes[:].bitcast(I32), 0)
+        nc.vector.memset(w_planes[:].bitcast(I32), 0)
+        nc.gpsimd.memset(bias_rows[:], 0.0)
+        make_identity(nc, ident[:])
+
+        def load_planes(queue, planes, first_row, scales):
+            for q in range(4):
+                rows = slice(32 * q + first_row, 32 * q + first_row + 4)
+                queue.dma_start(
+                    out=planes[rows, :, :].bitcast(I32),
+                    in_=scales[:, 4 * q : 4 * q + 4, :].bitcast(I32).rearrange("a r n -> r a n"),
+                )
+
+        def load_x(a, c):
+            rows = x[512 * a : 512 * (a + 1), PIECE * c : PIECE * (c + 1)]
+            nc.sync.dma_start(out=raw[a, c][:], in_=rows.rearrange("(p i) j -> p i j", i=4))
+
+        def load_w(tile, words, lo, hi):
+            view = words.rearrange("a p n i -> p a (n i)")[:, :, 4 * lo : 4 * hi].bitcast(I32)
+            nc.sync.dma_start(out=tile[:], in_=view)
+
+        def load_h(r):
+            nc.sync.dma_start(out=h[r][:], in_=hT[P * r : P * (r + 1), :])
+
+        nc.sync.dma_start(offsets[:], offs)
+        nc.sync.dma_start(out=tab[:], in_=tab_words[0].rearrange("p t b -> p (t b)").bitcast(I32))
+        load_planes(nc.scalar, tab_planes, 0, tab_scales)
+        nc.gpsimd.dma_start(out=bias_rows[0:TILES, :], in_=bn.rearrange("(r p) -> r p", p=P))
+        load_x(0, 0)
+        load_x(0, 1)
+        load_x(1, 0)
+        load_planes(nc.sync, w_planes, 0, un_scales)
+        load_x(1, 1)
+        load_w(un_head, un_words, 0, head_cols)
+        load_planes(nc.sync, w_planes, 4, wn_scales)
+        load_w(wn_head, wn_words, 0, head_cols)
+        load_h(0)
+        nc.sync.dma_start(out=weights[:, 0:HALF], in_=wgo[:, 0:HALF])
+        for a in range(PASSES):
+            load_x(a, 2)
+            load_x(a, 3)
+        load_h(1)
+        nc.sync.dma_start(out=weights[:, HALF:J], in_=wgo[:, HALF:J])
+        load_w(un_rest, un_words, head_cols, N)
+        load_w(wn_rest, wn_words, head_cols, N)
+        for r in range(2, TILES):
+            load_h(r)
+
+        nc.scalar.activation(out=warm[:], in_=ident[:, 0:1], func=TANH)
+
+        for w in windows:
+            nc.vector.memset(w[:], 0.0)
+
+        bias_t = psb.tile([P, P], F32, name="bias_t")
+        nc.tensor.transpose(bias_t[:], bias_rows[:], ident[:])
+        nc.scalar.copy(out=bias[:], in_=bias_t[:, 0:TILES])
+
+        def offsets_of(half):
+            return offsets[:, half * (HALF // 16) : (half + 1) * (HALF // 16)]
+
+        tab_codes, tab_sc, x_codes, x_sc = {}, {}, {}, {}
+
+        def gather_table(half):
+            pairs = keep.tile([P, HALF], U32, name=f"pairs{half}")
+            nc.vector.tensor_copy(out=pairs[:], in_=tab[:].bitcast(U32).indirect(offsets_of(half)))
+            for a in range(PASSES):
+                sc = keep.tile([P, HALF], U8, name=f"tab_sc{half}_{a}", align_bytes=64)
+                nc.vector.tensor_copy(out=sc[:], in_=tab_planes[:, a, :].indirect(offsets_of(half)))
+                tab_sc[a, half] = sc
+            codes = keep.tile([P, PASSES, HALF], U16, name=f"tab_codes{half}", align_bytes=64)
+            nc.vector.tensor_copy(
+                out=codes[:], in_=pairs[:].bitcast(U16).rearrange("p (j d) -> p d j", d=PASSES)
+            )
+            tab_codes[half] = codes
+
+        def quantise_x(half):
+            for a in range(PASSES):
+                codes = keep.tile([P, HALF], U32, name=f"x_codes{half}_{a}", align_bytes=64)
+                sc = keep.tile([P, HALF], U8, name=f"x_sc{half}_{a}", align_bytes=64)
+                for i in range(HALF // PIECE):
+                    c = half * (HALF // PIECE) + i
+                    cols = slice(i * PIECE, (i + 1) * PIECE)
+                    grouped = ring.tile([P, PIECE, 4], BF16, name="grouped", align_bytes=64)
+                    nc.scalar.copy(out=grouped[:], in_=raw[a, c][:].rearrange("p i j -> p j i"))
+                    nc.vector.quantize_mx(
+                        out=codes[:, cols].bitcast(FP8X4),
+                        scales=sc[:, cols],
+                        in_=grouped[:].rearrange("p j i -> p (j i)"),
+                    )
+                x_codes[a, half], x_sc[a, half] = codes, sc
+
+        def products(r, half, into):
+            if r < EARLY:
+                un_t, wn_t, c0 = un_head, wn_head, r * P
+            else:
+                un_t, wn_t, c0 = un_rest, wn_rest, (r - EARLY) * P
+            cols = slice(c0, c0 + P)
+            ncols = slice(r * P, (r + 1) * P)
+            acc = psum.tile([P, HALF], F32, name="acc")
+            for a in range(PASSES):
+                nc.tensor.matmul_mx(
+                    out=acc[:],
+                    lhsT=un_t[:, a, cols].bitcast(FP8X4),
+                    lhsT_scale=w_planes[:, a, ncols],
+                    rhs=tab_codes[half][:, a, :].bitcast(FP4X4),
+                    rhs_scale=tab_sc[a, half][:],
+                    start=(a == 0),
+                    stop=False,
+                )
+            for a in range(PASSES):
+                nc.tensor.matmul_mx(
+                    out=acc[:],
+                    lhsT=wn_t[:, a, cols].bitcast(FP8X4),
+                    lhsT_scale=w_planes[4:P, a, ncols],
+                    rhs=x_codes[a, half][:].bitcast(FP8X4),
+                    rhs_scale=x_sc[a, half][:],
+                    start=False,
+                    stop=(a == PASSES - 1),
+                )
+            nc.scalar.activation(out=into, in_=acc[:], func=TANH, bias=bias[:, r : r + 1])
+
+        def update(r, act, offs_ap, wcols, name):
+            width = act.shape[1]
+            total = keep.tile([P, width], F32, name=name)
+            nc.vector.tensor_tensor(out=total[:], in0=h[r][:].indirect(offs_ap), in1=act, op=ADD)
+            window = windows[r % WINDOWS]
+            nc.vector.tensor_tensor(
+                out=window[:].indirect(offs_ap), in0=total[:], in1=weights[:, wcols], op=MULT
+            )
+
+        def store(r):
+            nc.sync.dma_start(out=out[P * r : P * (r + 1), :], in_=windows[r % WINDOWS][:])
+
+        gather_table(0)
+        quantise_x(0)
+        gather_table(1)
+        quantise_x(1)
+        for half in range(2):
+            for r in range(EARLY):
+                act = ring.tile([P, J], F32, name="act")
+                products(r, half, act[:, 0:HALF])
+                update(r, act[:, 0:HALF], offsets_of(half), slice(half * HALF, (half + 1) * HALF), f"tot{r}_{half}")
+                if half == 1:
+                    store(r)
+        for r in range(EARLY, TILES):
+            act = ring.tile([P, J], F32, name="act")
+            for half in range(2):
+                products(r, half, act[:, half * HALF : (half + 1) * HALF])
+            update(r, act[:], offsets[:], slice(0, J), f"tot{r}")
+            store(r)

@@ -23,8 +23,9 @@ PASSES = 2
 HALF = 512
 PIECE = 256
 TILES = N // P
-EARLY = 2
-WINDOWS = 2
+EARLY = 3
+WINDOWS = 3
+W_GROUPS = ((0, 1), (1, 3), (3, TILES))
 
 
 def tile_list_tgn_rnn_kernel(
@@ -33,7 +34,8 @@ def tile_list_tgn_rnn_kernel(
     nc = tc.nc
     with ExitStack() as ctx:
         keep = ctx.enter_context(tc.tile_pool(name="keep", bufs=1))
-        ring = ctx.enter_context(tc.tile_pool(name="ring", bufs=3))
+        ring = ctx.enter_context(tc.tile_pool(name="ring", bufs=4))
+        acts = ctx.enter_context(tc.tile_pool(name="acts", bufs=4))
         psum = ctx.enter_context(tc.psum_pool(name="psum", bufs=4))
         psb = ctx.enter_context(tc.psum_pool(name="psb", bufs=1))
 
@@ -49,15 +51,12 @@ def tile_list_tgn_rnn_kernel(
         weights = keep.tile([P, J], F32, name="weights")
         h = [keep.tile([P, T], F32, name=f"h{r}") for r in range(TILES)]
         raw = {
-            (a, c): keep.tile([P, 4, PIECE], F32, name=f"raw{a}_{c}")
+            (a, c): keep.tile([P, 4, HALF], F32, name=f"raw{a}_{c}", tag=f"raw{a}_{c}")
             for a in range(PASSES)
-            for c in range(J // PIECE)
+            for c in range(2)
         }
-        head_cols = EARLY * P
-        wn_head = keep.tile([P, PASSES, head_cols], I32, name="wn_head", align_bytes=64)
-        un_head = keep.tile([P, PASSES, head_cols], I32, name="un_head", align_bytes=64)
-        wn_rest = keep.tile([P, PASSES, N - head_cols], I32, name="wn_rest", align_bytes=64)
-        un_rest = keep.tile([P, PASSES, N - head_cols], I32, name="un_rest", align_bytes=64)
+        wn_sb = [keep.tile([P, PASSES, (hi - lo) * P], I32, name=f"wn{lo}", align_bytes=64) for lo, hi in W_GROUPS]
+        un_sb = [keep.tile([P, PASSES, (hi - lo) * P], I32, name=f"un{lo}", align_bytes=64) for lo, hi in W_GROUPS]
 
         nc.vector.memset(tab_planes[:].bitcast(I32), 0)
         nc.vector.memset(w_planes[:].bitcast(I32), 0)
@@ -73,44 +72,47 @@ def tile_list_tgn_rnn_kernel(
                 )
 
         def load_x(a, c):
-            rows = x[512 * a : 512 * (a + 1), PIECE * c : PIECE * (c + 1)]
+            rows = x[512 * a : 512 * (a + 1), HALF * c : HALF * (c + 1)]
             nc.sync.dma_start(out=raw[a, c][:], in_=rows.rearrange("(p i) j -> p i j", i=4))
 
-        def load_w(tile, words, lo, hi):
-            view = words.rearrange("a p n i -> p a (n i)")[:, :, 4 * lo : 4 * hi].bitcast(I32)
-            nc.sync.dma_start(out=tile[:], in_=view)
+        def load_w(tiles, words, g):
+            lo, hi = W_GROUPS[g]
+            view = words.rearrange("a p n i -> p a (n i)")[:, :, 4 * P * lo : 4 * P * hi].bitcast(I32)
+            nc.sync.dma_start(out=tiles[g][:], in_=view)
 
         def load_h(r):
             nc.sync.dma_start(out=h[r][:], in_=hT[P * r : P * (r + 1), :])
 
         nc.sync.dma_start(offsets[:], offs)
         nc.sync.dma_start(out=tab[:], in_=tab_words[0].rearrange("p t b -> p (t b)").bitcast(I32))
-        load_planes(nc.scalar, tab_planes, 0, tab_scales)
-        nc.gpsimd.dma_start(out=bias_rows[0:TILES, :], in_=bn.rearrange("(r p) -> r p", p=P))
+        load_planes(nc.sync, tab_planes, 0, tab_scales)
+        load_w(un_sb, un_words, 0)
         load_x(0, 0)
-        load_x(0, 1)
-        load_x(1, 0)
         load_planes(nc.sync, w_planes, 0, un_scales)
-        load_x(1, 1)
-        load_w(un_head, un_words, 0, head_cols)
-        load_planes(nc.sync, w_planes, 4, wn_scales)
-        load_w(wn_head, wn_words, 0, head_cols)
+        load_w(wn_sb, wn_words, 0)
+        load_x(1, 0)
+        for q in range(4):
+            nc.sync.dma_start(
+                out=w_planes[32 * q + 4 : 32 * q + 12, 0, :].bitcast(I32),
+                in_=wn_scales[:, 4 * q : 4 * q + 4, :].bitcast(I32),
+            )
+        nc.sync.dma_start(out=bias_rows[0:TILES, :], in_=bn.rearrange("(r p) -> r p", p=P))
         load_h(0)
         nc.sync.dma_start(out=weights[:, 0:HALF], in_=wgo[:, 0:HALF])
-        for a in range(PASSES):
-            load_x(a, 2)
-            load_x(a, 3)
+        load_w(un_sb, un_words, 1)
+        load_w(wn_sb, wn_words, 1)
         load_h(1)
+        for a in range(PASSES):
+            load_x(a, 1)
+        load_h(2)
         nc.sync.dma_start(out=weights[:, HALF:J], in_=wgo[:, HALF:J])
-        load_w(un_rest, un_words, head_cols, N)
-        load_w(wn_rest, wn_words, head_cols, N)
-        for r in range(2, TILES):
+        load_w(un_sb, un_words, 2)
+        load_w(wn_sb, wn_words, 2)
+        for r in range(3, TILES):
             load_h(r)
 
         nc.scalar.activation(out=warm[:], in_=ident[:, 0:1], func=TANH)
 
-        for w in windows:
-            nc.vector.memset(w[:], 0.0)
 
         bias_t = psb.tile([P, P], F32, name="bias_t")
         nc.tensor.transpose(bias_t[:], bias_rows[:], ident[:])
@@ -122,7 +124,7 @@ def tile_list_tgn_rnn_kernel(
         tab_codes, tab_sc, x_codes, x_sc = {}, {}, {}, {}
 
         def gather_table(half):
-            pairs = keep.tile([P, HALF], U32, name=f"pairs{half}")
+            pairs = keep.tile([P, HALF], U32, name=f"pairs{half}", tag=("pairs", "raw1_0")[half])
             nc.vector.tensor_copy(out=pairs[:], in_=tab[:].bitcast(U32).indirect(offsets_of(half)))
             for a in range(PASSES):
                 sc = keep.tile([P, HALF], U8, name=f"tab_sc{half}_{a}", align_bytes=64)
@@ -139,10 +141,14 @@ def tile_list_tgn_rnn_kernel(
                 codes = keep.tile([P, HALF], U32, name=f"x_codes{half}_{a}", align_bytes=64)
                 sc = keep.tile([P, HALF], U8, name=f"x_sc{half}_{a}", align_bytes=64)
                 for i in range(HALF // PIECE):
-                    c = half * (HALF // PIECE) + i
                     cols = slice(i * PIECE, (i + 1) * PIECE)
                     grouped = ring.tile([P, PIECE, 4], BF16, name="grouped", align_bytes=64)
-                    nc.scalar.copy(out=grouped[:], in_=raw[a, c][:].rearrange("p i j -> p j i"))
+                    dst = grouped[:].rearrange("p (c e) i -> p c i e", e=4)
+                    src = raw[a, half][:, :, cols].rearrange("p i (c e) -> p c i e", e=4)
+                    if (half, a, i) == (0, 1, 0):
+                        nc.vector.tensor_copy(out=dst, in_=src)
+                    else:
+                        nc.scalar.copy(out=dst, in_=src)
                     nc.vector.quantize_mx(
                         out=codes[:, cols].bitcast(FP8X4),
                         scales=sc[:, cols],
@@ -151,10 +157,8 @@ def tile_list_tgn_rnn_kernel(
                 x_codes[a, half], x_sc[a, half] = codes, sc
 
         def products(r, half, into):
-            if r < EARLY:
-                un_t, wn_t, c0 = un_head, wn_head, r * P
-            else:
-                un_t, wn_t, c0 = un_rest, wn_rest, (r - EARLY) * P
+            g = [i for i, (lo, hi) in enumerate(W_GROUPS) if lo <= r < hi][0]
+            un_t, wn_t, c0 = un_sb[g], wn_sb[g], (r - W_GROUPS[g][0]) * P
             cols = slice(c0, c0 + P)
             ncols = slice(r * P, (r + 1) * P)
             acc = psum.tile([P, HALF], F32, name="acc")
@@ -172,7 +176,7 @@ def tile_list_tgn_rnn_kernel(
                 nc.tensor.matmul_mx(
                     out=acc[:],
                     lhsT=wn_t[:, a, cols].bitcast(FP8X4),
-                    lhsT_scale=w_planes[4:P, a, ncols],
+                    lhsT_scale=w_planes[4 + 4 * a : P, 0, ncols],
                     rhs=x_codes[a, half][:].bitcast(FP8X4),
                     rhs_scale=x_sc[a, half][:],
                     start=False,
@@ -180,13 +184,24 @@ def tile_list_tgn_rnn_kernel(
                 )
             nc.scalar.activation(out=into, in_=acc[:], func=TANH, bias=bias[:, r : r + 1])
 
-        def update(r, act, offs_ap, wcols, name):
-            width = act.shape[1]
-            total = keep.tile([P, width], F32, name=name)
-            nc.vector.tensor_tensor(out=total[:], in0=h[r][:].indirect(offs_ap), in1=act, op=ADD)
-            window = windows[r % WINDOWS]
+        def cols_of(half):
+            return slice(half * HALF, (half + 1) * HALF)
+
+        totals = [keep.tile([P, J], F32, name=f"total{r}") for r in range(TILES)]
+
+        def add_state(r, halves):
+            act = acts.tile([P, J], F32, name="act")
+            for half in halves:
+                products(r, half, act[:, cols_of(half)])
+            cols = slice(halves[0] * HALF, (halves[-1] + 1) * HALF)
+            offs_ap = offsets[:, cols.start // 16 : cols.stop // 16]
+            nc.vector.tensor_tensor(out=totals[r][:, cols], in0=h[r][:].indirect(offs_ap), in1=act[:, cols], op=ADD)
+
+        def place(r, halves):
+            cols = slice(halves[0] * HALF, (halves[-1] + 1) * HALF)
+            offs_ap = offsets[:, cols.start // 16 : cols.stop // 16]
             nc.vector.tensor_tensor(
-                out=window[:].indirect(offs_ap), in0=total[:], in1=weights[:, wcols], op=MULT
+                out=windows[r % WINDOWS][:].indirect(offs_ap), in0=totals[r][:, cols], in1=weights[:, cols], op=MULT
             )
 
         def store(r):
@@ -195,17 +210,20 @@ def tile_list_tgn_rnn_kernel(
         gather_table(0)
         quantise_x(0)
         gather_table(1)
+        for w in windows:
+            for c in range(2):
+                nc.vector.memset(w[:, c * J : (c + 1) * J], 0.0)
         quantise_x(1)
-        for half in range(2):
-            for r in range(EARLY):
-                act = ring.tile([P, J], F32, name="act")
-                products(r, half, act[:, 0:HALF])
-                update(r, act[:, 0:HALF], offsets_of(half), slice(half * HALF, (half + 1) * HALF), f"tot{r}_{half}")
-                if half == 1:
-                    store(r)
+        for r in range(EARLY):
+            add_state(r, (0,))
+            place(r, (0,))
+        for r in range(EARLY):
+            add_state(r, (1,))
+        for r in range(EARLY):
+            place(r, (1,))
+            store(r)
         for r in range(EARLY, TILES):
-            act = ring.tile([P, J], F32, name="act")
-            for half in range(2):
-                products(r, half, act[:, half * HALF : (half + 1) * HALF])
-            update(r, act[:], offsets[:], slice(0, J), f"tot{r}")
+            add_state(r, (0, 1))
+        for r in range(EARLY, TILES):
+            place(r, (0, 1))
             store(r)

@@ -43,7 +43,7 @@ def tile_list_tgn_rnn_kernel(
         tab = keep.tile([P, T], I32, name="tab", align_bytes=64)
         tab_planes = keep.tile([P, PASSES, T], U8, name="tab_planes", align_bytes=64)
         w_planes = keep.tile([P, PASSES, N], U8, name="w_planes", align_bytes=64)
-        windows = [keep.tile([P, T], F32, name=f"window{i}") for i in range(WINDOWS)]
+        windows = [keep.tile([P, T], F32, name=f"window{i}") for i in range(WINDOWS - 1)]
         bias_rows = keep.tile([P, P], F32, name="bias_rows")
         ident = keep.tile([P, P], F32, name="ident")
         bias = keep.tile([P, TILES], F32, name="bias")
@@ -51,7 +51,7 @@ def tile_list_tgn_rnn_kernel(
         weights = keep.tile([P, J], F32, name="weights")
         h = [keep.tile([P, T], F32, name=f"h{r}") for r in range(TILES)]
         raw = {
-            (a, c): keep.tile([P, 4, HALF], F32, name=f"raw{a}_{c}", tag=f"raw{a}_{c}")
+            (a, c): keep.tile([P, 4, HALF], F32, name=f"raw{a}_{c}", tag=f"raw{a}_{c}", align_bytes=64)
             for a in range(PASSES)
             for c in range(2)
         }
@@ -61,15 +61,14 @@ def tile_list_tgn_rnn_kernel(
         nc.vector.memset(tab_planes[:].bitcast(I32), 0)
         nc.vector.memset(w_planes[:].bitcast(I32), 0)
         nc.gpsimd.memset(bias_rows[:], 0.0)
+        nc.gpsimd.dma_start(out=bias_rows[0:TILES, :], in_=bn.rearrange("(r p) -> r p", p=P))
         make_identity(nc, ident[:])
 
-        def load_planes(queue, planes, first_row, scales):
-            for q in range(4):
-                rows = slice(32 * q + first_row, 32 * q + first_row + 4)
-                queue.dma_start(
-                    out=planes[rows, :, :].bitcast(I32),
-                    in_=scales[:, 4 * q : 4 * q + 4, :].bitcast(I32).rearrange("a r n -> r a n"),
-                )
+        def load_scale_row(planes, first_row, scales, r):
+            nc.sync.dma_start(
+                out=planes[first_row + r : P : 32, :, :].bitcast(I32),
+                in_=scales[:, r:16:4, :].bitcast(I32).rearrange("a q n -> q a n"),
+            )
 
         def load_x(a, c):
             rows = x[512 * a : 512 * (a + 1), HALF * c : HALF * (c + 1)]
@@ -85,18 +84,15 @@ def tile_list_tgn_rnn_kernel(
 
         nc.sync.dma_start(offsets[:], offs)
         nc.sync.dma_start(out=tab[:], in_=tab_words[0].rearrange("p t b -> p (t b)").bitcast(I32))
-        load_planes(nc.sync, tab_planes, 0, tab_scales)
+        for r in range(4):
+            load_scale_row(tab_planes, 0, tab_scales, r)
+        for a in range(PASSES):
+            load_x(a, 0)
+            for r in (2 * a, 2 * a + 1):
+                load_scale_row(w_planes, 0, un_scales, r)
+                load_scale_row(w_planes, 4, wn_scales, r)
         load_w(un_sb, un_words, 0)
-        load_x(0, 0)
-        load_planes(nc.sync, w_planes, 0, un_scales)
         load_w(wn_sb, wn_words, 0)
-        load_x(1, 0)
-        for q in range(4):
-            nc.sync.dma_start(
-                out=w_planes[32 * q + 4 : 32 * q + 12, 0, :].bitcast(I32),
-                in_=wn_scales[:, 4 * q : 4 * q + 4, :].bitcast(I32),
-            )
-        nc.sync.dma_start(out=bias_rows[0:TILES, :], in_=bn.rearrange("(r p) -> r p", p=P))
         load_h(0)
         nc.sync.dma_start(out=weights[:, 0:HALF], in_=wgo[:, 0:HALF])
         load_w(un_sb, un_words, 1)
@@ -123,18 +119,24 @@ def tile_list_tgn_rnn_kernel(
 
         tab_codes, tab_sc, x_codes, x_sc = {}, {}, {}, {}
 
-        def gather_table(half):
-            pairs = keep.tile([P, HALF], U32, name=f"pairs{half}", tag=("pairs", "raw1_0")[half])
-            nc.vector.tensor_copy(out=pairs[:], in_=tab[:].bitcast(U32).indirect(offsets_of(half)))
-            for a in range(PASSES):
-                sc = keep.tile([P, HALF], U8, name=f"tab_sc{half}_{a}", align_bytes=64)
-                nc.vector.tensor_copy(out=sc[:], in_=tab_planes[:, a, :].indirect(offsets_of(half)))
-                tab_sc[a, half] = sc
-            codes = keep.tile([P, PASSES, HALF], U16, name=f"tab_codes{half}", align_bytes=64)
+        def gather_words():
+            pairs = keep.tile([P, J], U32, name="pairs")
+            nc.vector.tensor_copy(out=pairs[:], in_=tab[:].bitcast(U32).indirect(offsets[:]))
+            return pairs
+
+        def part_words(pairs):
+            codes = keep.tile([P, PASSES, J], U16, name="tab_codes", align_bytes=64)
             nc.vector.tensor_copy(
                 out=codes[:], in_=pairs[:].bitcast(U16).rearrange("p (j d) -> p d j", d=PASSES)
             )
-            tab_codes[half] = codes
+            for half in range(2):
+                tab_codes[half] = codes[:, :, half * HALF : (half + 1) * HALF]
+
+        def gather_scales(half):
+            sc = keep.tile([P, PASSES, HALF], U8, name=f"tab_sc{half}", tag=("tab_sc", "raw1_0")[half], align_bytes=64)
+            for a in range(PASSES):
+                nc.vector.tensor_copy(out=sc[:, a, :], in_=tab_planes[:, a, :].indirect(offsets_of(half)))
+                tab_sc[a, half] = sc[:, a, :]
 
         def quantise_x(half):
             for a in range(PASSES):
@@ -143,8 +145,8 @@ def tile_list_tgn_rnn_kernel(
                 for i in range(HALF // PIECE):
                     cols = slice(i * PIECE, (i + 1) * PIECE)
                     grouped = ring.tile([P, PIECE, 4], BF16, name="grouped", align_bytes=64)
-                    dst = grouped[:].rearrange("p (c e) i -> p c i e", e=4)
-                    src = raw[a, half][:, :, cols].rearrange("p i (c e) -> p c i e", e=4)
+                    dst = grouped[:]
+                    src = raw[a, half][:, :, cols].rearrange("p i j -> p j i")
                     if (half, a, i) == (0, 1, 0):
                         nc.vector.tensor_copy(out=dst, in_=src)
                     else:
@@ -168,7 +170,7 @@ def tile_list_tgn_rnn_kernel(
                     lhsT=un_t[:, a, cols].bitcast(FP8X4),
                     lhsT_scale=w_planes[:, a, ncols],
                     rhs=tab_codes[half][:, a, :].bitcast(FP4X4),
-                    rhs_scale=tab_sc[a, half][:],
+                    rhs_scale=tab_sc[a, half],
                     start=(a == 0),
                     stop=False,
                 )
@@ -176,7 +178,7 @@ def tile_list_tgn_rnn_kernel(
                 nc.tensor.matmul_mx(
                     out=acc[:],
                     lhsT=wn_t[:, a, cols].bitcast(FP8X4),
-                    lhsT_scale=w_planes[4 + 4 * a : P, 0, ncols],
+                    lhsT_scale=w_planes[4:P, a, ncols],
                     rhs=x_codes[a, half][:].bitcast(FP8X4),
                     rhs_scale=x_sc[a, half][:],
                     start=False,
@@ -207,13 +209,16 @@ def tile_list_tgn_rnn_kernel(
         def store(r):
             nc.sync.dma_start(out=out[P * r : P * (r + 1), :], in_=windows[r % WINDOWS][:])
 
-        gather_table(0)
-        quantise_x(0)
-        gather_table(1)
         for w in windows:
-            for c in range(2):
-                nc.vector.memset(w[:, c * J : (c + 1) * J], 0.0)
+            nc.vector.memset(w[:], 0.0)
+        pairs = gather_words()
+        gather_scales(0)
+        part_words(pairs)
+        quantise_x(0)
+        gather_scales(1)
         quantise_x(1)
+        windows.append(keep.tile([P, T], F32, name="window_late", tag="raw0_1", align_bytes=64))
+        nc.vector.memset(windows[-1][:], 0.0)
         for r in range(EARLY):
             add_state(r, (0,))
             place(r, (0,))

@@ -54,12 +54,13 @@ def tile_list_tgn_rnn_kernel(
             (a, c): keep.tile([P, 4, HALF], F32, name=f"raw{a}_{c}", tag=f"raw{a}_{c}", align_bytes=64)
             for a in range(PASSES)
             for c in range(2)
+            if (a, c) != (1, 0)
         }
+        split = [keep.tile([P, 4, PIECE], F32, name=f"split{i}", tag=f"split{i}", align_bytes=64) for i in range(2)]
         wn_sb = [keep.tile([P, PASSES, (hi - lo) * P], I32, name=f"wn{lo}", align_bytes=64) for lo, hi in W_GROUPS]
         un_sb = [keep.tile([P, PASSES, (hi - lo) * P], I32, name=f"un{lo}", align_bytes=64) for lo, hi in W_GROUPS]
 
         nc.vector.memset(tab_planes[:].bitcast(I32), 0)
-        nc.vector.memset(w_planes[:].bitcast(I32), 0)
         nc.gpsimd.memset(bias_rows[:], 0.0)
         nc.gpsimd.dma_start(out=bias_rows[0:TILES, :], in_=bn.rearrange("(r p) -> r p", p=P))
         make_identity(nc, ident[:])
@@ -83,11 +84,16 @@ def tile_list_tgn_rnn_kernel(
             nc.sync.dma_start(out=h[r][:], in_=hT[P * r : P * (r + 1), :])
 
         nc.sync.dma_start(offsets[:], offs)
-        nc.sync.dma_start(out=tab[:], in_=tab_words[0].rearrange("p t b -> p (t b)").bitcast(I32))
         for r in range(4):
             load_scale_row(tab_planes, 0, tab_scales, r)
+        nc.sync.dma_start(out=tab[:], in_=tab_words[0].rearrange("p t b -> p (t b)").bitcast(I32))
         for a in range(PASSES):
-            load_x(a, 0)
+            if a == 0:
+                load_x(a, 0)
+            else:
+                for i in range(2):
+                    rows = x[512:1024, PIECE * i : PIECE * (i + 1)]
+                    nc.sync.dma_start(out=split[i][:], in_=rows.rearrange("(p i) j -> p i j", i=4))
             for r in (2 * a, 2 * a + 1):
                 load_scale_row(w_planes, 0, un_scales, r)
                 load_scale_row(w_planes, 4, wn_scales, r)
@@ -133,7 +139,7 @@ def tile_list_tgn_rnn_kernel(
                 tab_codes[half] = codes[:, :, half * HALF : (half + 1) * HALF]
 
         def gather_scales(half):
-            sc = keep.tile([P, PASSES, HALF], U8, name=f"tab_sc{half}", tag=("tab_sc", "raw1_0")[half], align_bytes=64)
+            sc = keep.tile([P, PASSES, HALF], U8, name=f"tab_sc{half}", tag=("tab_sc", "split1")[half], align_bytes=64)
             for a in range(PASSES):
                 nc.vector.tensor_copy(out=sc[:, a, :], in_=tab_planes[:, a, :].indirect(offsets_of(half)))
                 tab_sc[a, half] = sc[:, a, :]
@@ -145,12 +151,8 @@ def tile_list_tgn_rnn_kernel(
                 for i in range(HALF // PIECE):
                     cols = slice(i * PIECE, (i + 1) * PIECE)
                     grouped = ring.tile([P, PIECE, 4], BF16, name="grouped", align_bytes=64)
-                    dst = grouped[:]
-                    src = raw[a, half][:, :, cols].rearrange("p i j -> p j i")
-                    if (half, a, i) == (0, 1, 0):
-                        nc.vector.tensor_copy(out=dst, in_=src)
-                    else:
-                        nc.scalar.copy(out=dst, in_=src)
+                    src = split[i][:] if (a, half) == (1, 0) else raw[a, half][:, :, cols]
+                    nc.scalar.copy(out=grouped[:], in_=src.rearrange("p i j -> p j i"))
                     nc.vector.quantize_mx(
                         out=codes[:, cols].bitcast(FP8X4),
                         scales=sc[:, cols],
@@ -192,7 +194,10 @@ def tile_list_tgn_rnn_kernel(
         totals = [keep.tile([P, J], F32, name=f"total{r}") for r in range(TILES)]
 
         def add_state(r, halves):
-            act = acts.tile([P, J], F32, name="act")
+            if (r, halves) == (0, (0,)):
+                act = keep.tile([P, J], F32, name="first_act", tag="late")
+            else:
+                act = acts.tile([P, J], F32, name="act")
             for half in halves:
                 products(r, half, act[:, cols_of(half)])
             cols = slice(halves[0] * HALF, (halves[-1] + 1) * HALF)
@@ -211,16 +216,16 @@ def tile_list_tgn_rnn_kernel(
 
         for w in windows:
             nc.vector.memset(w[:], 0.0)
-        pairs = gather_words()
         gather_scales(0)
-        part_words(pairs)
+        part_words(gather_words())
         quantise_x(0)
         gather_scales(1)
         quantise_x(1)
-        windows.append(keep.tile([P, T], F32, name="window_late", tag="raw0_1", align_bytes=64))
-        nc.vector.memset(windows[-1][:], 0.0)
         for r in range(EARLY):
             add_state(r, (0,))
+            if r == 0:
+                windows.append(keep.tile([P, T], F32, name="window_late", tag="late"))
+                nc.gpsimd.memset(windows[-1][:], 0.0)
             place(r, (0,))
         for r in range(EARLY):
             add_state(r, (1,))

@@ -23,9 +23,9 @@ PASSES = 2
 HALF = 512
 PIECE = 256
 TILES = N // P
-EARLY = 3
-WINDOWS = 3
-W_GROUPS = ((0, 1), (1, 3), (3, TILES))
+EARLY = 5
+W_GROUPS = ((0, 1), (1, 3), (3, 5), (5, TILES))
+KIB = 1024
 
 
 def tile_list_tgn_rnn_kernel(
@@ -34,35 +34,39 @@ def tile_list_tgn_rnn_kernel(
     nc = tc.nc
     with ExitStack() as ctx:
         keep = ctx.enter_context(tc.tile_pool(name="keep", bufs=1))
+        shared = ctx.enter_context(tc.tile_pool(name="shared", bufs=1))
         ring = ctx.enter_context(tc.tile_pool(name="ring", bufs=4))
-        acts = ctx.enter_context(tc.tile_pool(name="acts", bufs=4))
+        acts = ctx.enter_context(tc.tile_pool(name="acts", bufs=1))
         psum = ctx.enter_context(tc.psum_pool(name="psum", bufs=4))
         psb = ctx.enter_context(tc.psum_pool(name="psb", bufs=1))
 
         offsets = keep.tile([P, J // 16], U16, name="offsets")
-        tab = keep.tile([P, T], I32, name="tab", align_bytes=64)
         tab_planes = keep.tile([P, PASSES, T], U8, name="tab_planes", align_bytes=64)
         w_planes = keep.tile([P, PASSES, N], U8, name="w_planes", align_bytes=64)
-        windows = [keep.tile([P, T], F32, name=f"window{i}") for i in range(WINDOWS - 1)]
-        bias_rows = keep.tile([P, P], F32, name="bias_rows")
+        windows = [keep.tile([P, T], F32, name="window0")]
+        vec_rows = keep.tile([P, P], F32, name="vec_rows")
         ident = keep.tile([P, P], F32, name="ident")
-        bias = keep.tile([P, TILES], F32, name="bias")
+        vec_cols = keep.tile([P, 2 * TILES], F32, name="vec_cols")
         warm = keep.tile([P, 1], F32, name="warm")
-        weights = keep.tile([P, J], F32, name="weights")
         h = [keep.tile([P, T], F32, name=f"h{r}") for r in range(TILES)]
-        raw = {
-            (a, c): keep.tile([P, 4, HALF], F32, name=f"raw{a}_{c}", tag=f"raw{a}_{c}", align_bytes=64)
-            for a in range(PASSES)
-            for c in range(2)
-            if (a, c) != (1, 0)
-        }
-        split = [keep.tile([P, 4, PIECE], F32, name=f"split{i}", tag=f"split{i}", align_bytes=64) for i in range(2)]
+        totals = [keep.tile([P, J], F32, name=f"total{r}") for r in range(TILES)]
         wn_sb = [keep.tile([P, PASSES, (hi - lo) * P], I32, name=f"wn{lo}", align_bytes=64) for lo, hi in W_GROUPS]
         un_sb = [keep.tile([P, PASSES, (hi - lo) * P], I32, name=f"un{lo}", align_bytes=64) for lo, hi in W_GROUPS]
 
+        tab = shared.tile([P, T], I32, name="tab", offset=0, align_bytes=64)
+        raw = {(0, 0): shared.tile([P, 4, HALF], F32, name="raw0_0", offset=8 * KIB, align_bytes=64)}
+        for a in range(PASSES):
+            raw[a, 1] = keep.tile([P, 4, HALF], F32, name=f"raw{a}_1")
+        split = [
+            shared.tile([P, 4, PIECE], F32, name=f"split{i}", offset=(16 * KIB, 33 * KIB)[i], align_bytes=64)
+            for i in range(2)
+        ]
+
         nc.vector.memset(tab_planes[:].bitcast(I32), 0)
-        nc.gpsimd.memset(bias_rows[:], 0.0)
-        nc.gpsimd.dma_start(out=bias_rows[0:TILES, :], in_=bn.rearrange("(r p) -> r p", p=P))
+        nc.vector.memset(windows[0][:], 0.0)
+        nc.gpsimd.memset(vec_rows[:], 0.0)
+        nc.gpsimd.dma_start(out=vec_rows[0:TILES, :], in_=bn.rearrange("(r p) -> r p", p=P))
+        nc.gpsimd.dma_start(out=vec_rows[TILES : 2 * TILES, :], in_=wgo[0].rearrange("(r p) -> r p", p=P))
         make_identity(nc, ident[:])
 
         def load_scale_row(planes, first_row, scales, r):
@@ -71,78 +75,69 @@ def tile_list_tgn_rnn_kernel(
                 in_=scales[:, r:16:4, :].bitcast(I32).rearrange("a q n -> q a n"),
             )
 
-        def load_x(a, c):
-            rows = x[512 * a : 512 * (a + 1), HALF * c : HALF * (c + 1)]
-            nc.sync.dma_start(out=raw[a, c][:], in_=rows.rearrange("(p i) j -> p i j", i=4))
+        def load_x(tile, a, lo, hi):
+            rows = x[512 * a : 512 * (a + 1), lo:hi]
+            nc.sync.dma_start(out=tile[:], in_=rows.rearrange("(p i) j -> p i j", i=4))
 
-        def load_w(tiles, words, g):
+        def load_w(g):
             lo, hi = W_GROUPS[g]
-            view = words.rearrange("a p n i -> p a (n i)")[:, :, 4 * P * lo : 4 * P * hi].bitcast(I32)
-            nc.sync.dma_start(out=tiles[g][:], in_=view)
+            for tiles, words in ((un_sb, un_words), (wn_sb, wn_words)):
+                view = words.rearrange("a p n i -> p a (n i)")[:, :, 4 * P * lo : 4 * P * hi].bitcast(I32)
+                nc.sync.dma_start(out=tiles[g][:], in_=view)
+
+        def load_w_scales(rows):
+            for r in rows:
+                load_scale_row(w_planes, 0, un_scales, r)
+                load_scale_row(w_planes, 4, wn_scales, r)
 
         def load_h(r):
             nc.sync.dma_start(out=h[r][:], in_=hT[P * r : P * (r + 1), :])
 
         nc.sync.dma_start(offsets[:], offs)
+        nc.sync.dma_start(out=tab[:], in_=tab_words[0].rearrange("p t b -> p (t b)").bitcast(I32))
         for r in range(4):
             load_scale_row(tab_planes, 0, tab_scales, r)
-        nc.sync.dma_start(out=tab[:], in_=tab_words[0].rearrange("p t b -> p (t b)").bitcast(I32))
-        for a in range(PASSES):
-            if a == 0:
-                load_x(a, 0)
-            else:
-                for i in range(2):
-                    rows = x[512:1024, PIECE * i : PIECE * (i + 1)]
-                    nc.sync.dma_start(out=split[i][:], in_=rows.rearrange("(p i) j -> p i j", i=4))
-            for r in (2 * a, 2 * a + 1):
-                load_scale_row(w_planes, 0, un_scales, r)
-                load_scale_row(w_planes, 4, wn_scales, r)
-        load_w(un_sb, un_words, 0)
-        load_w(wn_sb, wn_words, 0)
+        load_x(raw[0, 0], 0, 0, HALF)
+        load_w_scales((0, 1))
+        for i in range(2):
+            load_x(split[i], 1, PIECE * i, PIECE * (i + 1))
+        load_w_scales((2, 3))
+        load_w(0)
         load_h(0)
-        nc.sync.dma_start(out=weights[:, 0:HALF], in_=wgo[:, 0:HALF])
-        load_w(un_sb, un_words, 1)
-        load_w(wn_sb, wn_words, 1)
+        load_w(1)
         load_h(1)
-        for a in range(PASSES):
-            load_x(a, 1)
         load_h(2)
-        nc.sync.dma_start(out=weights[:, HALF:J], in_=wgo[:, HALF:J])
-        load_w(un_sb, un_words, 2)
-        load_w(wn_sb, wn_words, 2)
-        for r in range(3, TILES):
+        load_w(2)
+        load_h(3)
+        load_x(raw[0, 1], 0, HALF, J)
+        load_x(raw[1, 1], 1, HALF, J)
+        load_h(4)
+        load_w(3)
+        for r in range(EARLY, TILES):
             load_h(r)
 
         nc.scalar.activation(out=warm[:], in_=ident[:, 0:1], func=TANH)
 
+        turned = psb.tile([P, P], F32, name="turned")
+        nc.tensor.transpose(turned[:], vec_rows[:], ident[:])
+        nc.scalar.copy(out=vec_cols[:], in_=turned[:, 0 : 2 * TILES])
+        spread = [psb.tile([P, HALF], F32, name=f"spread{half}") for half in range(2)]
+        for m in range(TILES):
+            column = vec_cols[:, TILES + m : TILES + m + 1].to_broadcast([P, P])
+            nc.tensor.transpose(spread[m // 4][:, (m % 4) * P : (m % 4 + 1) * P], column, ident[:])
 
-        bias_t = psb.tile([P, P], F32, name="bias_t")
-        nc.tensor.transpose(bias_t[:], bias_rows[:], ident[:])
-        nc.scalar.copy(out=bias[:], in_=bias_t[:, 0:TILES])
+        def cols_of(half):
+            return slice(half * HALF, (half + 1) * HALF)
 
-        def offsets_of(half):
-            return offsets[:, half * (HALF // 16) : (half + 1) * (HALF // 16)]
+        def offsets_of(cols):
+            return offsets[:, cols.start // 16 : cols.stop // 16]
 
-        tab_codes, tab_sc, x_codes, x_sc = {}, {}, {}, {}
+        tab_sc, x_codes, x_sc = {}, {}, {}
 
-        def gather_words():
-            pairs = keep.tile([P, J], U32, name="pairs")
-            nc.vector.tensor_copy(out=pairs[:], in_=tab[:].bitcast(U32).indirect(offsets[:]))
-            return pairs
-
-        def part_words(pairs):
-            codes = keep.tile([P, PASSES, J], U16, name="tab_codes", align_bytes=64)
-            nc.vector.tensor_copy(
-                out=codes[:], in_=pairs[:].bitcast(U16).rearrange("p (j d) -> p d j", d=PASSES)
-            )
-            for half in range(2):
-                tab_codes[half] = codes[:, :, half * HALF : (half + 1) * HALF]
-
-        def gather_scales(half):
-            sc = keep.tile([P, PASSES, HALF], U8, name=f"tab_sc{half}", tag=("tab_sc", "split1")[half], align_bytes=64)
+        def gather_scales(half, sc):
             for a in range(PASSES):
-                nc.vector.tensor_copy(out=sc[:, a, :], in_=tab_planes[:, a, :].indirect(offsets_of(half)))
-                tab_sc[a, half] = sc[:, a, :]
+                nc.vector.tensor_copy(out=sc[:, a, :], in_=tab_planes[:, a, :].indirect(offsets_of(cols_of(half))))
+            tab_sc[half] = sc
 
         def quantise_x(half):
             for a in range(PASSES):
@@ -162,78 +157,84 @@ def tile_list_tgn_rnn_kernel(
 
         def products(r, half, into):
             g = [i for i, (lo, hi) in enumerate(W_GROUPS) if lo <= r < hi][0]
-            un_t, wn_t, c0 = un_sb[g], wn_sb[g], (r - W_GROUPS[g][0]) * P
+            c0 = (r - W_GROUPS[g][0]) * P
             cols = slice(c0, c0 + P)
             ncols = slice(r * P, (r + 1) * P)
             acc = psum.tile([P, HALF], F32, name="acc")
             for a in range(PASSES):
                 nc.tensor.matmul_mx(
                     out=acc[:],
-                    lhsT=un_t[:, a, cols].bitcast(FP8X4),
+                    lhsT=un_sb[g][:, a, cols].bitcast(FP8X4),
                     lhsT_scale=w_planes[:, a, ncols],
-                    rhs=tab_codes[half][:, a, :].bitcast(FP4X4),
-                    rhs_scale=tab_sc[a, half],
+                    rhs=tab_codes[:, a, cols_of(half)].bitcast(FP4X4),
+                    rhs_scale=tab_sc[half][:, a, :],
                     start=(a == 0),
                     stop=False,
                 )
             for a in range(PASSES):
                 nc.tensor.matmul_mx(
                     out=acc[:],
-                    lhsT=wn_t[:, a, cols].bitcast(FP8X4),
+                    lhsT=wn_sb[g][:, a, cols].bitcast(FP8X4),
                     lhsT_scale=w_planes[4:P, a, ncols],
                     rhs=x_codes[a, half][:].bitcast(FP8X4),
                     rhs_scale=x_sc[a, half][:],
                     start=False,
                     stop=(a == PASSES - 1),
                 )
-            nc.scalar.activation(out=into, in_=acc[:], func=TANH, bias=bias[:, r : r + 1])
+            nc.scalar.activation(out=into, in_=acc[:], func=TANH, bias=vec_cols[:, r : r + 1])
 
-        def cols_of(half):
-            return slice(half * HALF, (half + 1) * HALF)
-
-        totals = [keep.tile([P, J], F32, name=f"total{r}") for r in range(TILES)]
-
-        def add_state(r, halves):
-            if (r, halves) == (0, (0,)):
-                act = keep.tile([P, J], F32, name="first_act", tag="late")
-            else:
-                act = acts.tile([P, J], F32, name="act")
-            for half in halves:
-                products(r, half, act[:, cols_of(half)])
+        def add_state(r, halves, act):
             cols = slice(halves[0] * HALF, (halves[-1] + 1) * HALF)
-            offs_ap = offsets[:, cols.start // 16 : cols.stop // 16]
-            nc.vector.tensor_tensor(out=totals[r][:, cols], in0=h[r][:].indirect(offs_ap), in1=act[:, cols], op=ADD)
+            for i, half in enumerate(halves):
+                products(r, half, act[:, cols_of(i)])
+            nc.vector.tensor_tensor(
+                out=totals[r][:, cols],
+                in0=h[r][:].indirect(offsets_of(cols)),
+                in1=act[:, 0 : len(halves) * HALF],
+                op=ADD,
+            )
 
         def place(r, halves):
             cols = slice(halves[0] * HALF, (halves[-1] + 1) * HALF)
-            offs_ap = offsets[:, cols.start // 16 : cols.stop // 16]
             nc.vector.tensor_tensor(
-                out=windows[r % WINDOWS][:].indirect(offs_ap), in0=totals[r][:, cols], in1=weights[:, cols], op=MULT
+                out=windows[r % EARLY][:].indirect(offsets_of(cols)),
+                in0=totals[r][:, cols],
+                in1=weights[:, cols],
+                op=MULT,
             )
 
         def store(r):
-            nc.sync.dma_start(out=out[P * r : P * (r + 1), :], in_=windows[r % WINDOWS][:])
+            nc.sync.dma_start(out=out[P * r : P * (r + 1), :], in_=windows[r % EARLY][:])
 
-        for w in windows:
-            nc.vector.memset(w[:], 0.0)
-        gather_scales(0)
-        part_words(gather_words())
+        pairs = shared.tile([P, J], U32, name="pairs", offset=20 * KIB, align_bytes=64)
+        nc.vector.tensor_copy(out=pairs[:], in_=tab[:].bitcast(U32).indirect(offsets[:]))
+        gather_scales(0, keep.tile([P, PASSES, HALF], U8, name="tab_sc0", align_bytes=64))
+        tab_codes = keep.tile([P, PASSES, J], U16, name="tab_codes", align_bytes=64)
+        nc.vector.tensor_copy(out=tab_codes[:], in_=pairs[:].bitcast(U16).rearrange("p (j d) -> p d j", d=PASSES))
         quantise_x(0)
-        gather_scales(1)
+        gather_scales(1, shared.tile([P, PASSES, HALF], U8, name="tab_sc1", offset=36 * KIB, align_bytes=64))
+        weights = shared.tile([P, J], F32, name="weights", offset=32 * KIB, align_bytes=64)
+        for half in range(2):
+            nc.scalar.copy(out=weights[:, cols_of(half)], in_=spread[half][:])
         quantise_x(1)
         for r in range(EARLY):
-            add_state(r, (0,))
-            if r == 0:
-                windows.append(keep.tile([P, T], F32, name="window_late", tag="late"))
-                nc.gpsimd.memset(windows[-1][:], 0.0)
+            if r < 2:
+                act = shared.tile([P, HALF], F32, name=f"early_act{r}", offset=(16 * r + 7) * KIB, align_bytes=64)
+            else:
+                act = acts.tile([P, HALF], F32, name=f"act{r}_0")
+            add_state(r, (0,), act)
+            if r < 2:
+                for i in (2 * r, 2 * r + 1):
+                    windows.append(shared.tile([P, T], F32, name=f"window{i + 1}", offset=8 * KIB * i, align_bytes=64))
+                    nc.gpsimd.memset(windows[-1][:], 0.0)
             place(r, (0,))
         for r in range(EARLY):
-            add_state(r, (1,))
+            add_state(r, (1,), acts.tile([P, HALF], F32, name=f"act{r}_1"))
         for r in range(EARLY):
             place(r, (1,))
             store(r)
         for r in range(EARLY, TILES):
-            add_state(r, (0, 1))
+            add_state(r, (0, 1), acts.tile([P, J], F32, name=f"act{r}"))
         for r in range(EARLY, TILES):
             place(r, (0, 1))
             store(r)

@@ -23,8 +23,8 @@ PASSES = 2
 HALF = 512
 PIECE = 256
 TILES = N // P
-EARLY = 5
-W_GROUPS = ((0, 1), (1, 3), (3, 5), (5, TILES))
+EARLY = 4
+W_GROUPS = ((0, 1), (1, 2), (2, 4), (4, TILES))
 KIB = 1024
 
 
@@ -35,7 +35,7 @@ def tile_list_tgn_rnn_kernel(
     with ExitStack() as ctx:
         keep = ctx.enter_context(tc.tile_pool(name="keep", bufs=1))
         shared = ctx.enter_context(tc.tile_pool(name="shared", bufs=1))
-        ring = ctx.enter_context(tc.tile_pool(name="ring", bufs=4))
+        ring = ctx.enter_context(tc.tile_pool(name="ring", bufs=3))
         acts = ctx.enter_context(tc.tile_pool(name="acts", bufs=1))
         psum = ctx.enter_context(tc.psum_pool(name="psum", bufs=4))
         psb = ctx.enter_context(tc.psum_pool(name="psb", bufs=1))
@@ -43,27 +43,25 @@ def tile_list_tgn_rnn_kernel(
         offsets = keep.tile([P, J // 16], U16, name="offsets")
         tab_planes = keep.tile([P, PASSES, T], U8, name="tab_planes", align_bytes=64)
         w_planes = keep.tile([P, PASSES, N], U8, name="w_planes", align_bytes=64)
-        windows = [keep.tile([P, T], F32, name="window0")]
+        windows = [keep.tile([P, T], F32, name=f"window{i}") for i in range(EARLY - 1)]
         vec_rows = keep.tile([P, P], F32, name="vec_rows")
         ident = keep.tile([P, P], F32, name="ident")
         vec_cols = keep.tile([P, 2 * TILES], F32, name="vec_cols")
-        warm = keep.tile([P, 1], F32, name="warm")
         h = [keep.tile([P, T], F32, name=f"h{r}") for r in range(TILES)]
         totals = [keep.tile([P, J], F32, name=f"total{r}") for r in range(TILES)]
         wn_sb = [keep.tile([P, PASSES, (hi - lo) * P], I32, name=f"wn{lo}", align_bytes=64) for lo, hi in W_GROUPS]
         un_sb = [keep.tile([P, PASSES, (hi - lo) * P], I32, name=f"un{lo}", align_bytes=64) for lo, hi in W_GROUPS]
 
         tab = shared.tile([P, T], I32, name="tab", offset=0, align_bytes=64)
-        raw = {(0, 0): shared.tile([P, 4, HALF], F32, name="raw0_0", offset=8 * KIB, align_bytes=64)}
-        for a in range(PASSES):
-            raw[a, 1] = keep.tile([P, 4, HALF], F32, name=f"raw{a}_1")
+        raw = {(a, c): keep.tile([P, 4, HALF], F32, name=f"raw{a}_{c}") for a, c in ((0, 0), (0, 1), (1, 1))}
         split = [
-            shared.tile([P, 4, PIECE], F32, name=f"split{i}", offset=(16 * KIB, 33 * KIB)[i], align_bytes=64)
-            for i in range(2)
+            keep.tile([P, 4, PIECE], F32, name="split0"),
+            shared.tile([P, 4, PIECE], F32, name="split1", offset=9 * KIB, align_bytes=64),
         ]
 
         nc.vector.memset(tab_planes[:].bitcast(I32), 0)
-        nc.vector.memset(windows[0][:], 0.0)
+        for window in windows:
+            nc.vector.memset(window[:], 0.0)
         nc.gpsimd.memset(vec_rows[:], 0.0)
         nc.gpsimd.dma_start(out=vec_rows[0:TILES, :], in_=bn.rearrange("(r p) -> r p", p=P))
         nc.gpsimd.dma_start(out=vec_rows[TILES : 2 * TILES, :], in_=wgo[0].rearrange("(r p) -> r p", p=P))
@@ -106,17 +104,14 @@ def tile_list_tgn_rnn_kernel(
         load_h(0)
         load_w(1)
         load_h(1)
-        load_h(2)
         load_w(2)
+        load_h(2)
+        for a in range(PASSES):
+            load_x(raw[a, 1], a, HALF, J)
         load_h(3)
-        load_x(raw[0, 1], 0, HALF, J)
-        load_x(raw[1, 1], 1, HALF, J)
-        load_h(4)
         load_w(3)
         for r in range(EARLY, TILES):
             load_h(r)
-
-        nc.scalar.activation(out=warm[:], in_=ident[:, 0:1], func=TANH)
 
         turned = psb.tile([P, P], F32, name="turned")
         nc.tensor.transpose(turned[:], vec_rows[:], ident[:])
@@ -143,11 +138,12 @@ def tile_list_tgn_rnn_kernel(
             for a in range(PASSES):
                 codes = keep.tile([P, HALF], U32, name=f"x_codes{half}_{a}", align_bytes=64)
                 sc = keep.tile([P, HALF], U8, name=f"x_sc{half}_{a}", align_bytes=64)
-                for i in range(HALF // PIECE):
-                    cols = slice(i * PIECE, (i + 1) * PIECE)
-                    grouped = ring.tile([P, PIECE, 4], BF16, name="grouped", align_bytes=64)
-                    src = split[i][:] if (a, half) == (1, 0) else raw[a, half][:, :, cols]
-                    nc.scalar.copy(out=grouped[:], in_=src.rearrange("p i j -> p j i"))
+                sources = split if (a, half) == (1, 0) else [raw[a, half]]
+                width = HALF // len(sources)
+                for i, source in enumerate(sources):
+                    cols = slice(i * width, (i + 1) * width)
+                    grouped = ring.tile([P, width, 4], BF16, name="grouped", align_bytes=64)
+                    nc.scalar.copy(out=grouped[:], in_=source[:].rearrange("p i j -> p j i"))
                     nc.vector.quantize_mx(
                         out=codes[:, cols].bitcast(FP8X4),
                         scales=sc[:, cols],
@@ -206,27 +202,26 @@ def tile_list_tgn_rnn_kernel(
         def store(r):
             nc.sync.dma_start(out=out[P * r : P * (r + 1), :], in_=windows[r % EARLY][:])
 
-        pairs = shared.tile([P, J], U32, name="pairs", offset=20 * KIB, align_bytes=64)
+        pairs = keep.tile([P, J], U32, name="pairs")
         nc.vector.tensor_copy(out=pairs[:], in_=tab[:].bitcast(U32).indirect(offsets[:]))
         gather_scales(0, keep.tile([P, PASSES, HALF], U8, name="tab_sc0", align_bytes=64))
         tab_codes = keep.tile([P, PASSES, J], U16, name="tab_codes", align_bytes=64)
         nc.vector.tensor_copy(out=tab_codes[:], in_=pairs[:].bitcast(U16).rearrange("p (j d) -> p d j", d=PASSES))
         quantise_x(0)
-        gather_scales(1, shared.tile([P, PASSES, HALF], U8, name="tab_sc1", offset=36 * KIB, align_bytes=64))
-        weights = shared.tile([P, J], F32, name="weights", offset=32 * KIB, align_bytes=64)
+        gather_scales(1, shared.tile([P, PASSES, HALF], U8, name="tab_sc1", offset=12 * KIB, align_bytes=64))
+        weights = shared.tile([P, J], F32, name="weights", offset=8 * KIB, align_bytes=64)
         for half in range(2):
             nc.scalar.copy(out=weights[:, cols_of(half)], in_=spread[half][:])
         quantise_x(1)
         for r in range(EARLY):
-            if r < 2:
-                act = shared.tile([P, HALF], F32, name=f"early_act{r}", offset=(16 * r + 7) * KIB, align_bytes=64)
+            if r == 0:
+                act = shared.tile([P, HALF], F32, name="first_act", offset=0, align_bytes=64)
             else:
                 act = acts.tile([P, HALF], F32, name=f"act{r}_0")
             add_state(r, (0,), act)
-            if r < 2:
-                for i in (2 * r, 2 * r + 1):
-                    windows.append(shared.tile([P, T], F32, name=f"window{i + 1}", offset=8 * KIB * i, align_bytes=64))
-                    nc.gpsimd.memset(windows[-1][:], 0.0)
+            if r == 0:
+                windows.append(shared.tile([P, T], F32, name="late_window", offset=0, align_bytes=64))
+                nc.gpsimd.memset(windows[-1][:], 0.0)
             place(r, (0,))
         for r in range(EARLY):
             add_state(r, (1,), acts.tile([P, HALF], F32, name=f"act{r}_1"))
@@ -234,7 +229,7 @@ def tile_list_tgn_rnn_kernel(
             place(r, (1,))
             store(r)
         for r in range(EARLY, TILES):
-            add_state(r, (0, 1), acts.tile([P, J], F32, name=f"act{r}"))
+            add_state(r, (0, 1), acts.tile([P, J], F32, name="act", bufs=2))
         for r in range(EARLY, TILES):
             place(r, (0, 1))
             store(r)

@@ -35,7 +35,7 @@ def tile_list_tgn_rnn_kernel(
     with ExitStack() as ctx:
         keep = ctx.enter_context(tc.tile_pool(name="keep", bufs=1))
         shared = ctx.enter_context(tc.tile_pool(name="shared", bufs=1))
-        ring = ctx.enter_context(tc.tile_pool(name="ring", bufs=3))
+        ring = ctx.enter_context(tc.tile_pool(name="ring", bufs=4))
         acts = ctx.enter_context(tc.tile_pool(name="acts", bufs=1))
         psum = ctx.enter_context(tc.psum_pool(name="psum", bufs=4))
         psb = ctx.enter_context(tc.psum_pool(name="psb", bufs=1))
@@ -43,7 +43,7 @@ def tile_list_tgn_rnn_kernel(
         offsets = keep.tile([P, J // 16], U16, name="offsets")
         tab_planes = keep.tile([P, PASSES, T], U8, name="tab_planes", align_bytes=64)
         w_planes = keep.tile([P, PASSES, N], U8, name="w_planes", align_bytes=64)
-        windows = [keep.tile([P, T], F32, name=f"window{i}") for i in range(EARLY - 1)]
+        windows = [keep.tile([P, T], F32, name="window0")]
         vec_rows = keep.tile([P, P], F32, name="vec_rows")
         ident = keep.tile([P, P], F32, name="ident")
         vec_cols = keep.tile([P, 2 * TILES], F32, name="vec_cols")
@@ -52,19 +52,18 @@ def tile_list_tgn_rnn_kernel(
         wn_sb = [keep.tile([P, PASSES, (hi - lo) * P], I32, name=f"wn{lo}", align_bytes=64) for lo, hi in W_GROUPS]
         un_sb = [keep.tile([P, PASSES, (hi - lo) * P], I32, name=f"un{lo}", align_bytes=64) for lo, hi in W_GROUPS]
 
+        weights = keep.tile([P, J], F32, name="weights")
         tab = shared.tile([P, T], I32, name="tab", offset=0, align_bytes=64)
-        raw = {(a, c): keep.tile([P, 4, HALF], F32, name=f"raw{a}_{c}") for a, c in ((0, 0), (0, 1), (1, 1))}
-        split = [
-            keep.tile([P, 4, PIECE], F32, name="split0"),
-            shared.tile([P, 4, PIECE], F32, name="split1", offset=9 * KIB, align_bytes=64),
-        ]
+        raw = {
+            (0, 0): shared.tile([P, 4, HALF], F32, name="raw0_0", offset=8 * KIB, align_bytes=64),
+            (1, 0): keep.tile([P, 4, HALF], F32, name="raw1_0", tag="raw1_0", align_bytes=64),
+            (0, 1): keep.tile([P, 4, HALF], F32, name="raw0_1"),
+            (1, 1): keep.tile([P, 4, HALF], F32, name="raw1_1"),
+        }
 
         nc.vector.memset(tab_planes[:].bitcast(I32), 0)
-        for window in windows:
-            nc.vector.memset(window[:], 0.0)
+        nc.vector.memset(windows[0][:], 0.0)
         nc.gpsimd.memset(vec_rows[:], 0.0)
-        nc.gpsimd.dma_start(out=vec_rows[0:TILES, :], in_=bn.rearrange("(r p) -> r p", p=P))
-        nc.gpsimd.dma_start(out=vec_rows[TILES : 2 * TILES, :], in_=wgo[0].rearrange("(r p) -> r p", p=P))
         make_identity(nc, ident[:])
 
         def load_scale_row(planes, first_row, scales, r):
@@ -93,13 +92,13 @@ def tile_list_tgn_rnn_kernel(
 
         nc.sync.dma_start(offsets[:], offs)
         nc.sync.dma_start(out=tab[:], in_=tab_words[0].rearrange("p t b -> p (t b)").bitcast(I32))
+        nc.sync.dma_start(out=vec_rows[0:TILES, :], in_=bn.rearrange("(r p) -> r p", p=P))
+        nc.sync.dma_start(out=vec_rows[TILES : 2 * TILES, :], in_=wgo[0].rearrange("(r p) -> r p", p=P))
         for r in range(4):
             load_scale_row(tab_planes, 0, tab_scales, r)
-        load_x(raw[0, 0], 0, 0, HALF)
-        load_w_scales((0, 1))
-        for i in range(2):
-            load_x(split[i], 1, PIECE * i, PIECE * (i + 1))
-        load_w_scales((2, 3))
+        for a in range(PASSES):
+            load_x(raw[a, 0], a, 0, HALF)
+            load_w_scales((2 * a, 2 * a + 1))
         load_w(0)
         load_h(0)
         load_w(1)
@@ -120,6 +119,8 @@ def tile_list_tgn_rnn_kernel(
         for m in range(TILES):
             column = vec_cols[:, TILES + m : TILES + m + 1].to_broadcast([P, P])
             nc.tensor.transpose(spread[m // 4][:, (m % 4) * P : (m % 4 + 1) * P], column, ident[:])
+        for half in range(2):
+            nc.scalar.copy(out=weights[:, half * HALF : (half + 1) * HALF], in_=spread[half][:])
 
         def cols_of(half):
             return slice(half * HALF, (half + 1) * HALF)
@@ -138,12 +139,15 @@ def tile_list_tgn_rnn_kernel(
             for a in range(PASSES):
                 codes = keep.tile([P, HALF], U32, name=f"x_codes{half}_{a}", align_bytes=64)
                 sc = keep.tile([P, HALF], U8, name=f"x_sc{half}_{a}", align_bytes=64)
-                sources = split if (a, half) == (1, 0) else [raw[a, half]]
-                width = HALF // len(sources)
-                for i, source in enumerate(sources):
-                    cols = slice(i * width, (i + 1) * width)
-                    grouped = ring.tile([P, width, 4], BF16, name="grouped", align_bytes=64)
-                    nc.scalar.copy(out=grouped[:], in_=source[:].rearrange("p i j -> p j i"))
+                for i in range(HALF // PIECE):
+                    cols = slice(i * PIECE, (i + 1) * PIECE)
+                    grouped = ring.tile([P, PIECE, 4], BF16, name="grouped", align_bytes=64)
+                    dst = grouped[:].rearrange("p (c e) i -> p c i e", e=4)
+                    src = raw[a, half][:, :, cols].rearrange("p i (c e) -> p c i e", e=4)
+                    if (half, a, i) == (0, 1, 0):
+                        nc.vector.tensor_copy(out=dst, in_=src)
+                    else:
+                        nc.scalar.copy(out=dst, in_=src)
                     nc.vector.quantize_mx(
                         out=codes[:, cols].bitcast(FP8X4),
                         scales=sc[:, cols],
@@ -208,19 +212,16 @@ def tile_list_tgn_rnn_kernel(
         tab_codes = keep.tile([P, PASSES, J], U16, name="tab_codes", align_bytes=64)
         nc.vector.tensor_copy(out=tab_codes[:], in_=pairs[:].bitcast(U16).rearrange("p (j d) -> p d j", d=PASSES))
         quantise_x(0)
-        gather_scales(1, shared.tile([P, PASSES, HALF], U8, name="tab_sc1", offset=12 * KIB, align_bytes=64))
-        weights = shared.tile([P, J], F32, name="weights", offset=8 * KIB, align_bytes=64)
-        for half in range(2):
-            nc.scalar.copy(out=weights[:, cols_of(half)], in_=spread[half][:])
+        gather_scales(1, keep.tile([P, PASSES, HALF], U8, name="tab_sc1", tag="raw1_0", align_bytes=64))
         quantise_x(1)
         for r in range(EARLY):
-            if r == 0:
-                act = shared.tile([P, HALF], F32, name="first_act", offset=0, align_bytes=64)
+            if r < 2:
+                act = shared.tile([P, HALF], F32, name=f"act{r}_0", offset=(7, 16)[r] * KIB, align_bytes=64)
             else:
                 act = acts.tile([P, HALF], F32, name=f"act{r}_0")
             add_state(r, (0,), act)
-            if r == 0:
-                windows.append(shared.tile([P, T], F32, name="late_window", offset=0, align_bytes=64))
+            for i in {0: (0, 1), 1: (2,)}.get(r, ()):
+                windows.append(shared.tile([P, T], F32, name=f"window{i + 1}", offset=8 * KIB * i, align_bytes=64))
                 nc.gpsimd.memset(windows[-1][:], 0.0)
             place(r, (0,))
         for r in range(EARLY):
@@ -229,7 +230,7 @@ def tile_list_tgn_rnn_kernel(
             place(r, (1,))
             store(r)
         for r in range(EARLY, TILES):
-            add_state(r, (0, 1), acts.tile([P, J], F32, name="act", bufs=2))
+            add_state(r, (0, 1), acts.tile([P, J], F32, name="act", bufs=3))
         for r in range(EARLY, TILES):
             place(r, (0, 1))
             store(r)

@@ -24,8 +24,9 @@ HALF = 512
 PIECE = 256
 TILES = N // P
 EARLY = 4
-W_GROUPS = ((0, 1), (1, 2), (2, 4), (4, TILES))
+W_GROUPS = ((0, 1), (1, 3), (3, 4), (4, TILES))
 KIB = 1024
+ALIGN = 256
 
 
 def tile_list_tgn_rnn_kernel(
@@ -41,24 +42,24 @@ def tile_list_tgn_rnn_kernel(
         psb = ctx.enter_context(tc.psum_pool(name="psb", bufs=1))
 
         offsets = keep.tile([P, J // 16], U16, name="offsets")
-        tab_planes = keep.tile([P, PASSES, T], U8, name="tab_planes", align_bytes=64)
-        w_planes = keep.tile([P, PASSES, N], U8, name="w_planes", align_bytes=64)
-        windows = [keep.tile([P, T], F32, name="window0")]
-        vec_rows = keep.tile([P, P], F32, name="vec_rows")
+        tab_planes = keep.tile([P, PASSES, T], U8, name="tab_planes", align_bytes=ALIGN)
+        w_planes = [keep.tile([P, PASSES, HALF], U8, name=f"w_planes{g}", align_bytes=ALIGN) for g in range(2)]
+        windows = {0: keep.tile([P, T], F32, name="window0", align_bytes=ALIGN)}
+        vec_rows = keep.tile([P, P], F32, name="vec_rows", align_bytes=ALIGN)
         ident = keep.tile([P, P], F32, name="ident")
         vec_cols = keep.tile([P, 2 * TILES], F32, name="vec_cols")
-        h = [keep.tile([P, T], F32, name=f"h{r}") for r in range(TILES)]
+        h = [keep.tile([P, T], F32, name=f"h{r}", align_bytes=ALIGN) for r in range(TILES)]
         totals = [keep.tile([P, J], F32, name=f"total{r}") for r in range(TILES)]
-        wn_sb = [keep.tile([P, PASSES, (hi - lo) * P], I32, name=f"wn{lo}", align_bytes=64) for lo, hi in W_GROUPS]
-        un_sb = [keep.tile([P, PASSES, (hi - lo) * P], I32, name=f"un{lo}", align_bytes=64) for lo, hi in W_GROUPS]
+        wn_sb = [keep.tile([P, PASSES, (hi - lo) * P], I32, name=f"wn{lo}", align_bytes=ALIGN) for lo, hi in W_GROUPS]
+        un_sb = [keep.tile([P, PASSES, (hi - lo) * P], I32, name=f"un{lo}", align_bytes=ALIGN) for lo, hi in W_GROUPS]
 
         weights = keep.tile([P, J], F32, name="weights")
-        tab = shared.tile([P, T], I32, name="tab", offset=0, align_bytes=64)
+        tab = shared.tile([P, T], I32, name="tab", offset=0, align_bytes=ALIGN)
         raw = {
-            (0, 0): shared.tile([P, 4, HALF], F32, name="raw0_0", offset=8 * KIB, align_bytes=64),
-            (1, 0): keep.tile([P, 4, HALF], F32, name="raw1_0", tag="raw1_0", align_bytes=64),
-            (0, 1): keep.tile([P, 4, HALF], F32, name="raw0_1"),
-            (1, 1): keep.tile([P, 4, HALF], F32, name="raw1_1"),
+            (0, 0): shared.tile([P, 4, HALF], F32, name="raw0_0", offset=8 * KIB, align_bytes=ALIGN),
+            (1, 0): keep.tile([P, 4, HALF], F32, name="raw1_0", tag="raw1_0", align_bytes=ALIGN),
+            (0, 1): keep.tile([P, 4, HALF], F32, name="raw0_1", align_bytes=ALIGN),
+            (1, 1): keep.tile([P, 4, HALF], F32, name="raw1_1", align_bytes=ALIGN),
         }
 
         nc.vector.memset(tab_planes[:].bitcast(I32), 0)
@@ -76,16 +77,16 @@ def tile_list_tgn_rnn_kernel(
             rows = x[512 * a : 512 * (a + 1), lo:hi]
             nc.sync.dma_start(out=tile[:], in_=rows.rearrange("(p i) j -> p i j", i=4))
 
-        def load_w(g):
+        def load_w(g, which=(0, 1)):
             lo, hi = W_GROUPS[g]
-            for tiles, words in ((un_sb, un_words), (wn_sb, wn_words)):
+            for tiles, words in [((un_sb, un_words), (wn_sb, wn_words))[i] for i in which]:
                 view = words.rearrange("a p n i -> p a (n i)")[:, :, 4 * P * lo : 4 * P * hi].bitcast(I32)
                 nc.sync.dma_start(out=tiles[g][:], in_=view)
 
-        def load_w_scales(rows):
+        def load_w_scales(g, rows):
             for r in rows:
-                load_scale_row(w_planes, 0, un_scales, r)
-                load_scale_row(w_planes, 4, wn_scales, r)
+                load_scale_row(w_planes[g], 0, un_scales[:, :, g * HALF : (g + 1) * HALF], r)
+                load_scale_row(w_planes[g], 4, wn_scales[:, :, g * HALF : (g + 1) * HALF], r)
 
         def load_h(r):
             nc.sync.dma_start(out=h[r][:], in_=hT[P * r : P * (r + 1), :])
@@ -98,17 +99,21 @@ def tile_list_tgn_rnn_kernel(
             load_scale_row(tab_planes, 0, tab_scales, r)
         for a in range(PASSES):
             load_x(raw[a, 0], a, 0, HALF)
-            load_w_scales((2 * a, 2 * a + 1))
+            load_w_scales(0, (2 * a, 2 * a + 1))
         load_w(0)
         load_h(0)
-        load_w(1)
+        load_w(1, (0,))
         load_h(1)
-        load_w(2)
+        load_w(1, (1,))
         load_h(2)
+        load_w(2)
         for a in range(PASSES):
             load_x(raw[a, 1], a, HALF, J)
         load_h(3)
-        load_w(3)
+        load_w_scales(1, (0, 1))
+        load_w(3, (0,))
+        load_w_scales(1, (2, 3))
+        load_w(3, (1,))
         for r in range(EARLY, TILES):
             load_h(r)
 
@@ -159,13 +164,14 @@ def tile_list_tgn_rnn_kernel(
             g = [i for i, (lo, hi) in enumerate(W_GROUPS) if lo <= r < hi][0]
             c0 = (r - W_GROUPS[g][0]) * P
             cols = slice(c0, c0 + P)
-            ncols = slice(r * P, (r + 1) * P)
+            gs, n0 = divmod(r * P, HALF)
+            ncols = slice(n0, n0 + P)
             acc = psum.tile([P, HALF], F32, name="acc")
             for a in range(PASSES):
                 nc.tensor.matmul_mx(
                     out=acc[:],
                     lhsT=un_sb[g][:, a, cols].bitcast(FP8X4),
-                    lhsT_scale=w_planes[:, a, ncols],
+                    lhsT_scale=w_planes[gs][:, a, ncols],
                     rhs=tab_codes[:, a, cols_of(half)].bitcast(FP4X4),
                     rhs_scale=tab_sc[half][:, a, :],
                     start=(a == 0),
@@ -175,7 +181,7 @@ def tile_list_tgn_rnn_kernel(
                 nc.tensor.matmul_mx(
                     out=acc[:],
                     lhsT=wn_sb[g][:, a, cols].bitcast(FP8X4),
-                    lhsT_scale=w_planes[4:P, a, ncols],
+                    lhsT_scale=w_planes[gs][4:P, a, ncols],
                     rhs=x_codes[a, half][:].bitcast(FP8X4),
                     rhs_scale=x_sc[a, half][:],
                     start=False,
@@ -212,19 +218,24 @@ def tile_list_tgn_rnn_kernel(
         tab_codes = keep.tile([P, PASSES, J], U16, name="tab_codes", align_bytes=64)
         nc.vector.tensor_copy(out=tab_codes[:], in_=pairs[:].bitcast(U16).rearrange("p (j d) -> p d j", d=PASSES))
         quantise_x(0)
-        gather_scales(1, keep.tile([P, PASSES, HALF], U8, name="tab_sc1", tag="raw1_0", align_bytes=64))
+        gather_scales(1, keep.tile([P, PASSES, HALF], U8, name="tab_sc1", tag="raw1_0", align_bytes=ALIGN))
         quantise_x(1)
         for r in range(EARLY):
-            if r < 2:
-                act = shared.tile([P, HALF], F32, name=f"act{r}_0", offset=(7, 16)[r] * KIB, align_bytes=64)
+            if r == 0:
+                act = shared.tile([P, 5 * HALF], F32, name=f"act{r}_0", offset=7 * KIB, align_bytes=ALIGN)
             else:
                 act = acts.tile([P, HALF], F32, name=f"act{r}_0")
             add_state(r, (0,), act)
-            for i in {0: (0, 1), 1: (2,)}.get(r, ()):
-                windows.append(shared.tile([P, T], F32, name=f"window{i + 1}", offset=8 * KIB * i, align_bytes=64))
-                nc.gpsimd.memset(windows[-1][:], 0.0)
-            place(r, (0,))
-        for r in range(EARLY):
+            if r == 0:
+                for w in range(1, EARLY):
+                    windows[w] = shared.tile([P, T], F32, name=f"window{w}", offset=8 * KIB * (w - 1), align_bytes=ALIGN)
+                for w, lo, hi in ((3, 0, T), (2, 0, 5 * T // 8), (1, 0, T), (2, 5 * T // 8, T)):
+                    nc.gpsimd.memset(windows[w][:, lo:hi], 0.0)
+            if r != 1:
+                place(max(r - 1, 0), (0,))
+        add_state(0, (1,), acts.tile([P, HALF], F32, name="act0_1"))
+        place(EARLY - 1, (0,))
+        for r in range(1, EARLY):
             add_state(r, (1,), acts.tile([P, HALF], F32, name=f"act{r}_1"))
         for r in range(EARLY):
             place(r, (1,))

@@ -27,6 +27,7 @@ EARLY = 4
 W_GROUPS = ((0, 1), (1, 3), (3, 4), (4, TILES))
 KIB = 1024
 ALIGN = 256
+LATE_BYTES = (64 + 15 + 2 + 20) * KIB
 
 
 def tile_list_tgn_rnn_kernel(
@@ -36,42 +37,63 @@ def tile_list_tgn_rnn_kernel(
     with ExitStack() as ctx:
         keep = ctx.enter_context(tc.tile_pool(name="keep", bufs=1))
         shared = ctx.enter_context(tc.tile_pool(name="shared", bufs=1))
+        late = ctx.enter_context(tc.tile_pool(name="late", bufs=1))
         ring = ctx.enter_context(tc.tile_pool(name="ring", bufs=4))
         acts = ctx.enter_context(tc.tile_pool(name="acts", bufs=1))
         psum = ctx.enter_context(tc.psum_pool(name="psum", bufs=4))
         psb = ctx.enter_context(tc.psum_pool(name="psb", bufs=1))
 
         offsets = keep.tile([P, J // 16], U16, name="offsets")
-        tab_planes = keep.tile([P, PASSES, T], U8, name="tab_planes", align_bytes=ALIGN)
-        w_planes = [keep.tile([P, PASSES, HALF], U8, name=f"w_planes{g}", align_bytes=ALIGN) for g in range(2)]
         windows = {0: keep.tile([P, T], F32, name="window0", align_bytes=ALIGN)}
         vec_rows = keep.tile([P, P], F32, name="vec_rows", align_bytes=ALIGN)
         ident = keep.tile([P, P], F32, name="ident")
         vec_cols = keep.tile([P, 2 * TILES], F32, name="vec_cols")
-        h = [keep.tile([P, T], F32, name=f"h{r}", align_bytes=ALIGN) for r in range(TILES)]
         totals = [keep.tile([P, J], F32, name=f"total{r}") for r in range(TILES)]
-        wn_sb = [keep.tile([P, PASSES, (hi - lo) * P], I32, name=f"wn{lo}", align_bytes=ALIGN) for lo, hi in W_GROUPS]
-        un_sb = [keep.tile([P, PASSES, (hi - lo) * P], I32, name=f"un{lo}", align_bytes=ALIGN) for lo, hi in W_GROUPS]
-
         weights = keep.tile([P, J], F32, name="weights")
         tab = shared.tile([P, T], I32, name="tab", offset=0, align_bytes=ALIGN)
-        raw = {
-            (0, 0): shared.tile([P, 4, HALF], F32, name="raw0_0", offset=8 * KIB, align_bytes=ALIGN),
-            (1, 0): keep.tile([P, 4, HALF], F32, name="raw1_0", tag="raw1_0", align_bytes=ALIGN),
-            (0, 1): keep.tile([P, 4, HALF], F32, name="raw0_1", align_bytes=ALIGN),
-            (1, 1): keep.tile([P, 4, HALF], F32, name="raw1_1", align_bytes=ALIGN),
-        }
+        tab_planes = late.tile([P, LATE_BYTES], U8, name="tab_planes", offset=0, align_bytes=ALIGN)
 
-        nc.vector.memset(tab_planes[:].bitcast(I32), 0)
-        nc.vector.memset(windows[0][:], 0.0)
+        taken = [0]
+
+        def late_tile(shape, dtype, name, size):
+            tile = late.tile(shape, dtype, name=name, offset=sum(taken), align_bytes=ALIGN)
+            taken.append(size)
+            return tile
+
+        def weight_tile(name, g):
+            lo, hi = W_GROUPS[g]
+            return late_tile([P, PASSES, (hi - lo) * P], I32, f"{name}{lo}", (hi - lo) * KIB)
+
+        h = [late_tile([P, T], F32, f"h{r}", 8 * KIB) for r in range(TILES)]
+        wn_sb = [weight_tile("wn", g) for g in range(len(W_GROUPS))]
+        un_sb = [keep.tile([P, PASSES, P], I32, name="un0", align_bytes=ALIGN)]
+        un_sb.extend(weight_tile("un", g) for g in range(1, len(W_GROUPS)))
+        un_planes = [
+            keep.tile([P, PASSES, HALF], U8, name="un_planes0", align_bytes=64),
+            late_tile([P, PASSES, HALF], U8, "un_planes1", KIB),
+        ]
+        wn_planes = [
+            keep.tile([P, PASSES, HALF], U8, name="wn_planes0", align_bytes=64),
+            late_tile([P, PASSES, HALF], U8, "wn_planes1", KIB),
+        ]
+        raw = {(0, 0): shared.tile([P, 4, HALF], F32, name="raw0_0", offset=8 * KIB, align_bytes=ALIGN)}
+        raw[1, 0, 0] = keep.tile([P, 4, PIECE], F32, name="raw1_0_0", align_bytes=ALIGN)
+        raw[1, 0, 1] = late_tile([P, 4, PIECE], F32, "raw1_0_1", 4 * KIB)
+        for a, half in ((0, 1), (1, 1)):
+            raw[a, half] = late_tile([P, 4, HALF], F32, f"raw{a}_{half}", 8 * KIB)
+        assert sum(taken) == LATE_BYTES
+
+        nc.gpsimd.memset(tab_planes[:, 0:T].bitcast(I32), 0)
         nc.gpsimd.memset(vec_rows[:], 0.0)
+        nc.vector.memset(windows[0][:], 0.0)
         make_identity(nc, ident[:])
 
-        def load_scale_row(planes, first_row, scales, r):
-            nc.sync.dma_start(
-                out=planes[first_row + r : P : 32, :, :].bitcast(I32),
-                in_=scales[:, r:16:4, :].bitcast(I32).rearrange("a q n -> q a n"),
-            )
+        def load_scale_rows(planes, scales, g, rows):
+            for r in rows:
+                nc.sync.dma_start(
+                    out=planes[g][r:P:32, :, :].bitcast(I32),
+                    in_=scales[:, r:16:4, g * HALF : (g + 1) * HALF].bitcast(I32).rearrange("a q n -> q a n"),
+                )
 
         def load_x(tile, a, lo, hi):
             rows = x[512 * a : 512 * (a + 1), lo:hi]
@@ -83,24 +105,33 @@ def tile_list_tgn_rnn_kernel(
                 view = words.rearrange("a p n i -> p a (n i)")[:, :, 4 * P * lo : 4 * P * hi].bitcast(I32)
                 nc.sync.dma_start(out=tiles[g][:], in_=view)
 
-        def load_w_scales(g, rows):
-            for r in rows:
-                load_scale_row(w_planes[g], 0, un_scales[:, :, g * HALF : (g + 1) * HALF], r)
-                load_scale_row(w_planes[g], 4, wn_scales[:, :, g * HALF : (g + 1) * HALF], r)
-
         def load_h(r):
             nc.sync.dma_start(out=h[r][:], in_=hT[P * r : P * (r + 1), :])
 
         nc.sync.dma_start(offsets[:], offs)
+        load_scale_rows(un_planes, un_scales, 0, (0, 1))
+        for r in range(4):
+            nc.sync.dma_start(
+                out=tab_planes[r:P:16, 0:T].bitcast(I32),
+                in_=tab_scales[:, r:16:4, :].bitcast(I32).rearrange("a q n -> q a n"),
+            )
         nc.sync.dma_start(out=tab[:], in_=tab_words[0].rearrange("p t b -> p (t b)").bitcast(I32))
+
         nc.sync.dma_start(out=vec_rows[0:TILES, :], in_=bn.rearrange("(r p) -> r p", p=P))
         nc.sync.dma_start(out=vec_rows[TILES : 2 * TILES, :], in_=wgo[0].rearrange("(r p) -> r p", p=P))
-        for r in range(4):
-            load_scale_row(tab_planes, 0, tab_scales, r)
-        for a in range(PASSES):
-            load_x(raw[a, 0], a, 0, HALF)
-            load_w_scales(0, (2 * a, 2 * a + 1))
-        load_w(0)
+        load_x(raw[0, 0], 0, 0, HALF)
+        load_scale_rows(un_planes, un_scales, 0, (2, 3))
+        load_w(0, (0,))
+        load_scale_rows(wn_planes, wn_scales, 0, (0,))
+        load_x(raw[1, 0, 0], 1, 0, PIECE)
+
+        tab_sc = [keep.tile([P, J], U8, name=f"tab_sc{a}", align_bytes=64) for a in range(PASSES)]
+        nc.vector.tensor_copy(out=tab_sc[0][:], in_=tab_planes[:, 0:T].indirect(offsets[:]))
+        nc.sync.dma_start(out=tab_sc[1][0 : P - 16, :].bitcast(I32), in_=tab_sc[0][16:P, :].bitcast(I32))
+
+        load_x(raw[1, 0, 1], 1, PIECE, HALF)
+        load_scale_rows(wn_planes, wn_scales, 0, (1, 2, 3))
+        load_w(0, (1,))
         load_h(0)
         load_w(1, (0,))
         load_h(1)
@@ -110,9 +141,9 @@ def tile_list_tgn_rnn_kernel(
         for a in range(PASSES):
             load_x(raw[a, 1], a, HALF, J)
         load_h(3)
-        load_w_scales(1, (0, 1))
+        load_scale_rows(un_planes, un_scales, 1, range(4))
         load_w(3, (0,))
-        load_w_scales(1, (2, 3))
+        load_scale_rows(wn_planes, wn_scales, 1, range(4))
         load_w(3, (1,))
         for r in range(EARLY, TILES):
             load_h(r)
@@ -133,57 +164,62 @@ def tile_list_tgn_rnn_kernel(
         def offsets_of(cols):
             return offsets[:, cols.start // 16 : cols.stop // 16]
 
-        tab_sc, x_codes, x_sc = {}, {}, {}
-
-        def gather_scales(half, sc):
+        x_codes, x_sc, tab_codes = {}, {}, {}
+        for half in range(2):
             for a in range(PASSES):
-                nc.vector.tensor_copy(out=sc[:, a, :], in_=tab_planes[:, a, :].indirect(offsets_of(cols_of(half))))
-            tab_sc[half] = sc
+                x_codes[a, half] = keep.tile([P, HALF], U32, name=f"x_codes{half}_{a}", align_bytes=64)
+                x_sc[a, half] = keep.tile([P, HALF], U8, name=f"x_sc{half}_{a}", align_bytes=64)
 
-        def quantise_x(half):
-            for a in range(PASSES):
-                codes = keep.tile([P, HALF], U32, name=f"x_codes{half}_{a}", align_bytes=64)
-                sc = keep.tile([P, HALF], U8, name=f"x_sc{half}_{a}", align_bytes=64)
-                for i in range(HALF // PIECE):
-                    cols = slice(i * PIECE, (i + 1) * PIECE)
-                    grouped = ring.tile([P, PIECE, 4], BF16, name="grouped", align_bytes=64)
-                    dst = grouped[:].rearrange("p (c e) i -> p c i e", e=4)
-                    src = raw[a, half][:, :, cols].rearrange("p i (c e) -> p c i e", e=4)
-                    if (half, a, i) == (0, 1, 0):
-                        nc.vector.tensor_copy(out=dst, in_=src)
-                    else:
-                        nc.scalar.copy(out=dst, in_=src)
-                    nc.vector.quantize_mx(
-                        out=codes[:, cols].bitcast(FP8X4),
-                        scales=sc[:, cols],
-                        in_=grouped[:].rearrange("p j i -> p (j i)"),
-                    )
-                x_codes[a, half], x_sc[a, half] = codes, sc
+        def round_x(copy, src, grouped):
+            copy(
+                out=grouped[:].rearrange("p (c e) i -> p c i e", e=4),
+                in_=src.rearrange("p i (c e) -> p c i e", e=4),
+            )
 
-        def products(r, half, into):
-            g = [i for i, (lo, hi) in enumerate(W_GROUPS) if lo <= r < hi][0]
+        def quantise(a, half, lo, hi, grouped):
+            nc.vector.quantize_mx(
+                out=x_codes[a, half][:, lo:hi].bitcast(FP8X4),
+                scales=x_sc[a, half][:, lo:hi],
+                in_=grouped[:].rearrange("p j i -> p (j i)"),
+            )
+
+        def ring_piece(copy, a, half, src, lo):
+            grouped = ring.tile([P, PIECE, 4], BF16, name="grouped", align_bytes=64)
+            round_x(copy, src, grouped)
+            quantise(a, half, lo, lo + PIECE, grouped)
+
+        def part_words(half, codes):
+            nc.vector.tensor_copy(
+                out=codes[:], in_=pairs[:, cols_of(half)].bitcast(U16).rearrange("p (j d) -> p d j", d=PASSES)
+            )
+            tab_codes[half] = codes
+
+        def products(r, half, lo, hi, into):
+            g = [i for i, (first, last) in enumerate(W_GROUPS) if first <= r < last][0]
             c0 = (r - W_GROUPS[g][0]) * P
             cols = slice(c0, c0 + P)
             gs, n0 = divmod(r * P, HALF)
             ncols = slice(n0, n0 + P)
-            acc = psum.tile([P, HALF], F32, name="acc")
+            acc = psum.tile([P, hi - lo], F32, name="acc")
+            step = HALF if hi - lo == HALF else P
             for a in range(PASSES):
-                nc.tensor.matmul_mx(
-                    out=acc[:],
-                    lhsT=un_sb[g][:, a, cols].bitcast(FP8X4),
-                    lhsT_scale=w_planes[gs][:, a, ncols],
-                    rhs=tab_codes[:, a, cols_of(half)].bitcast(FP4X4),
-                    rhs_scale=tab_sc[half][:, a, :],
-                    start=(a == 0),
-                    stop=False,
-                )
+                for c in range(lo, hi, step):
+                    nc.tensor.matmul_mx(
+                        out=acc[:, c - lo : c - lo + step],
+                        lhsT=un_sb[g][:, a, cols].bitcast(FP8X4),
+                        lhsT_scale=un_planes[gs][:, a, ncols],
+                        rhs=tab_codes[half][:, a, c : c + step].bitcast(FP4X4),
+                        rhs_scale=tab_sc[a][:, half * HALF + c : half * HALF + c + step],
+                        start=(a == 0 and c == lo),
+                        stop=False,
+                    )
             for a in range(PASSES):
                 nc.tensor.matmul_mx(
                     out=acc[:],
                     lhsT=wn_sb[g][:, a, cols].bitcast(FP8X4),
-                    lhsT_scale=w_planes[gs][4:P, a, ncols],
-                    rhs=x_codes[a, half][:].bitcast(FP8X4),
-                    rhs_scale=x_sc[a, half][:],
+                    lhsT_scale=wn_planes[gs][:, a, ncols],
+                    rhs=x_codes[a, half][:, lo:hi].bitcast(FP8X4),
+                    rhs_scale=x_sc[a, half][:, lo:hi],
                     start=False,
                     stop=(a == PASSES - 1),
                 )
@@ -192,7 +228,11 @@ def tile_list_tgn_rnn_kernel(
         def add_state(r, halves, act):
             cols = slice(halves[0] * HALF, (halves[-1] + 1) * HALF)
             for i, half in enumerate(halves):
-                products(r, half, act[:, cols_of(i)])
+                if (r, half) == (0, 0):
+                    for lo in range(0, HALF, PIECE):
+                        products(r, half, lo, lo + PIECE, act[:, lo : lo + PIECE])
+                else:
+                    products(r, half, 0, HALF, act[:, cols_of(i)])
             nc.vector.tensor_tensor(
                 out=totals[r][:, cols],
                 in0=h[r][:].indirect(offsets_of(cols)),
@@ -214,12 +254,19 @@ def tile_list_tgn_rnn_kernel(
 
         pairs = keep.tile([P, J], U32, name="pairs")
         nc.vector.tensor_copy(out=pairs[:], in_=tab[:].bitcast(U32).indirect(offsets[:]))
-        gather_scales(0, keep.tile([P, PASSES, HALF], U8, name="tab_sc0", align_bytes=64))
-        tab_codes = keep.tile([P, PASSES, J], U16, name="tab_codes", align_bytes=64)
-        nc.vector.tensor_copy(out=tab_codes[:], in_=pairs[:].bitcast(U16).rearrange("p (j d) -> p d j", d=PASSES))
-        quantise_x(0)
-        gather_scales(1, keep.tile([P, PASSES, HALF], U8, name="tab_sc1", tag="raw1_0", align_bytes=ALIGN))
-        quantise_x(1)
+        part_words(0, keep.tile([P, PASSES, HALF], U16, name="tab_codes0", align_bytes=64))
+        ring_piece(nc.vector.tensor_copy, 0, 0, raw[0, 0][:, :, PIECE:HALF], PIECE)
+        ring_piece(nc.scalar.copy, 0, 0, raw[0, 0][:, :, 0:PIECE], 0)
+        ring_piece(nc.scalar.copy, 1, 0, raw[1, 0, 0][:], 0)
+        last = [keep.tile([P, P, 4], BF16, name=f"last{i}", align_bytes=64) for i in range(2)]
+        round_x(nc.scalar.copy, raw[1, 0, 1][:, :, 0:P], last[0])
+        round_x(nc.vector.tensor_copy, raw[1, 0, 1][:, :, P:PIECE], last[1])
+        for i in range(2):
+            quantise(1, 0, PIECE + i * P, PIECE + (i + 1) * P, last[i])
+        part_words(1, keep.tile([P, PASSES, HALF], U16, name="tab_codes1", tag="last1", align_bytes=64))
+        for a in range(PASSES):
+            for lo in range(0, HALF, PIECE):
+                ring_piece(nc.scalar.copy, a, 1, raw[a, 1][:, :, lo : lo + PIECE], lo)
         for r in range(EARLY):
             if r == 0:
                 act = shared.tile([P, 5 * HALF], F32, name=f"act{r}_0", offset=7 * KIB, align_bytes=ALIGN)

@@ -84,7 +84,6 @@ def tile_list_tgn_rnn_kernel(
         assert sum(taken) == LATE_BYTES
 
         nc.gpsimd.memset(tab_planes[:, 0:T].bitcast(I32), 0)
-        nc.gpsimd.memset(vec_rows[:], 0.0)
         nc.vector.memset(windows[0][:], 0.0)
         make_identity(nc, ident[:])
 
@@ -109,7 +108,8 @@ def tile_list_tgn_rnn_kernel(
             nc.sync.dma_start(out=h[r][:], in_=hT[P * r : P * (r + 1), :])
 
         nc.sync.dma_start(offsets[:], offs)
-        load_scale_rows(un_planes, un_scales, 0, (0, 1))
+        nc.sync.dma_start(out=vec_rows[0:64, :], in_=bn.partition_broadcast(8).rearrange("u (r p) -> u r p", p=P))
+        nc.sync.dma_start(out=vec_rows[64:P, :], in_=wgo[0:8, :].rearrange("u (r p) -> (u r) p", p=P))
         for r in range(4):
             nc.sync.dma_start(
                 out=tab_planes[r:P:16, 0:T].bitcast(I32),
@@ -117,8 +117,7 @@ def tile_list_tgn_rnn_kernel(
             )
         nc.sync.dma_start(out=tab[:], in_=tab_words[0].rearrange("p t b -> p (t b)").bitcast(I32))
 
-        nc.sync.dma_start(out=vec_rows[0:TILES, :], in_=bn.rearrange("(r p) -> r p", p=P))
-        nc.sync.dma_start(out=vec_rows[TILES : 2 * TILES, :], in_=wgo[0].rearrange("(r p) -> r p", p=P))
+        load_scale_rows(un_planes, un_scales, 0, (0, 1))
         load_x(raw[0, 0], 0, 0, HALF)
         load_scale_rows(un_planes, un_scales, 0, (2, 3))
         load_w(0, (0,))
@@ -150,7 +149,7 @@ def tile_list_tgn_rnn_kernel(
 
         turned = psb.tile([P, P], F32, name="turned")
         nc.tensor.transpose(turned[:], vec_rows[:], ident[:])
-        nc.scalar.copy(out=vec_cols[:], in_=turned[:, 0 : 2 * TILES])
+        nc.scalar.copy(out=vec_cols[:], in_=turned[:, 64 - TILES : 64 + TILES])
         spread = [psb.tile([P, HALF], F32, name=f"spread{half}") for half in range(2)]
         for m in range(TILES):
             column = vec_cols[:, TILES + m : TILES + m + 1].to_broadcast([P, P])

@@ -18,16 +18,20 @@ ADD = mybir.AluOpType.add
 MULT = mybir.AluOpType.mult
 TANH = mybir.ActivationFunctionType.Tanh
 
+COPY = mybir.ActivationFunctionType.Copy
+
 P = 128
 PASSES = 2
 HALF = 512
 PIECE = 256
 TILES = N // P
-EARLY = 4
-W_GROUPS = ((0, 1), (1, 3), (3, 4), (4, TILES))
+W_GROUPS = ((0, 1), (1, 2), (2, 4), (4, TILES))
+WINDOWS = 4
+SUMS = 5
 KIB = 1024
 ALIGN = 256
-LATE_BYTES = (64 + 15 + 2 + 20) * KIB
+LATE_BYTES = (64 + 15 + 3 + 24) * KIB
+FIRST, SECOND, FRONT, BACK, ALL = slice(0, PIECE), slice(PIECE, HALF), slice(0, HALF), slice(HALF, J), slice(0, J)
 
 
 def tile_list_tgn_rnn_kernel(
@@ -40,8 +44,7 @@ def tile_list_tgn_rnn_kernel(
         late = ctx.enter_context(tc.tile_pool(name="late", bufs=1))
         ring = ctx.enter_context(tc.tile_pool(name="ring", bufs=4))
         acts = ctx.enter_context(tc.tile_pool(name="acts", bufs=1))
-        psum = ctx.enter_context(tc.psum_pool(name="psum", bufs=4))
-        psb = ctx.enter_context(tc.psum_pool(name="psb", bufs=1))
+        psum = ctx.enter_context(tc.psum_pool(name="psum", bufs=1))
 
         offsets = keep.tile([P, J // 16], U16, name="offsets")
         windows = {0: keep.tile([P, T], F32, name="window0", align_bytes=ALIGN)}
@@ -50,7 +53,7 @@ def tile_list_tgn_rnn_kernel(
         vec_cols = keep.tile([P, 2 * TILES], F32, name="vec_cols")
         totals = [keep.tile([P, J], F32, name=f"total{r}") for r in range(TILES)]
         weights = keep.tile([P, J], F32, name="weights")
-        tab = shared.tile([P, T], I32, name="tab", offset=0, align_bytes=ALIGN)
+        tab = shared.tile([P, T], I32, name="tab", offset=8 * KIB, align_bytes=ALIGN)
         tab_planes = late.tile([P, LATE_BYTES], U8, name="tab_planes", offset=0, align_bytes=ALIGN)
 
         taken = [0]
@@ -72,37 +75,33 @@ def tile_list_tgn_rnn_kernel(
             keep.tile([P, PASSES, HALF], U8, name="un_planes0", align_bytes=64),
             late_tile([P, PASSES, HALF], U8, "un_planes1", KIB),
         ]
-        wn_planes = [
-            keep.tile([P, PASSES, HALF], U8, name="wn_planes0", align_bytes=64),
-            late_tile([P, PASSES, HALF], U8, "wn_planes1", KIB),
-        ]
-        raw = {(0, 0): shared.tile([P, 4, HALF], F32, name="raw0_0", offset=8 * KIB, align_bytes=ALIGN)}
-        raw[1, 0, 0] = keep.tile([P, 4, PIECE], F32, name="raw1_0_0", align_bytes=ALIGN)
-        raw[1, 0, 1] = late_tile([P, 4, PIECE], F32, "raw1_0_1", 4 * KIB)
-        for a, half in ((0, 1), (1, 1)):
-            raw[a, half] = late_tile([P, 4, HALF], F32, f"raw{a}_{half}", 8 * KIB)
+        wn_planes = [late_tile([P, PASSES, HALF], U8, f"wn_planes{g}", KIB) for g in range(2)]
+        raw = {}
+        for a in range(PASSES):
+            raw[a, 0] = shared.tile([P, 4, PIECE], F32, name=f"raw{a}_0", offset=16 * a * KIB, align_bytes=ALIGN)
+            raw[a, PIECE] = late_tile([P, 4, PIECE], F32, f"raw{a}_1", 4 * KIB)
+            raw[a, HALF] = late_tile([P, 4, HALF], F32, f"raw{a}_2", 8 * KIB)
         assert sum(taken) == LATE_BYTES
 
         nc.gpsimd.memset(tab_planes[:, 0:T].bitcast(I32), 0)
         nc.vector.memset(windows[0][:], 0.0)
         make_identity(nc, ident[:])
 
-        def load_scale_rows(planes, scales, g, rows):
-            for r in rows:
+        def load_scale_rows(planes, scales, g):
+            for r in range(4):
                 nc.sync.dma_start(
                     out=planes[g][r:P:32, :, :].bitcast(I32),
                     in_=scales[:, r:16:4, g * HALF : (g + 1) * HALF].bitcast(I32).rearrange("a q n -> q a n"),
                 )
 
-        def load_x(tile, a, lo, hi):
-            rows = x[512 * a : 512 * (a + 1), lo:hi]
-            nc.sync.dma_start(out=tile[:], in_=rows.rearrange("(p i) j -> p i j", i=4))
+        def load_x(a, cols):
+            rows = x[512 * a : 512 * (a + 1), cols]
+            nc.sync.dma_start(out=raw[a, cols.start][:], in_=rows.rearrange("(p i) j -> p i j", i=4))
 
-        def load_w(g, which=(0, 1)):
+        def load_w(tiles, words, g):
             lo, hi = W_GROUPS[g]
-            for tiles, words in [((un_sb, un_words), (wn_sb, wn_words))[i] for i in which]:
-                view = words.rearrange("a p n i -> p a (n i)")[:, :, 4 * P * lo : 4 * P * hi].bitcast(I32)
-                nc.sync.dma_start(out=tiles[g][:], in_=view)
+            view = words.rearrange("a p n i -> p a (n i)")[:, :, 4 * P * lo : 4 * P * hi].bitcast(I32)
+            nc.sync.dma_start(out=tiles[g][:], in_=view)
 
         def load_h(r):
             nc.sync.dma_start(out=h[r][:], in_=hT[P * r : P * (r + 1), :])
@@ -116,49 +115,45 @@ def tile_list_tgn_rnn_kernel(
                 in_=tab_scales[:, r:16:4, :].bitcast(I32).rearrange("a q n -> q a n"),
             )
         nc.sync.dma_start(out=tab[:], in_=tab_words[0].rearrange("p t b -> p (t b)").bitcast(I32))
-
-        load_scale_rows(un_planes, un_scales, 0, (0, 1))
-        load_x(raw[0, 0], 0, 0, HALF)
-        load_scale_rows(un_planes, un_scales, 0, (2, 3))
-        load_w(0, (0,))
-        load_scale_rows(wn_planes, wn_scales, 0, (0,))
-        load_x(raw[1, 0, 0], 1, 0, PIECE)
+        load_x(0, FIRST)
+        load_scale_rows(un_planes, un_scales, 0)
+        load_w(un_sb, un_words, 0)
+        load_x(1, FIRST)
 
         tab_sc = [keep.tile([P, J], U8, name=f"tab_sc{a}", align_bytes=64) for a in range(PASSES)]
         nc.vector.tensor_copy(out=tab_sc[0][:], in_=tab_planes[:, 0:T].indirect(offsets[:]))
         nc.sync.dma_start(out=tab_sc[1][0 : P - 16, :].bitcast(I32), in_=tab_sc[0][16:P, :].bitcast(I32))
 
-        load_x(raw[1, 0, 1], 1, PIECE, HALF)
-        load_scale_rows(wn_planes, wn_scales, 0, (1, 2, 3))
-        load_w(0, (1,))
+        load_w(wn_sb, wn_words, 0)
+        load_scale_rows(wn_planes, wn_scales, 0)
         load_h(0)
-        load_w(1, (0,))
+        load_w(un_sb, un_words, 1)
+        load_w(wn_sb, wn_words, 1)
         load_h(1)
-        load_w(1, (1,))
-        load_h(2)
-        load_w(2)
         for a in range(PASSES):
-            load_x(raw[a, 1], a, HALF, J)
+            load_x(a, SECOND)
+        load_h(2)
+        load_w(un_sb, un_words, 2)
+        load_w(wn_sb, wn_words, 2)
+        for a in range(PASSES):
+            load_x(a, BACK)
         load_h(3)
-        load_scale_rows(un_planes, un_scales, 1, range(4))
-        load_w(3, (0,))
-        load_scale_rows(wn_planes, wn_scales, 1, range(4))
-        load_w(3, (1,))
-        for r in range(EARLY, TILES):
+        load_scale_rows(un_planes, un_scales, 1)
+        load_w(un_sb, un_words, 3)
+        load_scale_rows(wn_planes, wn_scales, 1)
+        load_w(wn_sb, wn_words, 3)
+        for r in range(WINDOWS, TILES):
             load_h(r)
 
-        turned = psb.tile([P, P], F32, name="turned")
+        turned = psum.tile([P, P], F32, name="turned")
         nc.tensor.transpose(turned[:], vec_rows[:], ident[:])
         nc.scalar.copy(out=vec_cols[:], in_=turned[:, 64 - TILES : 64 + TILES])
-        spread = [psb.tile([P, HALF], F32, name=f"spread{half}") for half in range(2)]
+        spread = [psum.tile([P, HALF], F32, name=f"spread{half}") for half in range(2)]
         for m in range(TILES):
             column = vec_cols[:, TILES + m : TILES + m + 1].to_broadcast([P, P])
             nc.tensor.transpose(spread[m // 4][:, (m % 4) * P : (m % 4 + 1) * P], column, ident[:])
         for half in range(2):
             nc.scalar.copy(out=weights[:, half * HALF : (half + 1) * HALF], in_=spread[half][:])
-
-        def cols_of(half):
-            return slice(half * HALF, (half + 1) * HALF)
 
         def offsets_of(cols):
             return offsets[:, cols.start // 16 : cols.stop // 16]
@@ -169,43 +164,42 @@ def tile_list_tgn_rnn_kernel(
                 x_codes[a, half] = keep.tile([P, HALF], U32, name=f"x_codes{half}_{a}", align_bytes=64)
                 x_sc[a, half] = keep.tile([P, HALF], U8, name=f"x_sc{half}_{a}", align_bytes=64)
 
-        def round_x(copy, src, grouped):
-            copy(
+        def quantise(a, src, first, grouped):
+            half, lo = divmod(first, HALF)
+            nc.scalar.copy(
                 out=grouped[:].rearrange("p (c e) i -> p c i e", e=4),
                 in_=src.rearrange("p i (c e) -> p c i e", e=4),
             )
-
-        def quantise(a, half, lo, hi, grouped):
             nc.vector.quantize_mx(
-                out=x_codes[a, half][:, lo:hi].bitcast(FP8X4),
-                scales=x_sc[a, half][:, lo:hi],
+                out=x_codes[a, half][:, lo : lo + PIECE].bitcast(FP8X4),
+                scales=x_sc[a, half][:, lo : lo + PIECE],
                 in_=grouped[:].rearrange("p j i -> p (j i)"),
             )
 
-        def ring_piece(copy, a, half, src, lo):
-            grouped = ring.tile([P, PIECE, 4], BF16, name="grouped", align_bytes=64)
-            round_x(copy, src, grouped)
-            quantise(a, half, lo, lo + PIECE, grouped)
+        def quantise_stage(cols):
+            for a in range(PASSES):
+                for lo in range(0, cols.stop - cols.start, PIECE):
+                    grouped = ring.tile([P, PIECE, 4], BF16, name="grouped", align_bytes=64)
+                    quantise(a, raw[a, cols.start][:, :, lo : lo + PIECE], cols.start + lo, grouped)
 
-        def part_words(half, codes):
-            nc.vector.tensor_copy(
-                out=codes[:], in_=pairs[:, cols_of(half)].bitcast(U16).rearrange("p (j d) -> p d j", d=PASSES)
-            )
-            tab_codes[half] = codes
+        sums = []
 
-        def products(r, half, lo, hi, into):
+        def products(r, cols, into):
+            half, lo = divmod(cols.start, HALF)
+            hi = lo + cols.stop - cols.start
             g = [i for i, (first, last) in enumerate(W_GROUPS) if first <= r < last][0]
             c0 = (r - W_GROUPS[g][0]) * P
-            cols = slice(c0, c0 + P)
+            wcols = slice(c0, c0 + P)
             gs, n0 = divmod(r * P, HALF)
             ncols = slice(n0, n0 + P)
-            acc = psum.tile([P, hi - lo], F32, name="acc")
+            acc = psum.tile([P, hi - lo], F32, name=f"acc{len(sums) % SUMS}")
+            sums.append(acc)
             step = HALF if hi - lo == HALF else P
             for a in range(PASSES):
                 for c in range(lo, hi, step):
                     nc.tensor.matmul_mx(
                         out=acc[:, c - lo : c - lo + step],
-                        lhsT=un_sb[g][:, a, cols].bitcast(FP8X4),
+                        lhsT=un_sb[g][:, a, wcols].bitcast(FP8X4),
                         lhsT_scale=un_planes[gs][:, a, ncols],
                         rhs=tab_codes[half][:, a, c : c + step].bitcast(FP4X4),
                         rhs_scale=tab_sc[a][:, half * HALF + c : half * HALF + c + step],
@@ -215,7 +209,7 @@ def tile_list_tgn_rnn_kernel(
             for a in range(PASSES):
                 nc.tensor.matmul_mx(
                     out=acc[:],
-                    lhsT=wn_sb[g][:, a, cols].bitcast(FP8X4),
+                    lhsT=wn_sb[g][:, a, wcols].bitcast(FP8X4),
                     lhsT_scale=wn_planes[gs][:, a, ncols],
                     rhs=x_codes[a, half][:, lo:hi].bitcast(FP8X4),
                     rhs_scale=x_sc[a, half][:, lo:hi],
@@ -224,70 +218,84 @@ def tile_list_tgn_rnn_kernel(
                 )
             nc.scalar.activation(out=into, in_=acc[:], func=TANH, bias=vec_cols[:, r : r + 1])
 
-        def add_state(r, halves, act):
-            cols = slice(halves[0] * HALF, (halves[-1] + 1) * HALF)
-            for i, half in enumerate(halves):
-                if (r, half) == (0, 0):
-                    for lo in range(0, HALF, PIECE):
-                        products(r, half, lo, lo + PIECE, act[:, lo : lo + PIECE])
-                else:
-                    products(r, half, 0, HALF, act[:, cols_of(i)])
+        def add_state(r, cols, act):
+            for lo in range(cols.start, cols.stop, HALF):
+                part = slice(lo, min(lo + HALF, cols.stop))
+                products(r, part, act[:, part.start - cols.start : part.stop - cols.start])
+            nc.vector.tensor_tensor(out=totals[r][:, cols], in0=h[r][:].indirect(offsets_of(cols)), in1=act[:], op=ADD)
+
+        def weigh_state(r, cols):
             nc.vector.tensor_tensor(
-                out=totals[r][:, cols],
-                in0=h[r][:].indirect(offsets_of(cols)),
-                in1=act[:, 0 : len(halves) * HALF],
-                op=ADD,
+                out=totals[r][:, cols], in0=h[r][:].indirect(offsets_of(cols)), in1=weights[:, cols], op=MULT
             )
 
-        def place(r, halves):
-            cols = slice(halves[0] * HALF, (halves[-1] + 1) * HALF)
+        def weigh_tanh(r, cols):
+            act = acts.tile([P, HALF], F32, name=f"act{r}_back")
+            products(r, cols, act[:])
+            by_event = psum.tile([P, HALF], F32, name="by_event", tag="spread0")
+            scaled = acts.tile([P, HALF], F32, name="scaled", bufs=2)
+            by_row = psum.tile([P, HALF], F32, name="by_row", tag="spread1")
+            blocks = [slice(b * P, (b + 1) * P) for b in range(HALF // P)]
+            for block in blocks:
+                nc.tensor.transpose(by_event[:, block], act[:, block], ident[:])
+            for block in blocks:
+                m = TILES + (cols.start + block.start) // P
+                nc.scalar.activation(out=scaled[:, block], in_=by_event[:, block], func=COPY, scale=vec_cols[:, m : m + 1])
+            for block in blocks:
+                nc.tensor.transpose(by_row[:, block], scaled[:, block], ident[:])
+            nc.scalar.copy(out=act[:], in_=by_row[:])
+            return act
+
+        def window_of(r):
+            return windows[r if r < WINDOWS else (r - 1) % WINDOWS]
+
+        def place(r, cols, other, op):
             nc.vector.tensor_tensor(
-                out=windows[r % EARLY][:].indirect(offsets_of(cols)),
-                in0=totals[r][:, cols],
-                in1=weights[:, cols],
-                op=MULT,
+                out=window_of(r)[:].indirect(offsets_of(cols)), in0=totals[r][:, cols], in1=other, op=op
             )
 
         def store(r):
-            nc.sync.dma_start(out=out[P * r : P * (r + 1), :], in_=windows[r % EARLY][:])
+            nc.sync.dma_start(out=out[P * r : P * (r + 1), :], in_=window_of(r)[:])
+
+        def clear_window(w):
+            windows[w] = shared.tile([P, T], F32, name=f"window{w}", offset=8 * KIB * (w - 1), align_bytes=ALIGN)
+            nc.gpsimd.memset(windows[w][:], 0.0)
 
         pairs = keep.tile([P, J], U32, name="pairs")
         nc.vector.tensor_copy(out=pairs[:], in_=tab[:].bitcast(U32).indirect(offsets[:]))
-        part_words(0, keep.tile([P, PASSES, HALF], U16, name="tab_codes0", align_bytes=64))
-        ring_piece(nc.vector.tensor_copy, 0, 0, raw[0, 0][:, :, PIECE:HALF], PIECE)
-        ring_piece(nc.scalar.copy, 0, 0, raw[0, 0][:, :, 0:PIECE], 0)
-        ring_piece(nc.scalar.copy, 1, 0, raw[1, 0, 0][:], 0)
-        last = [keep.tile([P, P, 4], BF16, name=f"last{i}", align_bytes=64) for i in range(2)]
-        round_x(nc.scalar.copy, raw[1, 0, 1][:, :, 0:P], last[0])
-        round_x(nc.vector.tensor_copy, raw[1, 0, 1][:, :, P:PIECE], last[1])
-        for i in range(2):
-            quantise(1, 0, PIECE + i * P, PIECE + (i + 1) * P, last[i])
-        part_words(1, keep.tile([P, PASSES, HALF], U16, name="tab_codes1", tag="last1", align_bytes=64))
+        for half, cols in enumerate((FRONT, BACK)):
+            tab_codes[half] = keep.tile([P, PASSES, HALF], U16, name=f"tab_codes{half}", align_bytes=64)
+            nc.vector.tensor_copy(
+                out=tab_codes[half][:], in_=pairs[:, cols].bitcast(U16).rearrange("p (j d) -> p d j", d=PASSES)
+            )
         for a in range(PASSES):
-            for lo in range(0, HALF, PIECE):
-                ring_piece(nc.scalar.copy, a, 1, raw[a, 1][:, :, lo : lo + PIECE], lo)
-        for r in range(EARLY):
-            if r == 0:
-                act = shared.tile([P, 5 * HALF], F32, name=f"act{r}_0", offset=7 * KIB, align_bytes=ALIGN)
-            else:
-                act = acts.tile([P, HALF], F32, name=f"act{r}_0")
-            add_state(r, (0,), act)
-            if r == 0:
-                for w in range(1, EARLY):
-                    windows[w] = shared.tile([P, T], F32, name=f"window{w}", offset=8 * KIB * (w - 1), align_bytes=ALIGN)
-                for w, lo, hi in ((3, 0, T), (2, 0, 5 * T // 8), (1, 0, T), (2, 5 * T // 8, T)):
-                    nc.gpsimd.memset(windows[w][:, lo:hi], 0.0)
-            if r != 1:
-                place(max(r - 1, 0), (0,))
-        add_state(0, (1,), acts.tile([P, HALF], F32, name="act0_1"))
-        place(EARLY - 1, (0,))
-        for r in range(1, EARLY):
-            add_state(r, (1,), acts.tile([P, HALF], F32, name=f"act{r}_1"))
-        for r in range(EARLY):
-            place(r, (1,))
+            grouped = shared.tile([P, PIECE, 4], BF16, name=f"grouped{a}", offset=(4 + 2 * a) * KIB, align_bytes=ALIGN)
+            quantise(a, raw[a, 0][:], 0, grouped)
+        clear_window(1)
+        for r in range(2):
+            act = shared.tile([P, PIECE], F32, name=f"act{r}_first", offset=(8 + 12 * r) * KIB, align_bytes=ALIGN)
+            add_state(r, FIRST, act)
+            clear_window(r + 2)
+            weigh_state(r, BACK)
+            place(r, FIRST, weights[:, FIRST], MULT)
+        quantise_stage(SECOND)
+        weigh_state(2, BACK)
+        for r in range(2):
+            add_state(r, SECOND, acts.tile([P, PIECE], F32, name=f"act{r}_second"))
+        for r in range(2):
+            place(r, SECOND, weights[:, SECOND], MULT)
+        add_state(2, FRONT, acts.tile([P, HALF], F32, name="act2_front"))
+        place(2, FRONT, weights[:, FRONT], MULT)
+        quantise_stage(BACK)
+        for cols in (FRONT, BACK):
+            add_state(3, cols, acts.tile([P, HALF], F32, name=f"act3_{cols.start}"))
+            place(3, cols, weights[:, cols], MULT)
+        store(3)
+        for r in range(3):
+            place(r, BACK, weigh_tanh(r, BACK)[:], ADD)
             store(r)
-        for r in range(EARLY, TILES):
-            add_state(r, (0, 1), acts.tile([P, J], F32, name="act", bufs=3))
-        for r in range(EARLY, TILES):
-            place(r, (0, 1))
+        for r in range(WINDOWS, TILES):
+            add_state(r, ALL, acts.tile([P, J], F32, name="act", bufs=3))
+        for r in range(WINDOWS, TILES):
+            place(r, ALL, weights[:], MULT)
             store(r)

@@ -25,9 +25,8 @@ PASSES = 2
 HALF = 512
 PIECE = 256
 TILES = N // P
-W_GROUPS = ((0, 1), (1, 2), (2, 4), (4, TILES))
+W_GROUPS = ((0, 1), (1, 2), (2, 3), (3, 4), (4, TILES))
 WINDOWS = 4
-SUMS = 5
 KIB = 1024
 ALIGN = 256
 LATE_BYTES = (64 + 15 + 3 + 24) * KIB
@@ -51,8 +50,7 @@ def tile_list_tgn_rnn_kernel(
         vec_rows = keep.tile([P, P], F32, name="vec_rows", align_bytes=ALIGN)
         ident = keep.tile([P, P], F32, name="ident")
         vec_cols = keep.tile([P, 2 * TILES], F32, name="vec_cols")
-        totals = [keep.tile([P, J], F32, name=f"total{r}") for r in range(TILES)]
-        weights = keep.tile([P, J], F32, name="weights")
+        totals = [keep.tile([P, J], F32, name=f"total{r}", align_bytes=64) for r in range(TILES)]
         tab = shared.tile([P, T], I32, name="tab", offset=8 * KIB, align_bytes=ALIGN)
         tab_planes = late.tile([P, LATE_BYTES], U8, name="tab_planes", offset=0, align_bytes=ALIGN)
 
@@ -78,17 +76,18 @@ def tile_list_tgn_rnn_kernel(
         wn_planes = [late_tile([P, PASSES, HALF], U8, f"wn_planes{g}", KIB) for g in range(2)]
         raw = {}
         for a in range(PASSES):
-            raw[a, 0] = shared.tile([P, 4, PIECE], F32, name=f"raw{a}_0", offset=16 * a * KIB, align_bytes=ALIGN)
+            raw[a, 0] = shared.tile([P, 4, PIECE], F32, name=f"raw{a}_0", offset=24 * a * KIB, align_bytes=ALIGN)
             raw[a, PIECE] = late_tile([P, 4, PIECE], F32, f"raw{a}_1", 4 * KIB)
             raw[a, HALF] = late_tile([P, 4, HALF], F32, f"raw{a}_2", 8 * KIB)
         assert sum(taken) == LATE_BYTES
 
         nc.gpsimd.memset(tab_planes[:, 0:T].bitcast(I32), 0)
+        nc.gpsimd.memset(vec_rows[:], 0.0)
         nc.vector.memset(windows[0][:], 0.0)
         make_identity(nc, ident[:])
 
-        def load_scale_rows(planes, scales, g):
-            for r in range(4):
+        def load_scale_rows(planes, scales, g, rows=range(4)):
+            for r in rows:
                 nc.sync.dma_start(
                     out=planes[g][r:P:32, :, :].bitcast(I32),
                     in_=scales[:, r:16:4, g * HALF : (g + 1) * HALF].bitcast(I32).rearrange("a q n -> q a n"),
@@ -107,8 +106,7 @@ def tile_list_tgn_rnn_kernel(
             nc.sync.dma_start(out=h[r][:], in_=hT[P * r : P * (r + 1), :])
 
         nc.sync.dma_start(offsets[:], offs)
-        nc.sync.dma_start(out=vec_rows[0:64, :], in_=bn.partition_broadcast(8).rearrange("u (r p) -> u r p", p=P))
-        nc.sync.dma_start(out=vec_rows[64:P, :], in_=wgo[0:8, :].rearrange("u (r p) -> (u r) p", p=P))
+        load_scale_rows(un_planes, un_scales, 0, (0, 1))
         for r in range(4):
             nc.sync.dma_start(
                 out=tab_planes[r:P:16, 0:T].bitcast(I32),
@@ -116,7 +114,9 @@ def tile_list_tgn_rnn_kernel(
             )
         nc.sync.dma_start(out=tab[:], in_=tab_words[0].rearrange("p t b -> p (t b)").bitcast(I32))
         load_x(0, FIRST)
-        load_scale_rows(un_planes, un_scales, 0)
+        load_scale_rows(un_planes, un_scales, 0, (2, 3))
+        nc.sync.dma_start(out=vec_rows[0:TILES, :], in_=bn.rearrange("(r p) -> r p", p=P))
+        nc.sync.dma_start(out=vec_rows[TILES : 2 * TILES, :], in_=wgo[0, :].rearrange("(r p) -> r p", p=P))
         load_w(un_sb, un_words, 0)
         load_x(1, FIRST)
 
@@ -133,27 +133,22 @@ def tile_list_tgn_rnn_kernel(
         for a in range(PASSES):
             load_x(a, SECOND)
         load_h(2)
-        load_w(un_sb, un_words, 2)
-        load_w(wn_sb, wn_words, 2)
+        for g in (2, 3):
+            load_w(un_sb, un_words, g)
+            load_w(wn_sb, wn_words, g)
         for a in range(PASSES):
             load_x(a, BACK)
         load_h(3)
         load_scale_rows(un_planes, un_scales, 1)
-        load_w(un_sb, un_words, 3)
+        load_w(un_sb, un_words, 4)
         load_scale_rows(wn_planes, wn_scales, 1)
-        load_w(wn_sb, wn_words, 3)
+        load_w(wn_sb, wn_words, 4)
         for r in range(WINDOWS, TILES):
             load_h(r)
 
         turned = psum.tile([P, P], F32, name="turned")
         nc.tensor.transpose(turned[:], vec_rows[:], ident[:])
-        nc.scalar.copy(out=vec_cols[:], in_=turned[:, 64 - TILES : 64 + TILES])
-        spread = [psum.tile([P, HALF], F32, name=f"spread{half}") for half in range(2)]
-        for m in range(TILES):
-            column = vec_cols[:, TILES + m : TILES + m + 1].to_broadcast([P, P])
-            nc.tensor.transpose(spread[m // 4][:, (m % 4) * P : (m % 4 + 1) * P], column, ident[:])
-        for half in range(2):
-            nc.scalar.copy(out=weights[:, half * HALF : (half + 1) * HALF], in_=spread[half][:])
+        nc.scalar.copy(out=vec_cols[:], in_=turned[:, 0 : 2 * TILES])
 
         def offsets_of(cols):
             return offsets[:, cols.start // 16 : cols.stop // 16]
@@ -167,24 +162,25 @@ def tile_list_tgn_rnn_kernel(
         def quantise(a, src, first, grouped):
             half, lo = divmod(first, HALF)
             nc.scalar.copy(
-                out=grouped[:].rearrange("p (c e) i -> p c i e", e=4),
+                out=grouped.rearrange("p (c e i) -> p c i e", e=4, i=4),
                 in_=src.rearrange("p i (c e) -> p c i e", e=4),
             )
             nc.vector.quantize_mx(
                 out=x_codes[a, half][:, lo : lo + PIECE].bitcast(FP8X4),
                 scales=x_sc[a, half][:, lo : lo + PIECE],
-                in_=grouped[:].rearrange("p j i -> p (j i)"),
+                in_=grouped,
             )
 
         def quantise_stage(cols):
             for a in range(PASSES):
                 for lo in range(0, cols.stop - cols.start, PIECE):
-                    grouped = ring.tile([P, PIECE, 4], BF16, name="grouped", align_bytes=64)
+                    if (a, cols) == (PASSES - 1, BACK):
+                        grouped = totals[3][:, 2 * lo : 2 * (lo + PIECE)].bitcast(BF16)
+                    else:
+                        grouped = ring.tile([P, 4 * PIECE], BF16, name="grouped", align_bytes=64)[:]
                     quantise(a, raw[a, cols.start][:, :, lo : lo + PIECE], cols.start + lo, grouped)
 
-        sums = []
-
-        def products(r, cols, into):
+        def products(r, cols, into, bank):
             half, lo = divmod(cols.start, HALF)
             hi = lo + cols.stop - cols.start
             g = [i for i, (first, last) in enumerate(W_GROUPS) if first <= r < last][0]
@@ -192,8 +188,7 @@ def tile_list_tgn_rnn_kernel(
             wcols = slice(c0, c0 + P)
             gs, n0 = divmod(r * P, HALF)
             ncols = slice(n0, n0 + P)
-            acc = psum.tile([P, hi - lo], F32, name=f"acc{len(sums) % SUMS}")
-            sums.append(acc)
+            acc = psum.tile([P, hi - lo], F32, name=f"acc{bank}")
             step = HALF if hi - lo == HALF else P
             for a in range(PASSES):
                 for c in range(lo, hi, step):
@@ -221,7 +216,7 @@ def tile_list_tgn_rnn_kernel(
         def add_state(r, cols, act):
             for lo in range(cols.start, cols.stop, HALF):
                 part = slice(lo, min(lo + HALF, cols.stop))
-                products(r, part, act[:, part.start - cols.start : part.stop - cols.start])
+                products(r, part, act[:, part.start - cols.start : part.stop - cols.start], r if r < WINDOWS else 2 + (2 * r + lo // HALF) % 3)
             nc.vector.tensor_tensor(out=totals[r][:, cols], in0=h[r][:].indirect(offsets_of(cols)), in1=act[:], op=ADD)
 
         def weigh_state(r, cols):
@@ -230,12 +225,13 @@ def tile_list_tgn_rnn_kernel(
             )
 
         def weigh_tanh(r, cols):
-            act = acts.tile([P, HALF], F32, name=f"act{r}_back")
-            products(r, cols, act[:])
-            by_event = psum.tile([P, HALF], F32, name="by_event", tag="spread0")
-            scaled = acts.tile([P, HALF], F32, name="scaled", bufs=2)
-            by_row = psum.tile([P, HALF], F32, name="by_row", tag="spread1")
-            blocks = [slice(b * P, (b + 1) * P) for b in range(HALF // P)]
+            width = cols.stop - cols.start
+            act = acts.tile([P, width], F32, name=f"act{r}_{cols.start}")
+            products(r, cols, act[:], r % 2)
+            by_event = psum.tile([P, width], F32, name="by_event", tag="spread0")
+            scaled = acts.tile([P, width], F32, name="scaled", bufs=2)
+            by_row = psum.tile([P, width], F32, name="by_row", tag="spread1")
+            blocks = [slice(lo, lo + P) for lo in range(0, width, P)]
             for block in blocks:
                 nc.tensor.transpose(by_event[:, block], act[:, block], ident[:])
             for block in blocks:
@@ -247,7 +243,7 @@ def tile_list_tgn_rnn_kernel(
             return act
 
         def window_of(r):
-            return windows[r if r < WINDOWS else (r - 1) % WINDOWS]
+            return windows[r % WINDOWS]
 
         def place(r, cols, other, op):
             nc.vector.tensor_tensor(
@@ -269,9 +265,16 @@ def tile_list_tgn_rnn_kernel(
                 out=tab_codes[half][:], in_=pairs[:, cols].bitcast(U16).rearrange("p (j d) -> p d j", d=PASSES)
             )
         for a in range(PASSES):
-            grouped = shared.tile([P, PIECE, 4], BF16, name=f"grouped{a}", offset=(4 + 2 * a) * KIB, align_bytes=ALIGN)
-            quantise(a, raw[a, 0][:], 0, grouped)
+            grouped = shared.tile([P, 4 * PIECE], BF16, name=f"grouped{a}", offset=(4 + 2 * a) * KIB, align_bytes=ALIGN)
+            quantise(a, raw[a, 0][:], 0, grouped[:])
         clear_window(1)
+        weights = shared.tile([P, J], F32, name="weights", offset=24 * KIB, align_bytes=ALIGN)
+        spread = [psum.tile([P, HALF], F32, name=f"spread{half}") for half in range(2)]
+        for m in range(TILES):
+            column = vec_cols[:, TILES + m : TILES + m + 1].to_broadcast([P, P])
+            nc.tensor.transpose(spread[m // 4][:, (m % 4) * P : (m % 4 + 1) * P], column, ident[:])
+        for half in (1, 0):
+            nc.scalar.copy(out=weights[:, half * HALF : (half + 1) * HALF], in_=spread[half][:])
         for r in range(2):
             act = shared.tile([P, PIECE], F32, name=f"act{r}_first", offset=(8 + 12 * r) * KIB, align_bytes=ALIGN)
             add_state(r, FIRST, act)
@@ -287,11 +290,10 @@ def tile_list_tgn_rnn_kernel(
         add_state(2, FRONT, acts.tile([P, HALF], F32, name="act2_front"))
         place(2, FRONT, weights[:, FRONT], MULT)
         quantise_stage(BACK)
-        for cols in (FRONT, BACK):
-            add_state(3, cols, acts.tile([P, HALF], F32, name=f"act3_{cols.start}"))
-            place(3, cols, weights[:, cols], MULT)
-        store(3)
-        for r in range(3):
+        add_state(3, FRONT, acts.tile([P, HALF], F32, name="act3_front"))
+        weigh_state(3, BACK)
+        place(3, FRONT, weights[:, FRONT], MULT)
+        for r in range(WINDOWS):
             place(r, BACK, weigh_tanh(r, BACK)[:], ADD)
             store(r)
         for r in range(WINDOWS, TILES):

@@ -25,11 +25,12 @@ PASSES = 2
 HALF = 512
 PIECE = 256
 TILES = N // P
-W_GROUPS = ((0, 1), (1, 2), (2, 3), (3, 4), (4, TILES))
+W_GROUPS = ((0, 1), (1, 3), (3, 4), (4, TILES))
 WINDOWS = 4
 KIB = 1024
 ALIGN = 256
 LATE_BYTES = (64 + 15 + 3 + 24) * KIB
+REST = slice(PIECE, J)
 FIRST, SECOND, FRONT, BACK, ALL = slice(0, PIECE), slice(PIECE, HALF), slice(0, HALF), slice(HALF, J), slice(0, J)
 
 
@@ -133,16 +134,15 @@ def tile_list_tgn_rnn_kernel(
         for a in range(PASSES):
             load_x(a, SECOND)
         load_h(2)
-        for g in (2, 3):
-            load_w(un_sb, un_words, g)
-            load_w(wn_sb, wn_words, g)
-        for a in range(PASSES):
-            load_x(a, BACK)
+        load_x(0, BACK)
+        load_w(un_sb, un_words, 2)
+        load_w(wn_sb, wn_words, 2)
+        load_x(1, BACK)
         load_h(3)
         load_scale_rows(un_planes, un_scales, 1)
-        load_w(un_sb, un_words, 4)
+        load_w(un_sb, un_words, 3)
         load_scale_rows(wn_planes, wn_scales, 1)
-        load_w(wn_sb, wn_words, 4)
+        load_w(wn_sb, wn_words, 3)
         for r in range(WINDOWS, TILES):
             load_h(r)
 
@@ -176,6 +176,8 @@ def tile_list_tgn_rnn_kernel(
                 for lo in range(0, cols.stop - cols.start, PIECE):
                     if (a, cols) == (PASSES - 1, BACK):
                         grouped = totals[3][:, 2 * lo : 2 * (lo + PIECE)].bitcast(BF16)
+                    elif (a, cols, lo) == (0, BACK, 0):
+                        grouped = acts.tile([P, 4 * PIECE], BF16, name="held", tag="scaled", bufs=2, align_bytes=64)[:]
                     else:
                         grouped = ring.tile([P, 4 * PIECE], BF16, name="grouped", align_bytes=64)[:]
                     quantise(a, raw[a, cols.start][:, :, lo : lo + PIECE], cols.start + lo, grouped)
@@ -224,12 +226,12 @@ def tile_list_tgn_rnn_kernel(
                 out=totals[r][:, cols], in0=h[r][:].indirect(offsets_of(cols)), in1=weights[:, cols], op=MULT
             )
 
-        def weigh_tanh(r, cols):
+        def weigh_tanh(r, cols, bank):
             width = cols.stop - cols.start
             act = acts.tile([P, width], F32, name=f"act{r}_{cols.start}")
-            products(r, cols, act[:], r % 2)
+            products(r, cols, act[:], bank)
             by_event = psum.tile([P, width], F32, name="by_event", tag="spread0")
-            scaled = acts.tile([P, width], F32, name="scaled", bufs=2)
+            scaled = acts.tile([P, width], F32, name="scaled", bufs=2, align_bytes=64)
             by_row = psum.tile([P, width], F32, name="by_row", tag="spread1")
             blocks = [slice(lo, lo + P) for lo in range(0, width, P)]
             for block in blocks:
@@ -279,22 +281,20 @@ def tile_list_tgn_rnn_kernel(
             act = shared.tile([P, PIECE], F32, name=f"act{r}_first", offset=(8 + 12 * r) * KIB, align_bytes=ALIGN)
             add_state(r, FIRST, act)
             clear_window(r + 2)
-            weigh_state(r, BACK)
+            weigh_state(r, REST)
             place(r, FIRST, weights[:, FIRST], MULT)
         quantise_stage(SECOND)
-        weigh_state(2, BACK)
-        for r in range(2):
-            add_state(r, SECOND, acts.tile([P, PIECE], F32, name=f"act{r}_second"))
-        for r in range(2):
-            place(r, SECOND, weights[:, SECOND], MULT)
-        add_state(2, FRONT, acts.tile([P, HALF], F32, name="act2_front"))
-        place(2, FRONT, weights[:, FRONT], MULT)
+        add_state(2, FIRST, acts.tile([P, PIECE], F32, name="act2_first"))
+        weigh_state(2, REST)
+        place(2, FIRST, weights[:, FIRST], MULT)
+        for r in range(3):
+            place(r, SECOND, weigh_tanh(r, SECOND, r % 2)[:], ADD)
         quantise_stage(BACK)
         add_state(3, FRONT, acts.tile([P, HALF], F32, name="act3_front"))
         weigh_state(3, BACK)
         place(3, FRONT, weights[:, FRONT], MULT)
         for r in range(WINDOWS):
-            place(r, BACK, weigh_tanh(r, BACK)[:], ADD)
+            place(r, BACK, weigh_tanh(r, BACK, r % 2)[:], ADD)
             store(r)
         for r in range(WINDOWS, TILES):
             add_state(r, ALL, acts.tile([P, J], F32, name="act", bufs=3))

@@ -77,7 +77,7 @@ def tile_list_tgn_rnn_kernel(
         wn_planes = [late_tile([P, PASSES, HALF], U8, f"wn_planes{g}", KIB) for g in range(2)]
         raw = {}
         for a in range(PASSES):
-            raw[a, 0] = shared.tile([P, 4, PIECE], F32, name=f"raw{a}_0", offset=24 * a * KIB, align_bytes=ALIGN)
+            raw[a, 0] = shared.tile([P, 4, PIECE], F32, name=f"raw{a}_0", offset=16 * a * KIB, align_bytes=ALIGN)
             raw[a, PIECE] = late_tile([P, 4, PIECE], F32, f"raw{a}_1", 4 * KIB)
             raw[a, HALF] = late_tile([P, 4, HALF], F32, f"raw{a}_2", 8 * KIB)
         assert sum(taken) == LATE_BYTES
@@ -114,10 +114,10 @@ def tile_list_tgn_rnn_kernel(
                 in_=tab_scales[:, r:16:4, :].bitcast(I32).rearrange("a q n -> q a n"),
             )
         nc.sync.dma_start(out=tab[:], in_=tab_words[0].rearrange("p t b -> p (t b)").bitcast(I32))
-        load_x(0, FIRST)
-        load_scale_rows(un_planes, un_scales, 0, (2, 3))
         nc.sync.dma_start(out=vec_rows[0:TILES, :], in_=bn.rearrange("(r p) -> r p", p=P))
         nc.sync.dma_start(out=vec_rows[TILES : 2 * TILES, :], in_=wgo[0, :].rearrange("(r p) -> r p", p=P))
+        load_x(0, FIRST)
+        load_scale_rows(un_planes, un_scales, 0, (2, 3))
         load_w(un_sb, un_words, 0)
         load_x(1, FIRST)
 
@@ -125,9 +125,9 @@ def tile_list_tgn_rnn_kernel(
         nc.vector.tensor_copy(out=tab_sc[0][:], in_=tab_planes[:, 0:T].indirect(offsets[:]))
         nc.sync.dma_start(out=tab_sc[1][0 : P - 16, :].bitcast(I32), in_=tab_sc[0][16:P, :].bitcast(I32))
 
+        load_h(0)
         load_w(wn_sb, wn_words, 0)
         load_scale_rows(wn_planes, wn_scales, 0)
-        load_h(0)
         load_w(un_sb, un_words, 1)
         load_w(wn_sb, wn_words, 1)
         load_h(1)
@@ -270,7 +270,7 @@ def tile_list_tgn_rnn_kernel(
             grouped = shared.tile([P, 4 * PIECE], BF16, name=f"grouped{a}", offset=(4 + 2 * a) * KIB, align_bytes=ALIGN)
             quantise(a, raw[a, 0][:], 0, grouped[:])
         clear_window(1)
-        weights = shared.tile([P, J], F32, name="weights", offset=24 * KIB, align_bytes=ALIGN)
+        weights = keep.tile([P, J], F32, name="weights")
         spread = [psum.tile([P, HALF], F32, name=f"spread{half}") for half in range(2)]
         for m in range(TILES):
             column = vec_cols[:, TILES + m : TILES + m + 1].to_broadcast([P, P])
@@ -279,9 +279,12 @@ def tile_list_tgn_rnn_kernel(
             nc.scalar.copy(out=weights[:, half * HALF : (half + 1) * HALF], in_=spread[half][:])
         for r in range(2):
             act = shared.tile([P, PIECE], F32, name=f"act{r}_first", offset=(8 + 12 * r) * KIB, align_bytes=ALIGN)
+            if r == 0:
+                weigh_state(r, REST)
             add_state(r, FIRST, act)
             clear_window(r + 2)
-            weigh_state(r, REST)
+            if r == 1:
+                weigh_state(r, REST)
             place(r, FIRST, weights[:, FIRST], MULT)
         quantise_stage(SECOND)
         add_state(2, FIRST, acts.tile([P, PIECE], F32, name="act2_first"))

@@ -297,7 +297,7 @@ def tile_list_tgn_rnn_kernel(
         weigh_state(3, BACK)
         place(3, FRONT, weights[:, FRONT], MULT)
         for r in range(WINDOWS):
-            place(r, BACK, weigh_tanh(r, BACK, r % 2)[:], ADD)
+            place(r, BACK, weigh_tanh(r, BACK, 4 if r == 0 else r % 2)[:], ADD)
             store(r)
         for r in range(WINDOWS, TILES):
             add_state(r, ALL, acts.tile([P, J], F32, name="act", bufs=3))

@@ -107,7 +107,8 @@ def tile_list_tgn_rnn_kernel(
             nc.sync.dma_start(out=h[r][:], in_=hT[P * r : P * (r + 1), :])
 
         nc.sync.dma_start(offsets[:], offs)
-        load_scale_rows(un_planes, un_scales, 0, (0, 1))
+        load_w(un_sb, un_words, 0)
+        load_scale_rows(un_planes, un_scales, 0, (0,))
         for r in range(4):
             nc.sync.dma_start(
                 out=tab_planes[r:P:16, 0:T].bitcast(I32),
@@ -117,8 +118,7 @@ def tile_list_tgn_rnn_kernel(
         nc.sync.dma_start(out=vec_rows[0:TILES, :], in_=bn.rearrange("(r p) -> r p", p=P))
         nc.sync.dma_start(out=vec_rows[TILES : 2 * TILES, :], in_=wgo[0, :].rearrange("(r p) -> r p", p=P))
         load_x(0, FIRST)
-        load_scale_rows(un_planes, un_scales, 0, (2, 3))
-        load_w(un_sb, un_words, 0)
+        load_scale_rows(un_planes, un_scales, 0, (1, 2, 3))
         load_x(1, FIRST)
 
         tab_sc = [keep.tile([P, J], U8, name=f"tab_sc{a}", align_bytes=64) for a in range(PASSES)]

@@ -29,7 +29,7 @@ W_GROUPS = ((0, 1), (1, 3), (3, 4), (4, TILES))
 WINDOWS = 4
 KIB = 1024
 ALIGN = 256
-LATE_BYTES = (64 + 15 + 3 + 24) * KIB
+LATE_BYTES = (64 + 14 + 3 + 24) * KIB
 REST = slice(PIECE, J)
 FIRST, SECOND, FRONT, BACK, ALL = slice(0, PIECE), slice(PIECE, HALF), slice(0, HALF), slice(HALF, J), slice(0, J)
 
@@ -67,7 +67,8 @@ def tile_list_tgn_rnn_kernel(
             return late_tile([P, PASSES, (hi - lo) * P], I32, f"{name}{lo}", (hi - lo) * KIB)
 
         h = [late_tile([P, T], F32, f"h{r}", 8 * KIB) for r in range(TILES)]
-        wn_sb = [weight_tile("wn", g) for g in range(len(W_GROUPS))]
+        wn_sb = [keep.tile([P, PASSES, P], I32, name="wn0", align_bytes=ALIGN)]
+        wn_sb.extend(weight_tile("wn", g) for g in range(1, len(W_GROUPS)))
         un_sb = [keep.tile([P, PASSES, P], I32, name="un0", align_bytes=ALIGN)]
         un_sb.extend(weight_tile("un", g) for g in range(1, len(W_GROUPS)))
         un_planes = [
@@ -120,13 +121,13 @@ def tile_list_tgn_rnn_kernel(
         load_x(0, FIRST)
         load_scale_rows(un_planes, un_scales, 0, (1, 2, 3))
         load_x(1, FIRST)
+        load_w(wn_sb, wn_words, 0)
 
         tab_sc = [keep.tile([P, J], U8, name=f"tab_sc{a}", align_bytes=64) for a in range(PASSES)]
         nc.vector.tensor_copy(out=tab_sc[0][:], in_=tab_planes[:, 0:T].indirect(offsets[:]))
         nc.sync.dma_start(out=tab_sc[1][0 : P - 16, :].bitcast(I32), in_=tab_sc[0][16:P, :].bitcast(I32))
 
         load_h(0)
-        load_w(wn_sb, wn_words, 0)
         load_scale_rows(wn_planes, wn_scales, 0)
         load_w(un_sb, un_words, 1)
         load_w(wn_sb, wn_words, 1)
@@ -182,7 +183,7 @@ def tile_list_tgn_rnn_kernel(
                         grouped = ring.tile([P, 4 * PIECE], BF16, name="grouped", align_bytes=64)[:]
                     quantise(a, raw[a, cols.start][:, :, lo : lo + PIECE], cols.start + lo, grouped)
 
-        def products(r, cols, into, bank):
+        def products(r, cols, bank):
             half, lo = divmod(cols.start, HALF)
             hi = lo + cols.stop - cols.start
             g = [i for i, (first, last) in enumerate(W_GROUPS) if first <= r < last][0]
@@ -213,12 +214,16 @@ def tile_list_tgn_rnn_kernel(
                     start=False,
                     stop=(a == PASSES - 1),
                 )
-            nc.scalar.activation(out=into, in_=acc[:], func=TANH, bias=vec_cols[:, r : r + 1])
+            return acc
+
+        def tanh_of(r, acc, into):
+            nc.scalar.activation(out=into, in_=acc, func=TANH, bias=vec_cols[:, r : r + 1])
 
         def add_state(r, cols, act):
             for lo in range(cols.start, cols.stop, HALF):
                 part = slice(lo, min(lo + HALF, cols.stop))
-                products(r, part, act[:, part.start - cols.start : part.stop - cols.start], r if r < WINDOWS else 2 + (2 * r + lo // HALF) % 3)
+                acc = products(r, part, r if r < WINDOWS else 2 + (2 * r + lo // HALF) % 3)
+                tanh_of(r, acc[:], act[:, part.start - cols.start : part.stop - cols.start])
             nc.vector.tensor_tensor(out=totals[r][:, cols], in0=h[r][:].indirect(offsets_of(cols)), in1=act[:], op=ADD)
 
         def weigh_state(r, cols):
@@ -226,22 +231,26 @@ def tile_list_tgn_rnn_kernel(
                 out=totals[r][:, cols], in0=h[r][:].indirect(offsets_of(cols)), in1=weights[:, cols], op=MULT
             )
 
-        def weigh_tanh(r, cols, bank):
+        def weigh_tanh(r, cols, bank, piece):
             width = cols.stop - cols.start
             act = acts.tile([P, width], F32, name=f"act{r}_{cols.start}")
-            products(r, cols, act[:], bank)
-            by_event = psum.tile([P, width], F32, name="by_event", tag="spread0")
-            scaled = acts.tile([P, width], F32, name="scaled", bufs=2, align_bytes=64)
-            by_row = psum.tile([P, width], F32, name="by_row", tag="spread1")
-            blocks = [slice(lo, lo + P) for lo in range(0, width, P)]
-            for block in blocks:
-                nc.tensor.transpose(by_event[:, block], act[:, block], ident[:])
-            for block in blocks:
-                m = TILES + (cols.start + block.start) // P
-                nc.scalar.activation(out=scaled[:, block], in_=by_event[:, block], func=COPY, scale=vec_cols[:, m : m + 1])
-            for block in blocks:
-                nc.tensor.transpose(by_row[:, block], scaled[:, block], ident[:])
-            nc.scalar.copy(out=act[:], in_=by_row[:])
+            acc = products(r, cols, bank)
+            for lo in range(0, width, piece):
+                tanh_of(r, acc[:, lo : lo + piece], act[:, lo : lo + piece])
+                by_event = psum.tile([P, piece], F32, name="by_event", tag="spread0")
+                scaled = acts.tile([P, piece], F32, name="scaled", bufs=2, align_bytes=64)
+                by_row = psum.tile([P, piece], F32, name="by_row", tag="spread1")
+                blocks = [slice(c, c + P) for c in range(0, piece, P)]
+                for block in blocks:
+                    nc.tensor.transpose(by_event[:, block], act[:, lo + block.start : lo + block.stop], ident[:])
+                for block in blocks:
+                    m = TILES + (cols.start + lo + block.start) // P
+                    nc.scalar.activation(
+                        out=scaled[:, block], in_=by_event[:, block], func=COPY, scale=vec_cols[:, m : m + 1]
+                    )
+                for block in blocks:
+                    nc.tensor.transpose(by_row[:, block], scaled[:, block], ident[:])
+                nc.scalar.copy(out=act[:, lo : lo + piece], in_=by_row[:])
             return act
 
         def window_of(r):
@@ -291,13 +300,13 @@ def tile_list_tgn_rnn_kernel(
         weigh_state(2, REST)
         place(2, FIRST, weights[:, FIRST], MULT)
         for r in range(3):
-            place(r, SECOND, weigh_tanh(r, SECOND, r % 2)[:], ADD)
+            place(r, SECOND, weigh_tanh(r, SECOND, r % 2, PIECE)[:], ADD)
         quantise_stage(BACK)
         add_state(3, FRONT, acts.tile([P, HALF], F32, name="act3_front"))
         weigh_state(3, BACK)
         place(3, FRONT, weights[:, FRONT], MULT)
         for r in range(WINDOWS):
-            place(r, BACK, weigh_tanh(r, BACK, 4 if r == 0 else r % 2)[:], ADD)
+            place(r, BACK, weigh_tanh(r, BACK, 4 if r == 0 else r % 2, PIECE if r == 0 else HALF)[:], ADD)
             store(r)
         for r in range(WINDOWS, TILES):
             add_state(r, ALL, acts.tile([P, J], F32, name="act", bufs=3))

@@ -29,7 +29,7 @@ W_GROUPS = ((0, 1), (1, 3), (3, 4), (4, TILES))
 WINDOWS = 4
 KIB = 1024
 ALIGN = 256
-LATE_BYTES = (64 + 14 + 3 + 24) * KIB
+LATE_BYTES = (64 + 15 + 3 + 24) * KIB
 REST = slice(PIECE, J)
 FIRST, SECOND, FRONT, BACK, ALL = slice(0, PIECE), slice(PIECE, HALF), slice(0, HALF), slice(HALF, J), slice(0, J)
 
@@ -67,8 +67,7 @@ def tile_list_tgn_rnn_kernel(
             return late_tile([P, PASSES, (hi - lo) * P], I32, f"{name}{lo}", (hi - lo) * KIB)
 
         h = [late_tile([P, T], F32, f"h{r}", 8 * KIB) for r in range(TILES)]
-        wn_sb = [keep.tile([P, PASSES, P], I32, name="wn0", align_bytes=ALIGN)]
-        wn_sb.extend(weight_tile("wn", g) for g in range(1, len(W_GROUPS)))
+        wn_sb = [weight_tile("wn", g) for g in range(len(W_GROUPS))]
         un_sb = [keep.tile([P, PASSES, P], I32, name="un0", align_bytes=ALIGN)]
         un_sb.extend(weight_tile("un", g) for g in range(1, len(W_GROUPS)))
         un_planes = [
@@ -108,8 +107,7 @@ def tile_list_tgn_rnn_kernel(
             nc.sync.dma_start(out=h[r][:], in_=hT[P * r : P * (r + 1), :])
 
         nc.sync.dma_start(offsets[:], offs)
-        load_w(un_sb, un_words, 0)
-        load_scale_rows(un_planes, un_scales, 0, (0,))
+        load_scale_rows(un_planes, un_scales, 0, (0, 1))
         for r in range(4):
             nc.sync.dma_start(
                 out=tab_planes[r:P:16, 0:T].bitcast(I32),
@@ -119,15 +117,16 @@ def tile_list_tgn_rnn_kernel(
         nc.sync.dma_start(out=vec_rows[0:TILES, :], in_=bn.rearrange("(r p) -> r p", p=P))
         nc.sync.dma_start(out=vec_rows[TILES : 2 * TILES, :], in_=wgo[0, :].rearrange("(r p) -> r p", p=P))
         load_x(0, FIRST)
-        load_scale_rows(un_planes, un_scales, 0, (1, 2, 3))
+        load_scale_rows(un_planes, un_scales, 0, (2, 3))
+        load_w(un_sb, un_words, 0)
         load_x(1, FIRST)
-        load_w(wn_sb, wn_words, 0)
 
         tab_sc = [keep.tile([P, J], U8, name=f"tab_sc{a}", align_bytes=64) for a in range(PASSES)]
         nc.vector.tensor_copy(out=tab_sc[0][:], in_=tab_planes[:, 0:T].indirect(offsets[:]))
         nc.sync.dma_start(out=tab_sc[1][0 : P - 16, :].bitcast(I32), in_=tab_sc[0][16:P, :].bitcast(I32))
 
         load_h(0)
+        load_w(wn_sb, wn_words, 0)
         load_scale_rows(wn_planes, wn_scales, 0)
         load_w(un_sb, un_words, 1)
         load_w(wn_sb, wn_words, 1)
@@ -140,11 +139,12 @@ def tile_list_tgn_rnn_kernel(
         load_w(wn_sb, wn_words, 2)
         load_x(1, BACK)
         load_h(3)
+        load_h(4)
         load_scale_rows(un_planes, un_scales, 1)
         load_w(un_sb, un_words, 3)
         load_scale_rows(wn_planes, wn_scales, 1)
         load_w(wn_sb, wn_words, 3)
-        for r in range(WINDOWS, TILES):
+        for r in range(WINDOWS + 1, TILES):
             load_h(r)
 
         turned = psum.tile([P, P], F32, name="turned")
@@ -172,16 +172,12 @@ def tile_list_tgn_rnn_kernel(
                 in_=grouped,
             )
 
-        def quantise_stage(cols):
-            for a in range(PASSES):
-                for lo in range(0, cols.stop - cols.start, PIECE):
-                    if (a, cols) == (PASSES - 1, BACK):
-                        grouped = totals[3][:, 2 * lo : 2 * (lo + PIECE)].bitcast(BF16)
-                    elif (a, cols, lo) == (0, BACK, 0):
-                        grouped = acts.tile([P, 4 * PIECE], BF16, name="held", tag="scaled", bufs=2, align_bytes=64)[:]
-                    else:
-                        grouped = ring.tile([P, 4 * PIECE], BF16, name="grouped", align_bytes=64)[:]
-                    quantise(a, raw[a, cols.start][:, :, lo : lo + PIECE], cols.start + lo, grouped)
+        def quantise_piece(a, cols, lo):
+            if (a, cols, lo) == (0, BACK, 0):
+                grouped = acts.tile([P, 4 * PIECE], BF16, name="held", tag="scaled", bufs=2, align_bytes=64)
+            else:
+                grouped = ring.tile([P, 4 * PIECE], BF16, name="grouped", align_bytes=64)
+            quantise(a, raw[a, cols.start][:, :, lo : lo + PIECE], cols.start + lo, grouped[:])
 
         def products(r, cols, bank):
             half, lo = divmod(cols.start, HALF)
@@ -231,9 +227,8 @@ def tile_list_tgn_rnn_kernel(
                 out=totals[r][:, cols], in0=h[r][:].indirect(offsets_of(cols)), in1=weights[:, cols], op=MULT
             )
 
-        def weigh_tanh(r, cols, bank, piece):
+        def weigh_tanh(r, cols, bank, piece, act):
             width = cols.stop - cols.start
-            act = acts.tile([P, width], F32, name=f"act{r}_{cols.start}")
             acc = products(r, cols, bank)
             for lo in range(0, width, piece):
                 tanh_of(r, acc[:, lo : lo + piece], act[:, lo : lo + piece])
@@ -251,7 +246,6 @@ def tile_list_tgn_rnn_kernel(
                 for block in blocks:
                     nc.tensor.transpose(by_row[:, block], scaled[:, block], ident[:])
                 nc.scalar.copy(out=act[:, lo : lo + piece], in_=by_row[:])
-            return act
 
         def window_of(r):
             return windows[r % WINDOWS]
@@ -295,21 +289,34 @@ def tile_list_tgn_rnn_kernel(
             if r == 1:
                 weigh_state(r, REST)
             place(r, FIRST, weights[:, FIRST], MULT)
-        quantise_stage(SECOND)
+        for a in range(PASSES):
+            quantise_piece(a, SECOND, 0)
         add_state(2, FIRST, acts.tile([P, PIECE], F32, name="act2_first"))
         weigh_state(2, REST)
         place(2, FIRST, weights[:, FIRST], MULT)
         for r in range(3):
-            place(r, SECOND, weigh_tanh(r, SECOND, r % 2, PIECE)[:], ADD)
-        quantise_stage(BACK)
+            act = acts.tile([P, PIECE], F32, name=f"act{r}_second")
+            weigh_tanh(r, SECOND, r % 2, PIECE, act)
+            place(r, SECOND, act[:], ADD)
+        for a, lo in ((0, 0), (0, PIECE), (1, 0)):
+            quantise_piece(a, BACK, lo)
         add_state(3, FRONT, acts.tile([P, HALF], F32, name="act3_front"))
         weigh_state(3, BACK)
+        quantise_piece(1, BACK, PIECE)
         place(3, FRONT, weights[:, FRONT], MULT)
+        weigh_state(4, ALL)
         for r in range(WINDOWS):
-            place(r, BACK, weigh_tanh(r, BACK, 4 if r == 0 else r % 2, PIECE if r == 0 else HALF)[:], ADD)
+            act = acts.tile([P, HALF], F32, name=f"act{r}_back")
+            weigh_tanh(r, BACK, 4 if r == 0 else r % 2, PIECE if r == 0 else HALF, act)
+            place(r, BACK, act[:], ADD)
             store(r)
-        for r in range(WINDOWS, TILES):
-            add_state(r, ALL, acts.tile([P, J], F32, name="act", bufs=3))
-        for r in range(WINDOWS, TILES):
+        act4 = acts.tile([P, J], F32, name="act4")
+        for half, cols in enumerate((FRONT, BACK)):
+            weigh_tanh(4, cols, 2 + half, HALF, act4[:, cols])
+        for r in range(WINDOWS + 1, TILES):
+            add_state(r, ALL, acts.tile([P, J], F32, name="act", bufs=2))
+        place(4, ALL, act4[:], ADD)
+        store(4)
+        for r in range(WINDOWS + 1, TILES):
             place(r, ALL, weights[:], MULT)
             store(r)

@@ -147,7 +147,7 @@ def tile_list_tgn_rnn_kernel(
         for r in range(WINDOWS + 1, TILES):
             load_h(r)
 
-        turned = psum.tile([P, P], F32, name="turned")
+        turned = psum.tile([P, P], F32, name="turned", tag="by_event", bufs=2)
         nc.tensor.transpose(turned[:], vec_rows[:], ident[:])
         nc.scalar.copy(out=vec_cols[:], in_=turned[:, 0 : 2 * TILES])
 
@@ -218,7 +218,7 @@ def tile_list_tgn_rnn_kernel(
         def add_state(r, cols, act):
             for lo in range(cols.start, cols.stop, HALF):
                 part = slice(lo, min(lo + HALF, cols.stop))
-                acc = products(r, part, r if r < WINDOWS else 2 + (2 * r + lo // HALF) % 3)
+                acc = products(r, part, min(r, 2) if r < WINDOWS else (2 * r + lo // HALF) % 4)
                 tanh_of(r, acc[:], act[:, part.start - cols.start : part.stop - cols.start])
             nc.vector.tensor_tensor(out=totals[r][:, cols], in0=h[r][:].indirect(offsets_of(cols)), in1=act[:], op=ADD)
 
@@ -232,9 +232,9 @@ def tile_list_tgn_rnn_kernel(
             acc = products(r, cols, bank)
             for lo in range(0, width, piece):
                 tanh_of(r, acc[:, lo : lo + piece], act[:, lo : lo + piece])
-                by_event = psum.tile([P, piece], F32, name="by_event", tag="spread0")
+                by_event = psum.tile([P, piece], F32, name="by_event", bufs=2)
                 scaled = acts.tile([P, piece], F32, name="scaled", bufs=2, align_bytes=64)
-                by_row = psum.tile([P, piece], F32, name="by_row", tag="spread1")
+                by_row = psum.tile([P, piece], F32, name="by_row", bufs=2)
                 blocks = [slice(c, c + P) for c in range(0, piece, P)]
                 for block in blocks:
                     nc.tensor.transpose(by_event[:, block], act[:, lo + block.start : lo + block.stop], ident[:])
@@ -274,7 +274,7 @@ def tile_list_tgn_rnn_kernel(
             quantise(a, raw[a, 0][:], 0, grouped[:])
         clear_window(1)
         weights = keep.tile([P, J], F32, name="weights")
-        spread = [psum.tile([P, HALF], F32, name=f"spread{half}") for half in range(2)]
+        spread = [psum.tile([P, HALF], F32, name=f"spread{half}", tag="by_row", bufs=2) for half in range(2)]
         for m in range(TILES):
             column = vec_cols[:, TILES + m : TILES + m + 1].to_broadcast([P, P])
             nc.tensor.transpose(spread[m // 4][:, (m % 4) * P : (m % 4 + 1) * P], column, ident[:])
@@ -307,7 +307,7 @@ def tile_list_tgn_rnn_kernel(
         weigh_state(4, ALL)
         for r in range(WINDOWS):
             act = acts.tile([P, HALF], F32, name=f"act{r}_back")
-            weigh_tanh(r, BACK, 4 if r == 0 else r % 2, PIECE if r == 0 else HALF, act)
+            weigh_tanh(r, BACK, 3 if r == 0 else r % 2, PIECE if r == 0 else HALF, act)
             place(r, BACK, act[:], ADD)
             store(r)
         act4 = acts.tile([P, J], F32, name="act4")

@@ -44,6 +44,7 @@ def tile_list_tgn_rnn_kernel(
         late = ctx.enter_context(tc.tile_pool(name="late", bufs=1))
         ring = ctx.enter_context(tc.tile_pool(name="ring", bufs=4))
         acts = ctx.enter_context(tc.tile_pool(name="acts", bufs=1))
+        front = ctx.enter_context(tc.tile_pool(name="front", bufs=1))
         psum = ctx.enter_context(tc.psum_pool(name="psum", bufs=1))
 
         offsets = keep.tile([P, J // 16], U16, name="offsets")
@@ -157,7 +158,8 @@ def tile_list_tgn_rnn_kernel(
         x_codes, x_sc, tab_codes = {}, {}, {}
         for half in range(2):
             for a in range(PASSES):
-                x_codes[a, half] = keep.tile([P, HALF], U32, name=f"x_codes{half}_{a}", align_bytes=64)
+                if (a, half) != (1, 1):
+                    x_codes[a, half] = keep.tile([P, HALF], U32, name=f"x_codes{half}_{a}", align_bytes=64)
                 x_sc[a, half] = keep.tile([P, HALF], U8, name=f"x_sc{half}_{a}", align_bytes=64)
 
         def quantise(a, src, first, grouped):
@@ -227,10 +229,8 @@ def tile_list_tgn_rnn_kernel(
                 out=totals[r][:, cols], in0=h[r][:].indirect(offsets_of(cols)), in1=weights[:, cols], op=MULT
             )
 
-        def weigh_tanh(r, cols, bank, piece, act):
-            width = cols.stop - cols.start
-            acc = products(r, cols, bank)
-            for lo in range(0, width, piece):
+        def weigh_tanh(r, cols, acc, piece, act, starts):
+            for lo in starts:
                 tanh_of(r, acc[:, lo : lo + piece], act[:, lo : lo + piece])
                 by_event = psum.tile([P, piece], F32, name="by_event", bufs=2)
                 scaled = acts.tile([P, piece], F32, name="scaled", bufs=2, align_bytes=64)
@@ -296,23 +296,31 @@ def tile_list_tgn_rnn_kernel(
         place(2, FIRST, weights[:, FIRST], MULT)
         for r in range(3):
             act = acts.tile([P, PIECE], F32, name=f"act{r}_second")
-            weigh_tanh(r, SECOND, r % 2, PIECE, act)
+            weigh_tanh(r, SECOND, products(r, SECOND, r % 2), PIECE, act, (0,))
             place(r, SECOND, act[:], ADD)
-        for a, lo in ((0, 0), (0, PIECE), (1, 0)):
-            quantise_piece(a, BACK, lo)
-        add_state(3, FRONT, acts.tile([P, HALF], F32, name="act3_front"))
+        for lo in (0, PIECE):
+            quantise_piece(0, BACK, lo)
+        add_state(3, FRONT, front.tile([P, HALF], F32, name="act3_front", offset=0, align_bytes=64))
         weigh_state(3, BACK)
-        quantise_piece(1, BACK, PIECE)
+        x_codes[1, 1] = front.tile([P, HALF], U32, name="x_codes1_1", offset=0, align_bytes=64)
+        for lo in (0, PIECE):
+            quantise_piece(1, BACK, lo)
         place(3, FRONT, weights[:, FRONT], MULT)
         weigh_state(4, ALL)
+        backs = [acts.tile([P, HALF], F32, name=f"act{r}_back") for r in range(WINDOWS)]
+        sums = [products(r, BACK, bank) for r, bank in ((0, 3), (1, 1))]
+        for lo in (0, PIECE):
+            for r in range(2):
+                weigh_tanh(r, BACK, sums[r], PIECE, backs[r], (lo,))
+                place(r, slice(HALF + lo, HALF + lo + PIECE), backs[r][:, lo : lo + PIECE], ADD)
         for r in range(WINDOWS):
-            act = acts.tile([P, HALF], F32, name=f"act{r}_back")
-            weigh_tanh(r, BACK, 3 if r == 0 else r % 2, PIECE if r == 0 else HALF, act)
-            place(r, BACK, act[:], ADD)
+            if r >= 2:
+                weigh_tanh(r, BACK, products(r, BACK, r % 2), HALF, backs[r], (0,))
+                place(r, BACK, backs[r][:], ADD)
             store(r)
         act4 = acts.tile([P, J], F32, name="act4")
         for half, cols in enumerate((FRONT, BACK)):
-            weigh_tanh(4, cols, 2 + half, HALF, act4[:, cols])
+            weigh_tanh(4, cols, products(4, cols, 2 + half), HALF, act4[:, cols], (0,))
         for r in range(WINDOWS + 1, TILES):
             add_state(r, ALL, acts.tile([P, J], F32, name="act", bufs=2))
         place(4, ALL, act4[:], ADD)

@@ -291,12 +291,13 @@ def tile_list_tgn_rnn_kernel(
             place(r, FIRST, weights[:, FIRST], MULT)
         for a in range(PASSES):
             quantise_piece(a, SECOND, 0)
-        add_state(2, FIRST, acts.tile([P, PIECE], F32, name="act2_first"))
-        weigh_state(2, REST)
-        place(2, FIRST, weights[:, FIRST], MULT)
-        for r in range(3):
+        for cols, early in ((FIRST, slice(HALF, J - P)), (SECOND, slice(J - P, J))):
+            add_state(2, cols, acts.tile([P, PIECE], F32, name="act2_front", bufs=2))
+            weigh_state(2, early)
+            place(2, cols, weights[:, cols], MULT)
+        for r in range(2):
             act = acts.tile([P, PIECE], F32, name=f"act{r}_second")
-            weigh_tanh(r, SECOND, products(r, SECOND, r % 2), PIECE, act, (0,))
+            weigh_tanh(r, SECOND, products(r, SECOND, r), PIECE, act, (0,))
             place(r, SECOND, act[:], ADD)
         for lo in (0, PIECE):
             quantise_piece(0, BACK, lo)

@@ -30,6 +30,7 @@ WINDOWS = 4
 KIB = 1024
 ALIGN = 256
 LATE_BYTES = (64 + 15 + 3 + 24) * KIB
+ROWS = 96
 REST = slice(PIECE, J)
 FIRST, SECOND, FRONT, BACK, ALL = slice(0, PIECE), slice(PIECE, HALF), slice(0, HALF), slice(HALF, J), slice(0, J)
 
@@ -83,13 +84,13 @@ def tile_list_tgn_rnn_kernel(
             raw[a, HALF] = late_tile([P, 4, HALF], F32, f"raw{a}_2", 8 * KIB)
         assert sum(taken) == LATE_BYTES
 
-        nc.gpsimd.memset(tab_planes[:, 0:T].bitcast(I32), 0)
         nc.gpsimd.memset(vec_rows[:], 0.0)
-        nc.vector.memset(windows[0][:], 0.0)
+        nc.vector.memset(tab_planes[0:ROWS, 0:T].bitcast(I32), 0)
         make_identity(nc, ident[:])
+        nc.gpsimd.memset(windows[0][:], 0.0)
 
-        def load_scale_rows(planes, scales, g, rows=range(4)):
-            for r in rows:
+        def load_scale_rows(planes, scales, g):
+            for r in range(4):
                 nc.sync.dma_start(
                     out=planes[g][r:P:32, :, :].bitcast(I32),
                     in_=scales[:, r:16:4, g * HALF : (g + 1) * HALF].bitcast(I32).rearrange("a q n -> q a n"),
@@ -108,23 +109,25 @@ def tile_list_tgn_rnn_kernel(
             nc.sync.dma_start(out=h[r][:], in_=hT[P * r : P * (r + 1), :])
 
         nc.sync.dma_start(offsets[:], offs)
-        load_scale_rows(un_planes, un_scales, 0, (0, 1))
-        for r in range(4):
-            nc.sync.dma_start(
-                out=tab_planes[r:P:16, 0:T].bitcast(I32),
-                in_=tab_scales[:, r:16:4, :].bitcast(I32).rearrange("a q n -> q a n"),
-            )
+        nc.sync.dma_start(
+            out=tab_planes[ROWS:P, 0:T].bitcast(I32), in_=tab_scales.bitcast(I32).rearrange("a q n -> q a n")
+        )
         nc.sync.dma_start(out=tab[:], in_=tab_words[0].rearrange("p t b -> p (t b)").bitcast(I32))
         nc.sync.dma_start(out=vec_rows[0:TILES, :], in_=bn.rearrange("(r p) -> r p", p=P))
         nc.sync.dma_start(out=vec_rows[TILES : 2 * TILES, :], in_=wgo[0, :].rearrange("(r p) -> r p", p=P))
-        load_x(0, FIRST)
-        load_scale_rows(un_planes, un_scales, 0, (2, 3))
+        load_scale_rows(un_planes, un_scales, 0)
+        for a in range(PASSES):
+            load_x(a, FIRST)
         load_w(un_sb, un_words, 0)
-        load_x(1, FIRST)
 
-        tab_sc = [keep.tile([P, J], U8, name=f"tab_sc{a}", align_bytes=64) for a in range(PASSES)]
-        nc.vector.tensor_copy(out=tab_sc[0][:], in_=tab_planes[:, 0:T].indirect(offsets[:]))
-        nc.sync.dma_start(out=tab_sc[1][0 : P - 16, :].bitcast(I32), in_=tab_sc[0][16:P, :].bitcast(I32))
+        picked = keep.tile([P, J], U8, name="picked", align_bytes=64)
+        tab_sc = keep.tile([P, PASSES, J], U8, name="tab_sc", align_bytes=64)
+        nc.vector.tensor_copy(out=picked[:], in_=tab_planes[:, 0:T].indirect(offsets[:]))
+        for q in range(4):
+            nc.sync.dma_start(
+                out=tab_sc[32 * q : 32 * q + 4, :, :].bitcast(I32),
+                in_=picked[ROWS + 8 * q : ROWS + 8 * (q + 1), :].bitcast(I32),
+            )
 
         load_h(0)
         load_w(wn_sb, wn_words, 0)
@@ -198,7 +201,7 @@ def tile_list_tgn_rnn_kernel(
                         lhsT=un_sb[g][:, a, wcols].bitcast(FP8X4),
                         lhsT_scale=un_planes[gs][:, a, ncols],
                         rhs=tab_codes[half][:, a, c : c + step].bitcast(FP4X4),
-                        rhs_scale=tab_sc[a][:, half * HALF + c : half * HALF + c + step],
+                        rhs_scale=tab_sc[:, a, half * HALF + c : half * HALF + c + step],
                         start=(a == 0 and c == lo),
                         stop=False,
                     )

@@ -29,7 +29,7 @@ W_GROUPS = ((0, 1), (1, 3), (3, 4), (4, TILES))
 WINDOWS = 4
 KIB = 1024
 ALIGN = 256
-LATE_BYTES = (64 + 15 + 3 + 24) * KIB
+LATE_BYTES = (64 + 15 + 2 + 24) * KIB
 ROWS = 96
 REST = slice(PIECE, J)
 FIRST, SECOND, FRONT, BACK, ALL = slice(0, PIECE), slice(PIECE, HALF), slice(0, HALF), slice(HALF, J), slice(0, J)
@@ -76,7 +76,7 @@ def tile_list_tgn_rnn_kernel(
             keep.tile([P, PASSES, HALF], U8, name="un_planes0", align_bytes=64),
             late_tile([P, PASSES, HALF], U8, "un_planes1", KIB),
         ]
-        wn_planes = [late_tile([P, PASSES, HALF], U8, f"wn_planes{g}", KIB) for g in range(2)]
+        wn_planes = late_tile([P, N], U8, "wn_planes", KIB)
         raw = {}
         for a in range(PASSES):
             raw[a, 0] = shared.tile([P, 4, PIECE], F32, name=f"raw{a}_0", offset=16 * a * KIB, align_bytes=ALIGN)
@@ -89,9 +89,9 @@ def tile_list_tgn_rnn_kernel(
         make_identity(nc, ident[:])
         nc.gpsimd.memset(windows[0][:], 0.0)
 
-        def load_scale_rows(planes, scales, g):
-            for r in range(4):
-                nc.sync.dma_start(
+        def load_scale_rows(planes, scales, g, queues):
+            for r, queue in enumerate(queues):
+                queue.dma_start(
                     out=planes[g][r:P:32, :, :].bitcast(I32),
                     in_=scales[:, r:16:4, g * HALF : (g + 1) * HALF].bitcast(I32).rearrange("a q n -> q a n"),
                 )
@@ -115,7 +115,7 @@ def tile_list_tgn_rnn_kernel(
         nc.sync.dma_start(out=tab[:], in_=tab_words[0].rearrange("p t b -> p (t b)").bitcast(I32))
         nc.sync.dma_start(out=vec_rows[0:TILES, :], in_=bn.rearrange("(r p) -> r p", p=P))
         nc.sync.dma_start(out=vec_rows[TILES : 2 * TILES, :], in_=wgo[0, :].rearrange("(r p) -> r p", p=P))
-        load_scale_rows(un_planes, un_scales, 0)
+        load_scale_rows(un_planes, un_scales, 0, (nc.scalar, nc.scalar, nc.scalar, nc.sync))
         for a in range(PASSES):
             load_x(a, FIRST)
         load_w(un_sb, un_words, 0)
@@ -131,7 +131,11 @@ def tile_list_tgn_rnn_kernel(
 
         load_h(0)
         load_w(wn_sb, wn_words, 0)
-        load_scale_rows(wn_planes, wn_scales, 0)
+        for q in range(4):
+            nc.sync.dma_start(
+                out=wn_planes[32 * q + 4 : 32 * q + 12, :].bitcast(I32),
+                in_=wn_scales[:, 4 * q : 4 * (q + 1), :].bitcast(I32),
+            )
         load_w(un_sb, un_words, 1)
         load_w(wn_sb, wn_words, 1)
         load_h(1)
@@ -144,9 +148,8 @@ def tile_list_tgn_rnn_kernel(
         load_x(1, BACK)
         load_h(3)
         load_h(4)
-        load_scale_rows(un_planes, un_scales, 1)
+        load_scale_rows(un_planes, un_scales, 1, 4 * (nc.sync,))
         load_w(un_sb, un_words, 3)
-        load_scale_rows(wn_planes, wn_scales, 1)
         load_w(wn_sb, wn_words, 3)
         for r in range(WINDOWS + 1, TILES):
             load_h(r)
@@ -209,7 +212,7 @@ def tile_list_tgn_rnn_kernel(
                 nc.tensor.matmul_mx(
                     out=acc[:],
                     lhsT=wn_sb[g][:, a, wcols].bitcast(FP8X4),
-                    lhsT_scale=wn_planes[gs][:, a, ncols],
+                    lhsT_scale=wn_planes[4 * (a + 1) : P, r * P : (r + 1) * P],
                     rhs=x_codes[a, half][:, lo:hi].bitcast(FP8X4),
                     rhs_scale=x_sc[a, half][:, lo:hi],
                     start=False,

@@ -123,7 +123,7 @@ def tile_list_tgn_rnn_kernel(
         picked = keep.tile([P, J], U8, name="picked", align_bytes=64)
         tab_sc = keep.tile([P, PASSES, J], U8, name="tab_sc", align_bytes=64)
         nc.vector.tensor_copy(out=picked[:], in_=tab_planes[:, 0:T].indirect(offsets[:]))
-        for q in range(4):
+        for q in (0, 2, 1, 3):
             nc.sync.dma_start(
                 out=tab_sc[32 * q : 32 * q + 4, :, :].bitcast(I32),
                 in_=picked[ROWS + 8 * q : ROWS + 8 * (q + 1), :].bitcast(I32),
@@ -164,7 +164,7 @@ def tile_list_tgn_rnn_kernel(
         x_codes, x_sc, tab_codes = {}, {}, {}
         for half in range(2):
             for a in range(PASSES):
-                if (a, half) != (1, 1):
+                if half == 0:
                     x_codes[a, half] = keep.tile([P, HALF], U32, name=f"x_codes{half}_{a}", align_bytes=64)
                 x_sc[a, half] = keep.tile([P, HALF], U8, name=f"x_sc{half}_{a}", align_bytes=64)
 
@@ -305,13 +305,12 @@ def tile_list_tgn_rnn_kernel(
             act = acts.tile([P, PIECE], F32, name=f"act{r}_second")
             weigh_tanh(r, SECOND, products(r, SECOND, r), PIECE, act, (0,))
             place(r, SECOND, act[:], ADD)
-        for lo in (0, PIECE):
-            quantise_piece(0, BACK, lo)
-        add_state(3, FRONT, front.tile([P, HALF], F32, name="act3_front", offset=0, align_bytes=64))
+        add_state(3, FRONT, front.tile([P, HALF], F32, name="act3_front", offset=KIB, align_bytes=64))
         weigh_state(3, BACK)
-        x_codes[1, 1] = front.tile([P, HALF], U32, name="x_codes1_1", offset=0, align_bytes=64)
-        for lo in (0, PIECE):
-            quantise_piece(1, BACK, lo)
+        for a in range(PASSES):
+            x_codes[a, 1] = front.tile([P, HALF], U32, name=f"x_codes1_{a}", offset=2 * a * KIB, align_bytes=64)
+            for lo in (0, PIECE):
+                quantise_piece(a, BACK, lo)
         place(3, FRONT, weights[:, FRONT], MULT)
         weigh_state(4, ALL)
         backs = [acts.tile([P, HALF], F32, name=f"act{r}_back") for r in range(WINDOWS)]

@@ -196,18 +196,16 @@ def tile_list_tgn_rnn_kernel(
             gs, n0 = divmod(r * P, HALF)
             ncols = slice(n0, n0 + P)
             acc = psum.tile([P, hi - lo], F32, name=f"acc{bank}")
-            step = HALF if hi - lo == HALF else P
             for a in range(PASSES):
-                for c in range(lo, hi, step):
-                    nc.tensor.matmul_mx(
-                        out=acc[:, c - lo : c - lo + step],
-                        lhsT=un_sb[g][:, a, wcols].bitcast(FP8X4),
-                        lhsT_scale=un_planes[gs][:, a, ncols],
-                        rhs=tab_codes[half][:, a, c : c + step].bitcast(FP4X4),
-                        rhs_scale=tab_sc[:, a, half * HALF + c : half * HALF + c + step],
-                        start=(a == 0 and c == lo),
-                        stop=False,
-                    )
+                nc.tensor.matmul_mx(
+                    out=acc[:],
+                    lhsT=un_sb[g][:, a, wcols].bitcast(FP8X4),
+                    lhsT_scale=un_planes[gs][:, a, ncols],
+                    rhs=tab_codes[half][:, a, lo:hi].bitcast(FP4X4),
+                    rhs_scale=tab_sc[:, a, cols],
+                    start=(a == 0),
+                    stop=False,
+                )
             for a in range(PASSES):
                 nc.tensor.matmul_mx(
                     out=acc[:],
@@ -226,7 +224,7 @@ def tile_list_tgn_rnn_kernel(
         def add_state(r, cols, act):
             for lo in range(cols.start, cols.stop, HALF):
                 part = slice(lo, min(lo + HALF, cols.stop))
-                acc = products(r, part, min(r, 2) if r < WINDOWS else (2 * r + lo // HALF) % 4)
+                acc = products(r, part, (0, 1, 0, 0)[r] if r < WINDOWS else (2 * r + lo // HALF) % 4)
                 tanh_of(r, acc[:], act[:, part.start - cols.start : part.stop - cols.start])
             nc.vector.tensor_tensor(out=totals[r][:, cols], in0=h[r][:].indirect(offsets_of(cols)), in1=act[:], op=ADD)
 
@@ -303,25 +301,27 @@ def tile_list_tgn_rnn_kernel(
             place(2, cols, weights[:, cols], MULT)
         for r in range(2):
             act = acts.tile([P, PIECE], F32, name=f"act{r}_second")
-            weigh_tanh(r, SECOND, products(r, SECOND, r), PIECE, act, (0,))
+            weigh_tanh(r, SECOND, products(r, SECOND, (3, 1)[r]), PIECE, act, (0,))
             place(r, SECOND, act[:], ADD)
         add_state(3, FRONT, front.tile([P, HALF], F32, name="act3_front", offset=KIB, align_bytes=64))
         weigh_state(3, BACK)
         for a in range(PASSES):
             x_codes[a, 1] = front.tile([P, HALF], U32, name=f"x_codes1_{a}", offset=2 * a * KIB, align_bytes=64)
-            for lo in (0, PIECE):
+        for lo in (0, PIECE):
+            for a in range(PASSES):
                 quantise_piece(a, BACK, lo)
         place(3, FRONT, weights[:, FRONT], MULT)
         weigh_state(4, ALL)
         backs = [acts.tile([P, HALF], F32, name=f"act{r}_back") for r in range(WINDOWS)]
-        sums = [products(r, BACK, bank) for r, bank in ((0, 3), (1, 1))]
-        for lo in (0, PIECE):
+        for lo, banks in ((0, (2, 1)), (PIECE, (3, 0))):
+            cols = slice(HALF + lo, HALF + lo + PIECE)
             for r in range(2):
-                weigh_tanh(r, BACK, sums[r], PIECE, backs[r], (lo,))
-                place(r, slice(HALF + lo, HALF + lo + PIECE), backs[r][:, lo : lo + PIECE], ADD)
+                act = backs[r][:, lo : lo + PIECE]
+                weigh_tanh(r, cols, products(r, cols, banks[r]), PIECE, act, (0,))
+                place(r, cols, act, ADD)
         for r in range(WINDOWS):
             if r >= 2:
-                weigh_tanh(r, BACK, products(r, BACK, r % 2), HALF, backs[r], (0,))
+                weigh_tanh(r, BACK, products(r, BACK, 3 - r), HALF, backs[r], (0,))
                 place(r, BACK, backs[r][:], ADD)
             store(r)
         act4 = acts.tile([P, J], F32, name="act4")

@@ -32,6 +32,7 @@ ALIGN = 256
 LATE_BYTES = (64 + 15 + 2 + 24) * KIB
 ROWS = 96
 REST = slice(PIECE, J)
+THIRD, FOURTH = slice(HALF, HALF + PIECE), slice(HALF + PIECE, J)
 FIRST, SECOND, FRONT, BACK, ALL = slice(0, PIECE), slice(PIECE, HALF), slice(0, HALF), slice(HALF, J), slice(0, J)
 
 
@@ -81,7 +82,9 @@ def tile_list_tgn_rnn_kernel(
         for a in range(PASSES):
             raw[a, 0] = shared.tile([P, 4, PIECE], F32, name=f"raw{a}_0", offset=16 * a * KIB, align_bytes=ALIGN)
             raw[a, PIECE] = late_tile([P, 4, PIECE], F32, f"raw{a}_1", 4 * KIB)
-            raw[a, HALF] = late_tile([P, 4, HALF], F32, f"raw{a}_2", 8 * KIB)
+        raw[0, HALF] = late_tile([P, 4, HALF], F32, "raw0_2", 8 * KIB)
+        for cols in (THIRD, FOURTH):
+            raw[1, cols.start] = late_tile([P, 4, PIECE], F32, f"raw1_{cols.start}", 4 * KIB)
         assert sum(taken) == LATE_BYTES
 
         nc.gpsimd.memset(vec_rows[:], 0.0)
@@ -145,7 +148,8 @@ def tile_list_tgn_rnn_kernel(
         load_x(0, BACK)
         load_w(un_sb, un_words, 2)
         load_w(wn_sb, wn_words, 2)
-        load_x(1, BACK)
+        load_x(1, THIRD)
+        load_x(1, FOURTH)
         load_h(3)
         load_h(4)
         load_scale_rows(un_planes, un_scales, 1, 4 * (nc.sync,))
@@ -307,9 +311,9 @@ def tile_list_tgn_rnn_kernel(
         weigh_state(3, BACK)
         for a in range(PASSES):
             x_codes[a, 1] = front.tile([P, HALF], U32, name=f"x_codes1_{a}", offset=2 * a * KIB, align_bytes=64)
-        for lo in (0, PIECE):
-            for a in range(PASSES):
-                quantise_piece(a, BACK, lo)
+        for lo, cols in ((0, THIRD), (PIECE, FOURTH)):
+            quantise_piece(0, BACK, lo)
+            quantise_piece(1, cols, 0)
         place(3, FRONT, weights[:, FRONT], MULT)
         weigh_state(4, ALL)
         backs = [acts.tile([P, HALF], F32, name=f"act{r}_back") for r in range(WINDOWS)]

from contextlib import ExitStack

import concourse.mybir as mybir
from concourse.masks import make_identity

K, M, N, T, J = 1024, 1024, 1024, 2048, 1024
FLOPS = 2 * (K + M) * N * J

F32 = mybir.dt.float32
BF16 = mybir.dt.bfloat16
I32 = mybir.dt.int32
U32 = mybir.dt.uint32
U16 = mybir.dt.uint16
U8 = mybir.dt.uint8
FP8X4 = mybir.dt.float8_e4m3fn_x4
FP4X4 = mybir.dt.float4_e2m1fn_x4
ADD = mybir.AluOpType.add
MULT = mybir.AluOpType.mult
TANH = mybir.ActivationFunctionType.Tanh

COPY = mybir.ActivationFunctionType.Copy

P = 128
PASSES = 2
HALF = 512
PIECE = 256
TILES = N // P
W_GROUPS = ((0, 1), (1, 3), (3, 4), (4, TILES))
WINDOWS = 4
KIB = 1024
ALIGN = 256
LATE_BYTES = (64 + 15 + 2 + 24) * KIB
ROWS = 96
REST = slice(PIECE, J)
THIRD, FOURTH = slice(HALF, HALF + PIECE), slice(HALF + PIECE, J)
FIRST, SECOND, FRONT, BACK, ALL = slice(0, PIECE), slice(PIECE, HALF), slice(0, HALF), slice(HALF, J), slice(0, J)


def tile_list_tgn_rnn_kernel(
    tc, x, tab_words, tab_scales, wn_words, wn_scales, un_words, un_scales, bn, hT, wgo, offs, out
):
    nc = tc.nc
    with ExitStack() as ctx:
        keep = ctx.enter_context(tc.tile_pool(name="keep", bufs=1))
        shared = ctx.enter_context(tc.tile_pool(name="shared", bufs=1))
        late = ctx.enter_context(tc.tile_pool(name="late", bufs=1))
        ring = ctx.enter_context(tc.tile_pool(name="ring", bufs=4))
        acts = ctx.enter_context(tc.tile_pool(name="acts", bufs=1))
        front = ctx.enter_context(tc.tile_pool(name="front", bufs=1))
        psum = ctx.enter_context(tc.psum_pool(name="psum", bufs=1))

        offsets = keep.tile([P, J // 16], U16, name="offsets")
        windows = {0: keep.tile([P, T], F32, name="window0", align_bytes=ALIGN)}
        vec_rows = keep.tile([P, P], F32, name="vec_rows", align_bytes=ALIGN)
        ident = keep.tile([P, P], F32, name="ident")
        vec_cols = keep.tile([P, 2 * TILES], F32, name="vec_cols")
        totals = [keep.tile([P, J], F32, name=f"total{r}", align_bytes=64) for r in range(TILES)]
        tab = shared.tile([P, T], I32, name="tab", offset=8 * KIB, align_bytes=ALIGN)
        tab_planes = late.tile([P, LATE_BYTES], U8, name="tab_planes", offset=0, align_bytes=ALIGN)

        taken = [0]

        def late_tile(shape, dtype, name, size):
            tile = late.tile(shape, dtype, name=name, offset=sum(taken), align_bytes=ALIGN)
            taken.append(size)
            return tile

        def weight_tile(name, g):
            lo, hi = W_GROUPS[g]
            return late_tile([P, PASSES, (hi - lo) * P], I32, f"{name}{lo}", (hi - lo) * KIB)

        h = [late_tile([P, T], F32, f"h{r}", 8 * KIB) for r in range(TILES)]
        wn_sb = [weight_tile("wn", g) for g in range(len(W_GROUPS))]
        un_sb = [keep.tile([P, PASSES, P], I32, name="un0", align_bytes=ALIGN)]
        un_sb.extend(weight_tile("un", g) for g in range(1, len(W_GROUPS)))
        un_planes = [
            keep.tile([P, PASSES, HALF], U8, name="un_planes0", align_bytes=64),
            late_tile([P, PASSES, HALF], U8, "un_planes1", KIB),
        ]
        wn_planes = late_tile([P, N], U8, "wn_planes", KIB)
        raw = {}
        for a in range(PASSES):
            raw[a, 0] = shared.tile([P, 4, PIECE], F32, name=f"raw{a}_0", offset=16 * a * KIB, align_bytes=ALIGN)
            raw[a, PIECE] = late_tile([P, 4, PIECE], F32, f"raw{a}_1", 4 * KIB)
        raw[0, HALF] = late_tile([P, 4, HALF], F32, "raw0_2", 8 * KIB)
        for cols in (THIRD, FOURTH):
            raw[1, cols.start] = late_tile([P, 4, PIECE], F32, f"raw1_{cols.start}", 4 * KIB)
        assert sum(taken) == LATE_BYTES

        nc.gpsimd.memset(vec_rows[:], 0.0)
        nc.vector.memset(tab_planes[0:ROWS, 0:T].bitcast(I32), 0)
        make_identity(nc, ident[:])
        nc.gpsimd.memset(windows[0][:], 0.0)

        def load_scale_rows(planes, scales, g, queues):
            for r, queue in enumerate(queues):
                queue.dma_start(
                    out=planes[g][r:P:32, :, :].bitcast(I32),
                    in_=scales[:, r:16:4, g * HALF : (g + 1) * HALF].bitcast(I32).rearrange("a q n -> q a n"),
                )

        def load_x(a, cols):
            rows = x[512 * a : 512 * (a + 1), cols]
            nc.sync.dma_start(out=raw[a, cols.start][:], in_=rows.rearrange("(p i) j -> p i j", i=4))

        def load_w(tiles, words, g):
            lo, hi = W_GROUPS[g]
            view = words.rearrange("a p n i -> p a (n i)")[:, :, 4 * P * lo : 4 * P * hi].bitcast(I32)
            nc.sync.dma_start(out=tiles[g][:], in_=view)

        def load_h(r):
            nc.sync.dma_start(out=h[r][:], in_=hT[P * r : P * (r + 1), :])

        nc.sync.dma_start(offsets[:], offs)
        nc.sync.dma_start(
            out=tab_planes[ROWS:P, 0:T].bitcast(I32), in_=tab_scales.bitcast(I32).rearrange("a q n -> q a n")
        )
        nc.sync.dma_start(out=tab[:], in_=tab_words[0].rearrange("p t b -> p (t b)").bitcast(I32))
        nc.sync.dma_start(out=vec_rows[0:TILES, :], in_=bn.rearrange("(r p) -> r p", p=P))
        nc.sync.dma_start(out=vec_rows[TILES : 2 * TILES, :], in_=wgo[0, :].rearrange("(r p) -> r p", p=P))
        load_scale_rows(un_planes, un_scales, 0, (nc.scalar, nc.scalar, nc.scalar, nc.sync))
        for a in range(PASSES):
            load_x(a, FIRST)
        load_w(un_sb, un_words, 0)

        picked = keep.tile([P, J], U8, name="picked", align_bytes=64)
        tab_sc = keep.tile([P, PASSES, J], U8, name="tab_sc", align_bytes=64)
        nc.vector.tensor_copy(out=picked[:], in_=tab_planes[:, 0:T].indirect(offsets[:]))
        for q in (0, 2, 1, 3):
            nc.sync.dma_start(
                out=tab_sc[32 * q : 32 * q + 4, :, :].bitcast(I32),
                in_=picked[ROWS + 8 * q : ROWS + 8 * (q + 1), :].bitcast(I32),
            )

        load_h(0)
        load_w(wn_sb, wn_words, 0)
        for q in range(4):
            nc.sync.dma_start(
                out=wn_planes[32 * q + 4 : 32 * q + 12, :].bitcast(I32),
                in_=wn_scales[:, 4 * q : 4 * (q + 1), :].bitcast(I32),
            )
        load_w(un_sb, un_words, 1)
        load_w(wn_sb, wn_words, 1)
        load_h(1)
        for a in range(PASSES):
            load_x(a, SECOND)
        load_h(2)
        load_x(0, BACK)
        load_w(un_sb, un_words, 2)
        load_w(wn_sb, wn_words, 2)
        load_x(1, THIRD)
        load_x(1, FOURTH)
        load_h(3)
        load_h(4)
        load_scale_rows(un_planes, un_scales, 1, 4 * (nc.sync,))
        load_w(un_sb, un_words, 3)
        load_w(wn_sb, wn_words, 3)
        for r in range(WINDOWS + 1, TILES):
            load_h(r)

        turned = psum.tile([P, P], F32, name="turned", tag="by_event", bufs=2)
        nc.tensor.transpose(turned[:], vec_rows[:], ident[:])
        nc.scalar.copy(out=vec_cols[:], in_=turned[:, 0 : 2 * TILES])

        def offsets_of(cols):
            return offsets[:, cols.start // 16 : cols.stop // 16]

        x_codes, x_sc, tab_codes = {}, {}, {}
        for half in range(2):
            for a in range(PASSES):
                if half == 0:
                    x_codes[a, half] = keep.tile([P, HALF], U32, name=f"x_codes{half}_{a}", align_bytes=64)
                x_sc[a, half] = keep.tile([P, HALF], U8, name=f"x_sc{half}_{a}", align_bytes=64)

        def quantise(a, src, first, grouped):
            half, lo = divmod(first, HALF)
            nc.scalar.copy(
                out=grouped.rearrange("p (c e i) -> p c i e", e=4, i=4),
                in_=src.rearrange("p i (c e) -> p c i e", e=4),
            )
            nc.vector.quantize_mx(
                out=x_codes[a, half][:, lo : lo + PIECE].bitcast(FP8X4),
                scales=x_sc[a, half][:, lo : lo + PIECE],
                in_=grouped,
            )

        def quantise_piece(a, cols, lo):
            if (a, cols, lo) == (0, BACK, 0):
                grouped = acts.tile([P, 4 * PIECE], BF16, name="held", tag="scaled", bufs=2, align_bytes=64)
            else:
                grouped = ring.tile([P, 4 * PIECE], BF16, name="grouped", align_bytes=64)
            quantise(a, raw[a, cols.start][:, :, lo : lo + PIECE], cols.start + lo, grouped[:])

        def products(r, cols, bank):
            half, lo = divmod(cols.start, HALF)
            hi = lo + cols.stop - cols.start
            g = [i for i, (first, last) in enumerate(W_GROUPS) if first <= r < last][0]
            c0 = (r - W_GROUPS[g][0]) * P
            wcols = slice(c0, c0 + P)
            gs, n0 = divmod(r * P, HALF)
            ncols = slice(n0, n0 + P)
            acc = psum.tile([P, hi - lo], F32, name=f"acc{bank}")
            for a in range(PASSES):
                nc.tensor.matmul_mx(
                    out=acc[:],
                    lhsT=un_sb[g][:, a, wcols].bitcast(FP8X4),
                    lhsT_scale=un_planes[gs][:, a, ncols],
                    rhs=tab_codes[half][:, a, lo:hi].bitcast(FP4X4),
                    rhs_scale=tab_sc[:, a, cols],
                    start=(a == 0),
                    stop=False,
                )
            for a in range(PASSES):
                nc.tensor.matmul_mx(
                    out=acc[:],
                    lhsT=wn_sb[g][:, a, wcols].bitcast(FP8X4),
                    lhsT_scale=wn_planes[4 * (a + 1) : P, r * P : (r + 1) * P],
                    rhs=x_codes[a, half][:, lo:hi].bitcast(FP8X4),
                    rhs_scale=x_sc[a, half][:, lo:hi],
                    start=False,
                    stop=(a == PASSES - 1),
                )
            return acc

        def tanh_of(r, acc, into):
            nc.scalar.activation(out=into, in_=acc, func=TANH, bias=vec_cols[:, r : r + 1])

        def add_state(r, cols, act):
            for lo in range(cols.start, cols.stop, HALF):
                part = slice(lo, min(lo + HALF, cols.stop))
                acc = products(r, part, (0, 1, 0, 0)[r] if r < WINDOWS else (2 * r + lo // HALF) % 4)
                tanh_of(r, acc[:], act[:, part.start - cols.start : part.stop - cols.start])
            nc.vector.tensor_tensor(out=totals[r][:, cols], in0=h[r][:].indirect(offsets_of(cols)), in1=act[:], op=ADD)

        def weigh_state(r, cols):
            nc.vector.tensor_tensor(
                out=totals[r][:, cols], in0=h[r][:].indirect(offsets_of(cols)), in1=weights[:, cols], op=MULT
            )

        def weigh_tanh(r, cols, acc, piece, act, starts):
            for lo in starts:
                tanh_of(r, acc[:, lo : lo + piece], act[:, lo : lo + piece])
                by_event = psum.tile([P, piece], F32, name="by_event", bufs=2)
                scaled = acts.tile([P, piece], F32, name="scaled", bufs=2, align_bytes=64)
                by_row = psum.tile([P, piece], F32, name="by_row", bufs=2)
                blocks = [slice(c, c + P) for c in range(0, piece, P)]
                for block in blocks:
                    nc.tensor.transpose(by_event[:, block], act[:, lo + block.start : lo + block.stop], ident[:])
                for block in blocks:
                    m = TILES + (cols.start + lo + block.start) // P
                    nc.scalar.activation(
                        out=scaled[:, block], in_=by_event[:, block], func=COPY, scale=vec_cols[:, m : m + 1]
                    )
                for block in blocks:
                    nc.tensor.transpose(by_row[:, block], scaled[:, block], ident[:])
                nc.scalar.copy(out=act[:, lo : lo + piece], in_=by_row[:])

        def window_of(r):
            return windows[r % WINDOWS]

        def place(r, cols, other, op):
            nc.vector.tensor_tensor(
                out=window_of(r)[:].indirect(offsets_of(cols)), in0=totals[r][:, cols], in1=other, op=op
            )

        def store(r):
            nc.sync.dma_start(out=out[P * r : P * (r + 1), :], in_=window_of(r)[:])

        def clear_window(w):
            windows[w] = shared.tile([P, T], F32, name=f"window{w}", offset=8 * KIB * (w - 1), align_bytes=ALIGN)
            nc.gpsimd.memset(windows[w][:], 0.0)

        pairs = keep.tile([P, J], U32, name="pairs")
        nc.vector.tensor_copy(out=pairs[:], in_=tab[:].bitcast(U32).indirect(offsets[:]))
        for half, cols in enumerate((FRONT, BACK)):
            tab_codes[half] = keep.tile([P, PASSES, HALF], U16, name=f"tab_codes{half}", align_bytes=64)
            nc.vector.tensor_copy(
                out=tab_codes[half][:], in_=pairs[:, cols].bitcast(U16).rearrange("p (j d) -> p d j", d=PASSES)
            )
        for a in range(PASSES):
            grouped = shared.tile([P, 4 * PIECE], BF16, name=f"grouped{a}", offset=(4 + 2 * a) * KIB, align_bytes=ALIGN)
            quantise(a, raw[a, 0][:], 0, grouped[:])
        clear_window(1)
        weights = keep.tile([P, J], F32, name="weights")
        spread = [psum.tile([P, HALF], F32, name=f"spread{half}", tag="by_row", bufs=2) for half in range(2)]
        for m in range(TILES):
            column = vec_cols[:, TILES + m : TILES + m + 1].to_broadcast([P, P])
            nc.tensor.transpose(spread[m // 4][:, (m % 4) * P : (m % 4 + 1) * P], column, ident[:])
        for half in (1, 0):
            nc.scalar.copy(out=weights[:, half * HALF : (half + 1) * HALF], in_=spread[half][:])
        for r in range(2):
            act = shared.tile([P, PIECE], F32, name=f"act{r}_first", offset=(8 + 12 * r) * KIB, align_bytes=ALIGN)
            if r == 0:
                weigh_state(r, REST)
            add_state(r, FIRST, act)
            clear_window(r + 2)
            if r == 1:
                weigh_state(r, REST)
            place(r, FIRST, weights[:, FIRST], MULT)
        for a in range(PASSES):
            quantise_piece(a, SECOND, 0)
        for cols, early in ((FIRST, slice(HALF, J - P)), (SECOND, slice(J - P, J))):
            add_state(2, cols, acts.tile([P, PIECE], F32, name="act2_front", bufs=2))
            weigh_state(2, early)
            place(2, cols, weights[:, cols], MULT)
        for r in range(2):
            act = acts.tile([P, PIECE], F32, name=f"act{r}_second")
            weigh_tanh(r, SECOND, products(r, SECOND, (3, 1)[r]), PIECE, act, (0,))
            place(r, SECOND, act[:], ADD)
        add_state(3, FRONT, front.tile([P, HALF], F32, name="act3_front", offset=KIB, align_bytes=64))
        weigh_state(3, BACK)
        for a in range(PASSES):
            x_codes[a, 1] = front.tile([P, HALF], U32, name=f"x_codes1_{a}", offset=2 * a * KIB, align_bytes=64)
        for lo, cols in ((0, THIRD), (PIECE, FOURTH)):
            quantise_piece(0, BACK, lo)
            quantise_piece(1, cols, 0)
        place(3, FRONT, weights[:, FRONT], MULT)
        weigh_state(4, ALL)
        backs = [acts.tile([P, HALF], F32, name=f"act{r}_back") for r in range(WINDOWS)]
        for lo, banks in ((0, (2, 1)), (PIECE, (3, 0))):
            cols = slice(HALF + lo, HALF + lo + PIECE)
            for r in range(2):
                act = backs[r][:, lo : lo + PIECE]
                weigh_tanh(r, cols, products(r, cols, banks[r]), PIECE, act, (0,))
                place(r, cols, act, ADD)
        for r in range(WINDOWS):
            if r >= 2:
                weigh_tanh(r, BACK, products(r, BACK, 3 - r), HALF, backs[r], (0,))
                place(r, BACK, backs[r][:], ADD)
            store(r)
        act4 = acts.tile([P, J], F32, name="act4")
        for half, cols in enumerate((FRONT, BACK)):
            weigh_tanh(4, cols, products(4, cols, 2 + half), HALF, act4[:, cols], (0,))
        for r in range(WINDOWS + 1, TILES):
            add_state(r, ALL, acts.tile([P, J], F32, name="act", bufs=2))
        place(4, ALL, act4[:], ADD)
        store(4)
        for r in range(WINDOWS + 1, TILES):
            place(r, ALL, weights[:], MULT)
            store(r)
